import numpy as np, ml_dtypes
CORES = [2,6,10,14,18,22,26,30]
N = 8
BF = ml_dtypes.bfloat16
def gentries(a):
    return np.ascontiguousarray(a.reshape(8, 16, -1).transpose(0, 2, 1)).reshape(8, -1)
def gtable(e):
    e = np.asarray(e); return np.ascontiguousarray(e.reshape(8, -1, 16).transpose(0, 2, 1)).reshape(128, -1).astype(np.int32)
S, G, CAP, WN, M, Q, RO, H, T0 = 3328, 112, 16, 144, 512, 4096, 3, 4, 192
W, L = S + (N - 1) * G, (N - 1) * CAP + WN
def lines(rng, n):
    base = rng.integers(0, 256, (N, 8, 1, n)); amp = rng.choice(np.array([0.0, 2.0, 12.0, 50.0]), (N, 8, 1, n))
    return np.clip(np.rint(base + amp * rng.standard_normal((N, 8, 15, n))), 0, 255).astype(np.int64)
def parts(rng):
    st = np.where(rng.random((N, 8, S)) < rng.choice(np.array([0.3, 0.45, 0.6]), (N, 8, 1)), -1, rng.integers(0, T0, (N, 8, S)))
    x = np.concatenate([lines(rng, S), st[:, :, None, :]], axis=2)
    order = np.argsort(st, axis=-1, kind="stable"); pos = np.argsort(order, axis=-1)
    span = rng.choice(np.array([4, 32, 300]), (N, 8, 1, S))
    at = np.clip(pos[:, :, None, :] + (span * (rng.random((N, 8, 16, S)) * 4 - 3)).astype(np.int64), 0, S - 1)
    nb = np.take_along_axis(order[:, :, None, :], at, 3)
    gh = rng.random((N, 8, 16, S)) < rng.choice(np.array([0.01, 0.03, 0.08]), (N, 8, 1, 1))
    nb = np.where(gh, rng.integers(S, W, (N, 8, 16, S)), nb)
    pl = np.concatenate([lines(rng, M), rng.integers(0, 256, (N, 8, 1, M))], axis=2); w = rng.integers(0, 256, (N, 8, 16, 1))
    none = np.sum(st < 0, axis=-1)[:, :, None]; k = np.minimum(none + (rng.random((N, 8, RO * WN)) * (S - none)).astype(np.int64), S - 1)
    wl = np.take_along_axis(order, k, 2); wl = np.where(rng.random(wl.shape) < 0.1, rng.integers(0, S, wl.shape), wl).reshape(N, 8, RO, WN)
    return x, nb, pl, w, wl, rng.integers(0, S, (N, 8, N - 1, G))
def pack(x, nb, pl, w, wl, sl):
    return {"x0": x.reshape(N, 128, S).astype(np.float32).astype(BF), "nb": np.ascontiguousarray(nb.reshape(N, 128, S)).astype(np.int32),
            "pull": pl.reshape(N, 128, M).astype(np.float32).astype(BF), "wt": w.reshape(N, 128, 1).astype(np.int32),
            "wants": np.stack([gtable(a.reshape(8, -1)) for a in wl]), "snd": np.stack([gtable(a.reshape(8, -1)) for a in sl])}
def aim(bl, lo):
    place = np.array([np.sum(bl[:i] == bl[i]) for i in range(len(bl))])
    return S + bl * G + lo + place % CAP
def brim(rng, x, nb, w, wl, sl, g):
    K = (N - 1) * CAP; w[:, g] = 0; w[:, g, 0] = 16; w[:, g, 1] = 1
    for r in range(N):
        zs = rng.permutation(Q); h = ((zs * zs >> 5) + 194) & (Q - 1)
        u, i = np.unique(np.where(h >= S, h - S, h), return_index=True)
        p = rng.permutation(np.nonzero(u)[0])[:L]; z = zs[i[p]]
        o = rng.permutation(np.setdiff1d(np.arange(1, S), u[p]))[:3 * WN + 2 * K]
        o[2 * WN + K + int(rng.integers(0, K))] = 0
        one, two, asked, late, last = np.split(o, [WN, 2 * WN, 2 * WN + K, 2 * WN + 2 * K])
        x[r, g, 15, u[p]] = -1
        for q, k in ((one, 0), (two, 0), (asked, 1), (late, 2)):
            x[r, g, 2, q] = 100 * k + rng.integers(0, 50, len(q)); x[r, g, 3, q] = 250 - 100 * k - rng.integers(0, 50, len(q))
            x[r, g, 15, q] = 60 * k + rng.integers(0, 50, len(q))
        end = np.concatenate([late, last]); x[r, g, 0, end] = z >> 4; x[r, g, 1, end] = z & 15
        x[r, g, 15, last] = rng.integers(0, T0, WN)
        nb[r, g][:, o] = o
        sl[r, g, :, :CAP] = asked.reshape(N - 1, CAP); sl[r, g, :, G - CAP:] = late.reshape(N - 1, CAP)
        bl = np.concatenate([rng.permutation(np.repeat(np.arange(N - 1), CAP)), rng.integers(0, N - 1, WN - K)])
        nb[r, g][rng.integers(0, 16, WN), one] = aim(bl, 0)
        b = int(rng.integers(0, N - 1)); bl = rng.permutation(np.arange(L - CAP) % (N - 2))
        bl = np.concatenate([bl + (bl >= b), np.full(CAP, b)])
        nb[r, g][rng.integers(0, 16, L), np.concatenate([asked, two])] = aim(bl, G - CAP)
        wl[r, g, 0] = one; wl[r, g, 1] = two; wl[r, g, 2] = last
def setup_inputs(rng):
    return pack(*parts(rng))
def setup_inputs_room(rng):
    x, nb, pl, w, wl, sl = parts(rng); k = S // 8
    for r in range(N):
        for g in range(8):
            o = rng.permutation(S); a, b, c, e = o[:k], o[k:2 * k], o[2 * k:3 * k], o[3 * k:]
            x[r, g, 15, a] = T0 - 1; x[r, g, 0, a] = 255; x[r, g, 1, a] = 0
            x[r, g, 15, b] = 0; x[r, g, 0, b] = rng.integers(0, 255, k); x[r, g, 1, b] = rng.integers(1, 256, k)
            x[r, g, 15, c] = rng.integers(0, T0, k); x[r, g, 15, e] = -1
            for q in (a[:k // 2], b, c): nb[r, g][:, q] = q
            sl[r, g] = a[rng.integers(0, k, (N - 1, G))]
            n = rng.choice(np.array([0, 1, CAP - 1, CAP, CAP + 1]), N - 1)
            if r == 0: n[0] = (CAP, CAP + 1, CAP - 1, 0, 1, CAP + 9, CAP, CAP + 1)[g]
            else: n[rng.integers(0, N - 1)] = CAP + 9
            to = np.concatenate([S + j * G + rng.integers(0, G, int(n[j])) for j in range(N - 1)])
            go = rng.permutation(b)[:len(to)]; nb[r, g][rng.integers(0, 16, len(to)), go] = to
            wl[r, g, 0] = rng.permutation(np.concatenate([go, rng.permutation(c)[:WN - len(to)]]))
    brim(rng, x, nb, w, wl, sl, 6)
    return pack(x, nb, pl, w, wl, sl)
def setup_inputs_ties(rng):
    x, nb, pl, w, wl, sl = parts(rng); n = (N, 8, 1, S); row = np.arange(15)[:, None]
    p = 100 + (row == rng.integers(0, 22, n)).astype(np.int64) - (row == rng.integers(0, 22, n)) + (rng.random(n) < 0.1)
    x = np.concatenate([p, rng.choice(np.array([-1, -1, -1, 0, 1, 2, T0 - 2, T0 - 1]), n)], axis=2); x[:, :, 15, ::S - 1] = 0
    wl[:, :, :, 0] = 0; wl[:, :, :, 1] = S - 1; nb[:, 1::2, 8:] = nb[:, 1::2, :8]
    return pack(x, nb, pl, w, wl, sl)
def setup_inputs_crowd(rng):
    x, nb, pl, w, wl, sl = parts(rng)
    x[:, :4, :15] = np.take_along_axis(x[:, :4, :15], rng.integers(0, 8, (N, 4, 1, S)), 3)
    nb = np.where(rng.random((N, 8, 1, S)) < 0.6, np.arange(S), nb)
    w[:, 5] = 0; x[:, 5, 15][:, 97 * np.arange(RO)] = -1
    ts, zs = np.nonzero((((np.arange(Q) ** 2 >> 5) + 97 * np.arange(RO)[:, None]) & (Q - 1)) == S)
    t = int(ts[0]); z = int(zs[rng.integers(0, int(np.sum(ts == t)))])
    w[:, 7] = 0; w[:, 7, 0] = z >> 4; w[:, 7, 1] = 1
    for r in range(N):
        for g in (0, 2, 4, 6):
            few = np.concatenate([np.array([0, S - 1]), rng.integers(0, S, 10)])
            x[r, g, 15, few] = T0 - 1; nb[r, g][:, few] = few; wl[r, g] = few[rng.integers(0, 12, (RO, WN))]
        half = 1 + rng.permutation(S - 1)[:S // 2]; few = half[:8]
        x[r, 7, 0, half] = 16; x[r, 7, 1, half] = z & 15; x[r, 7, 15, 0] = -1
        x[r, 7, 15, few] = T0 - 1; nb[r, 7][:, few] = few; wl[r, 7, t, :8] = few
    return pack(x, nb, pl, w, wl, sl)
def setup_inputs_bare(rng):
    x, nb, pl, w, wl, sl = parts(rng); q = rng.permutation(N); g = rng.permutation(8)
    x[:, g[0], 15] = -1; v = x[:, g[1], 15]; x[:, g[1], 15] = np.where(v < 0, rng.integers(0, T0, v.shape), v)
    nb[:, g[3]] = rng.choice(np.array([0, S - 1, S, W - 1]), (N, 16, S)); sl[:, g[2]] = rng.choice(np.array([0, S - 1, S // 2, 3]), (N, N - 1, G))
    nb[q[0]] = rng.integers(S, W, (8, 16, S)); nb[q[1]] = rng.integers(0, S, (8, 16, S))
    return pack(x, nb, pl, w, wl, sl)
def setup_inputs_spread(rng):
    x, nb, pl, w, wl, sl = parts(rng)
    p = np.minimum((np.exp2(8 * rng.random((N, 8, 1, S))) * rng.random((N, 8, 15, S))).astype(np.int64), 255)
    st = np.minimum(np.exp2(7.6 * rng.random((N, 8, 1, S))).astype(np.int64) - 1, T0 - 1)
    st = np.where(rng.random((N, 8, 1, S)) < rng.choice(np.array([0.1, 0.4, 0.8]), (N, 8, 1, 1)), -1, st)
    w = np.minimum(np.exp2(8 * rng.random((N, 8, 16, 1))).astype(np.int64), 255)
    pl = np.minimum((np.exp2(8 * rng.random((N, 8, 1, M))) * rng.random((N, 8, 16, M))).astype(np.int64), 255)
    nb = np.where(rng.random((N, 8, 1, S)) < 0.5, rng.integers(0, W, nb.shape), nb)
    return pack(np.concatenate([p, st], axis=2), nb, pl, w, rng.integers(0, S, wl.shape), sl)
def check_inputs(d):
    bad = []
    v = np.asarray(d["x0"]).astype(np.float32).reshape(N, 8, 16, S)
    for k, a, lo, hi in (("paths of x0", v[:, :, :15], 0, 255), ("stamps of x0", v[:, :, 15], -1, T0 - 1), ("pull", np.asarray(d["pull"]).astype(np.float32), 0, 255), ("wt", d["wt"], 0, 255),
                         ("nb", d["nb"], 0, W - 1), ("wants", d["wants"], 0, S - 1), ("snd", d["snd"], 0, S - 1)):
        if not np.all((a >= lo) & (a <= hi) & (a == np.floor(a))): bad.append("range of " + k)
    return bad
def reference(x0, nb, pull, wt, wants, snd):
    x = x0.astype(np.float32).astype(np.int64).reshape(N, 8, 16, S); nbr = nb.astype(np.int64).reshape(N, 8, 16, S)
    pl = pull.astype(np.float32).astype(np.int64).reshape(N, 8, 16, M); w = wt.astype(np.int64).reshape(N, 8, 1, 16)[..., :15]
    wl = np.stack([gentries(a) for a in wants]).astype(np.int64).reshape(N, 8, RO, WN); sl = np.stack([gentries(a) for a in snd]).astype(np.int64).reshape(N, 8, N - 1, G)
    gi = np.arange(8)[:, None]; g3 = gi[:, :, None]; lane = np.arange(L)
    req = np.full((N, 8, N - 1, CAP), -1, np.int64)
    for t in range(RO):
        new = x.copy(); ask = np.full((N, 8, N - 1, CAP), -1, np.int64)
        for r in range(N):
            f = np.concatenate([x[r]] + [np.take_along_axis(x[(r - e) % N], sl[(r - e) % N, :, e - 1][:, None, :], 2) for e in range(1, N)], axis=2)
            s = np.concatenate([req[r].reshape(8, -1), wl[r, :, t]], axis=1)
            climb = s >= 0; s = np.maximum(s, 0); climb = climb & (f[gi, 15, s] >= 0); done = np.zeros((8, L), bool)
            for h in range(H):
                c = nbr[r][g3, np.arange(16), np.minimum(s, S - 1)[:, :, None]]
                a = f[g3, :, c]; b = f[gi, :, s][:, :, None, :]
                cov = (a[..., 15] > b[..., 15]) & np.any(a[..., :15] > b[..., :15], axis=3) & np.any(a[..., :15] < b[..., :15], axis=3)
                may = climb & (s < S); cov = cov & may[:, :, None]
                best = np.argmax(np.where(cov, a[..., 15], -1), axis=2)
                hit = np.any(cov, axis=2); done = done | (may & ~hit); climb = climb & hit
                s = np.where(hit, np.take_along_axis(c, best[:, :, None], 2)[:, :, 0], s)
            for e in range(1, N):
                q = (r - e) % N; k = s - S - (e - 1) * G; on = ((k >= 0) & (k < G)).astype(np.int64)
                before = np.add.accumulate(on, axis=1) - on; gs, ls = np.nonzero((on == 1) & (before < CAP))
                ask[q, gs, e - 1, before[gs, ls]] = sl[q, gs, e - 1, k[gs, ls]]
            v = f[gi, :, s]
            z = np.sum(v[:, :, :15] * w[r], axis=2) & (Q - 1); d = ((z * z >> 5) + 97 * t) & (Q - 1); d = np.where(d >= S, d - S, d)
            ok = done & (f[gi, 15, d] < 0); gs, ls = np.nonzero(ok)
            first = np.full((8, S), L, np.int64); np.minimum.at(first, (gs, d[gs, ls]), ls)
            gs, ls = np.nonzero(ok & (first[gi, d] == lane)); dd = d[gs, ls]
            new[r][gs, :15, dd] = (v[gs, ls, :15] + pl[r][gs, :15, dd & (M - 1)]) >> 1
            new[r][gs, 15, dd] = T0 + t; new[r][gs, 15, s[gs, ls]] = -1
        x = new; req = ask
    return {"y": x.reshape(N, 128, S).astype(np.float32).astype(BF)}

@@ -1,0 +1,658 @@
+from concourse.bass import DstId, RemoteDMATransfer
+from concourse.mybir import dt, AluOpType, AxisListType, ActivationFunctionType
+
+ADD, SUB, MUL, MAX, MIN = AluOpType.add, AluOpType.subtract, AluOpType.mult, AluOpType.max, AluOpType.min
+GE, GT, LE, LT, EQ = AluOpType.is_ge, AluOpType.is_gt, AluOpType.is_le, AluOpType.is_lt, AluOpType.is_equal
+SHR, AND = AluOpType.arith_shift_right, AluOpType.bitwise_and
+IDEN, COPY = ActivationFunctionType.Identity, ActivationFunctionType.Copy
+
+N, S, G, CAP, WN, M, RO, H, T0 = 8, 3328, 112, 16, 144, 512, 3, 4, 192
+OWN = 512
+NULL = S + (N - 1) * G
+FW = OWN + NULL + 16
+BW = 120
+K17 = 17 * 8192
+OFS = 99 * K17
+NV = 16
+RR = 4
+NC = NV // RR
+MAGIC = 12582912.0
+K1 = 2
+
+SCRATCH = {}
+for _n, _w, _t in (
+        ("f", FW, "bfloat16"), ("nbw", NULL + 16, "int32"), ("pl", M, "bfloat16"), ("wti", 1, "int32"), ("wni", 27, "int32"), ("sdi", 49, "int32"),
+        ("sdp", 56, "uint16"), ("sdf", 56, "float32"), ("sdw", 800, "float32"), ("sdx", 784, "float32"), ("wl", 30, "uint16"), ("rep", 50, "uint16"),
+        ("wq", 432, "float32"), ("jf", 128, "float32"), ("jmf", 256, "float32"), ("j4", 128, "float32"), ("j7", 128, "float32"), ("j3", 64, "float32"),
+        ("ji", 64, "int32"), ("cols", 40, "float32"), ("idf", 128, "float32"), ("idh", 128, "float16"), ("idb", 128, "bfloat16"),
+        ("mask", 256, "float32"), ("rep8", 8, "uint16"), ("rep87", 16, "uint16"), ("blk", 128, "float32"), ("wm", 24, "bfloat16"),
+        ("wa", 24, "bfloat16"), ("wb", 264, "bfloat16"), ("wz", 8, "bfloat16"), ("ws", 8, "bfloat16"), ("rsm", 128, "float32"), ("rsa", 112, "float32"),
+        ("rs8", 128, "float32"), ("tril", 128, "bfloat16"), ("ones", 128, "bfloat16"), ("k9", 8, "bfloat16"), ("ec", 128, "float32"), ("onf", 128, "float32"),
+        ("gm", 64, "float32"), ("b", 256, "bfloat16"), ("xx", 256, "float32"), ("dx", 256, "float32"), ("dl", 16, "uint16"), ("dlm", 16, "uint16"),
+        ("fd", 256, "bfloat16"), ("uu", 256, "bfloat16"), ("uv", 256, "float32"), ("val", 512, "bfloat16"), ("ex", 256, "float16"), ("da", 256, "float16"),
+        ("trash", 256, "bfloat16"), ("ofl", 32, "uint16"), ("on", 128, "bfloat16"), ("qb", 128, "float32"), ("qs", 128, "float32"),
+        ("mh", 256, "bfloat16"), ("ek", 128, "bfloat16"), ("rq", 64, "float32"), ("gg", 7 * BW, "bfloat16"), ("ld0", 7 * BW, "bfloat16"),
+        ("ld1", 7 * BW, "bfloat16"), ("ld2", 7 * BW, "bfloat16"), ("rki", 8, "uint16"), ("qa", 128, "float32"), ("qc", 128, "float32")):
+    SCRATCH[_n] = ("sbuf", [128, _w], _t)
+for _x in "AB":
+    for _n, _w, _t in (("l", 8, "uint16"), ("off", 128, "uint16"), ("a", 2048, "bfloat16"), ("m", 2048, "bfloat16"), ("cp", 128, "float32"),
+                       ("t1", 128, "float32"), ("u", 128, "float32"), ("k", 128, "float32"), ("sc", 128, "float32")):
+        SCRATCH[_n + _x] = ("sbuf", [128, _w], _t)
+for _n, _t in (("jm3", "float32"), ("dg", "bfloat16"), ("dgs", "float32"), ("trw", "float32"), ("tru", "float32")):
+    SCRATCH[_n] = ("sbuf", [128, 16, 16], _t)
+SCRATCH["e3"] = ("sbuf", [128, 16, 272], "bfloat16")
+for _n in ("accA", "accB", "bpA", "bpB", "q1", "q2", "q3"):
+    SCRATCH[_n] = ("psum", [128, 512], "float32")
+SCRATCH["tri3"] = ("psum", [128, 16, 16], "float32")
+PSUMS = [k for k in SCRATCH if SCRATCH[k][0] == "psum"]
+ALIAS = {}
+for _buf, _t, _names in (
+        ("tf", "float32", (("sL", 16), ("idp", 16), ("alive", 16), ("dT", 16), ("em", 16), ("dmu", 16), ("dc", 16), ("cnt", 16), ("eb", 16), ("kq", 16), ("se", 16),
+                           ("ucode", 16), ("uc2", 16), ("dLc", 16), ("c113", 8), ("rk", 8), ("cm", 8), ("sfA", 8), ("sfB", 8), ("fl", 16), ("base", 32),
+                           ("basm", 32), ("w2", 32), ("of", 32), ("a12", 32), ("wf", 32))),
+        ("ti", "int32", (("vi", 16), ("id0", 16), ("id1", 16), ("zi", 16), ("zm", 16), ("zq", 16), ("zh", 16), ("zg", 16), ("dLi", 16), ("dLm", 16),
+                         ("ebi", 16), ("rpi", 8), ("ci", 8)))):
+    _o = 0
+    for _n, _w in _names:
+        ALIAS[_n] = (_buf, _o, _w)
+        _o += _w
+    SCRATCH[_buf] = ("sbuf", [128, _o], _t)
+SEMAPHORES = ["sv", "ss", "sp", "sg"] + ["d%d" % i for i in range(12)] + ["arr0", "arr1", "arr2"] + ["snd%d" % i for i in range(9)]
+
+
+def R(name, lo=None, hi=None, step=None, rows=128, extra=None):
+    if name in ALIAS:
+        buf, o, w = ALIAS[name]
+        return (buf, o + (0 if lo is None else lo), o + (w if hi is None else hi), step, rows, extra)
+    return (name, lo, hi, step, rows, extra)
+
+
+def rank_program(g, core, T, topo):
+    rank = T.rank_of(core)
+    if rank is None:
+        return
+    qs = {"v": g.vector, "s": g.scalar, "p": g.tensor, "g": g, "y": g.sync}
+    semof = {"v": "sv", "s": "ss", "p": "sp", "g": "sg"}
+    cnt = {"v": 0, "s": 0, "p": 0, "g": 0}
+    known = {"v": {}, "s": {}, "p": {}, "g": {}, "y": {}}
+    hist = {}
+    dman = [0]
+    sent = {}
+
+    def ap(r):
+        name, lo, hi, step, rows, extra = r
+        t = T[name]
+        if extra is not None:
+            return t[(slice(0, rows),) + extra]
+        if lo is None:
+            return t[:] if rows == 128 else t[0:rows]
+        return t[0:rows, lo:hi] if step is None else t[0:rows, lo:hi:step]
+
+    def span(r):
+        name, lo, hi, step, rows, extra = r
+        if extra is not None and not isinstance(extra[0], slice):
+            return name, 1000 * extra[0], 1000 * extra[0] + 1000
+        if name in PSUMS or lo is None:
+            return name, 0, 1 << 20
+        return name, lo, hi
+
+    def emit(q, fn, reads, writes, sem=None, inc=1, dma=False):
+        acc = [(span(r), False) for r in reads] + [(span(r), True) for r in writes]
+        deps = []
+        for (name, lo, hi), w in acc:
+            for rec in hist.get(name, ()):
+                if rec[1] <= lo or rec[0] >= hi:
+                    continue
+                same = rec[3] == q and not dma and not rec[7]
+                if same and name in PSUMS and q == "p":
+                    need = False
+                elif name in PSUMS and not same:
+                    need = True
+                else:
+                    need = rec[2] or w
+                if need:
+                    deps.append(rec)
+        deps.sort(key=lambda rec: -len(rec[6]) * 100000 - rec[5])
+        kn = known[q]
+        for rec in deps:
+            if kn.get(rec[4], 0) >= rec[5]:
+                continue
+            val = rec[5]
+            for o in deps:
+                if o[4] == rec[4]:
+                    val = max(val, o[5])
+            qs[q].wait_ge(T.sem[rec[4]], val)
+            kn[rec[4]] = val
+            for o in deps:
+                if o[4] == rec[4] and o[5] <= val:
+                    for k, v in o[6].items():
+                        if kn.get(k, 0) < v:
+                            kn[k] = v
+        ins = fn()
+        if sem is None:
+            sem = semof[q]
+            cnt[q] += 1
+            val = cnt[q]
+            ins.then_inc(T.sem[sem], 1)
+        else:
+            val = inc
+        snap = dict(kn)
+        snap[sem] = val
+        for (name, lo, hi), w in acc:
+            lst = hist.get(name, [])
+            if w:
+                lst = [rec for rec in lst if not (rec[0] >= lo and rec[1] <= hi)]
+            else:
+                lst = [rec for rec in lst if not (not rec[2] and rec[3] == q and rec[4] == sem and rec[0] >= lo and rec[1] <= hi)]
+            lst.append((lo, hi, w, q, sem, val, snap, dma))
+            hist[name] = lst
+        return ins
+
+    def dma(q, out, in_, outr, inr):
+        sem = "d%d" % dman[0]
+        dman[0] += 1
+        emit(q, lambda: qs[q].dma_start(out, in_).then_inc(T.sem[sem], 16), inr, outr, sem=sem, inc=16, dma=True)
+
+    def ts(out, in0, s1, s2, o0, o1=None, ind=None):
+        rd = [in0] + [x for x in (s1, s2, ind) if isinstance(x, tuple)]
+        a1 = ap(s1) if isinstance(s1, tuple) else s1
+        a2 = ap(s2) if isinstance(s2, tuple) else s2
+        i0 = ap(in0).indirect(ap(ind)) if ind else ap(in0)
+        if o1 is None:
+            emit("v", lambda: g.vector.tensor_scalar(ap(out), i0, a1, None, o0), rd, [out])
+        else:
+            emit("v", lambda: g.vector.tensor_scalar(ap(out), i0, a1, a2, o0, o1), rd, [out])
+
+    def tt(out, in0, in1, op, ind=None):
+        i0 = ap(in0).indirect(ap(ind)) if ind else ap(in0)
+        emit("v", lambda: g.vector.tensor_tensor(ap(out), i0, ap(in1), op), [in0, in1] + ([ind] if ind else []), [out])
+
+    def tc(out, in_, ind=None, oind=None):
+        i0 = ap(in_).indirect(ap(ind)) if ind else ap(in_)
+        o = ap(out).indirect(ap(oind)) if oind else ap(out)
+        emit("v", lambda: g.vector.tensor_copy(o, i0), [in_] + ([ind] if ind else []) + ([oind] if oind else []), [out])
+
+    def scan(out, d0, d1, init, o0, o1):
+        emit("v", lambda: g.vector.tensor_tensor_scan(ap(out), ap(d0), ap(d1), init, o0, o1), [d0, d1], [out])
+
+    def ms(out, c):
+        emit("v", lambda: g.vector.memset(ap(out), c), [], [out])
+
+    def act(out, in_, func, bias=None, scale=None, ind=None, accum=None):
+        i0 = ap(in_).indirect(ap(ind)) if ind else ap(in_)
+        kw = {}
+        rd = [in_] + ([ind] if ind else [])
+        wr = [out]
+        if bias is not None:
+            kw["bias"] = ap(bias)
+            rd.append(bias)
+        if scale is not None:
+            kw["scale"] = ap(scale)
+            rd.append(scale)
+        if accum is not None:
+            kw["accum_out"] = ap(accum)
+            wr.append(accum)
+        emit("s", lambda: g.scalar.activation(ap(out), i0, func, **kw), rd, wr)
+
+    def mm(out, lhsT, rhs, start, stop):
+        emit("p", lambda: g.tensor.matmul(ap(out), ap(lhsT), ap(rhs), start, stop), [lhsT, rhs], [out])
+
+    def iota(out, pattern, base, cmul, flt=True):
+        if flt:
+            emit("g", lambda: g.iota(ap(out), pattern, base, cmul, allow_small_or_imprecise_dtypes=True), [], [out])
+        else:
+            emit("g", lambda: g.iota(ap(out), pattern, base, cmul), [], [out])
+
+    COL = {}
+
+    def col(name):
+        if name not in COL:
+            COL[name] = len(COL)
+        return R("cols", COL[name], COL[name] + 1)
+
+    hx = S // 2
+    dma("y", T.sdi[:], T.snd[:], [R("sdi")], [])
+    dma("s", T.f[:, OWN + hx:OWN + S], T.x0[:, hx:S], [R("f", OWN + hx, OWN + S)], [])
+    dma("y", T.f[:, OWN:OWN + hx], T.x0[:, 0:hx], [R("f", OWN, OWN + hx)], [])
+    dma("s", T.wti[:], T.wt[:], [R("wti")], [])
+    dma("y", T.wni[:], T.wants[:], [R("wni")], [])
+    dma("s", T.nbw[:, hx:S], T.nb[:, hx:S], [R("nbw", hx, S)], [])
+    dma("y", T.nbw[:, 0:hx], T.nb[:, 0:hx], [R("nbw", 0, hx)], [])
+    dma("y", T.pl[:], T.pull[:], [R("pl")], [])
+
+    iota(R("ci", 0, 1), [[0, 1]], 0, 1, False)
+    iota(R("jf"), [[1, 128]], 0, 0)
+    iota(R("jmf"), [[0, 16], [1, 16]], 0, 0)
+    iota(R("j4"), [[1, 8], [0, 16]], 0, 0)
+    iota(R("ji"), [[1, 64]], 0, 0, False)
+    iota(R("nbw", S, NULL + 1), [[1, NULL + 1 - S]], S, 0, False)
+
+    ms(R("gg"), 0.0)
+    for nm in ("id0", "id1"):
+        ms(R(nm), 0)
+    ms(R("alive"), 0.0)
+    ms(R("cnt"), 0.0)
+    ms(R("q1", 0, 64), 0.0)
+    ms(R("q3", 0, 128), 0.0)
+    ms(R("f", OWN + NULL, FW), -1.0)
+    ms(R("ones"), 1.0)
+    ms(R("k9"), -11.0 * K17)
+    ms(R("wm", 0, 8), 0.0)
+    ms(R("wa", 16, 24), 0.0)
+    ts(R("ci", 1, 2), R("ci", 0, 1), 15, None, AND)
+    ts(R("ci", 2, 3), R("ci", 0, 1), 4, None, SHR)
+    tc(col("p"), R("ci", 0, 1))
+    tc(col("q"), R("ci", 1, 2))
+    tc(col("g"), R("ci", 2, 3))
+    ts(R("ci", 3, 4), R("ci", 1, 2), 3, None, SHR)
+    for e in range(7):
+        tc(R("sdp", 8 * e, 8 * e + 7), R("sdi", 7 * e, 7 * e + 7))
+    P34, P26 = float(2 ** 34), float(2 ** 26)
+    ts(col("r15"), col("q"), 15.0, None, EQ)
+    ts(col("rl"), col("q"), 15.0, None, LT)
+    ts(col("b2"), col("r15"), 2.0, None, MUL)
+    ts(col("nb"), col("q"), -8192.0, -8192.0 - OFS, MUL, ADD)
+    ts(col("k17"), col("r15"), float(K17), None, MUL)
+    ts(col("t34"), col("rl"), P34, None, MUL)
+    ts(col("m34"), col("rl"), -P34, None, MUL)
+    ts(col("m26"), col("r15"), -P26, None, MUL)
+    tt(col("mt2"), col("m34"), col("m26"), ADD)
+    ts(R("cm"), R("jf", 0, 8), col("g"), None, EQ)
+    ts(R("idf"), R("jf"), col("p"), None, EQ)
+    ts(R("blk"), R("j4"), col("g"), None, EQ)
+    act(R("idb"), R("idf"), COPY)
+    for k in (1, 2):
+        act(R("wm", 8 * k, 8 * k + 8), R("cm"), COPY, scale=col("t34"))
+    act(R("wa", 0, 8), R("cm"), COPY, scale=col("k17"))
+    act(R("wa", 8, 16), R("cm"), COPY, scale=col("m34"))
+    act(R("wb", 0, 128), R("blk"), COPY, scale=col("m26"))
+    act(R("wb", 128, 256), R("blk"), COPY, scale=col("mt2"))
+    act(R("wb", 256, 264), R("cm"), COPY, scale=col("k17"))
+    act(R("ws"), R("cm"), COPY, scale=col("r15"))
+    ts(R("mask"), R("jmf"), col("q"), None, EQ)
+    ts(R("rsm"), R("jmf", 0, 128), 0.0, -1e29, EQ, MUL)
+
+    off = [e for e in range(1, 8) if topo.chip(T.cores[(rank + e) % N]) != topo.chip(core)]
+    near = [e for e in range(1, 8) if e not in off]
+    calls = [off[0:4], off[4:] + near]
+
+    def ghosts(t):
+        order = calls[0] + calls[1]
+        for e in order:
+            o, w, i = R("gg", (e - 1) * BW, (e - 1) * BW + G), R("f", OWN, OWN + S), R("sdp", 8 * (e - 1), 8 * e - 1)
+            if e == order[-1] or (t == 0 and e in order[-3:]):
+                tc(o, w, ind=i)
+            else:
+                act(o, w, COPY, ind=i)
+
+    def engines_of(src, es, e):
+        me = T.cores[src]
+        away = [x for x in es if topo.chip(T.cores[(src + x) % N]) != topo.chip(me)]
+        out = {}
+        used = []
+        for x in away + [y for y in es if y not in away]:
+            eng = topo.engines(me, T.cores[(src + x) % N])
+            free = [y for y in eng if y not in used]
+            room = len(eng) // len(away) if x in away else len(free)
+            n = 1
+            while n * 2 <= room:
+                n *= 2
+            out[x] = free[0:n]
+            used = used + out[x]
+        return out[e]
+
+    def send(t):
+        for k, es in enumerate(calls):
+            trs = []
+            inc = 0
+            for e in es:
+                dst = T.cores[(rank + e) % N]
+                mine = engines_of(rank, es, e)
+                rid, pid, se = topo.addr(dst)
+                mk = 0
+                for x in mine:
+                    mk += 1 << x
+                p = 7 - e
+                trs.append(RemoteDMATransfer(dst_ids=[DstId(rid=rid, pnc=pid)], dma_engine_mask=mk, remote_sem=T.sem["arr%d" % t],
+                                             srcs=[T.gg[:, (e - 1) * BW:e * BW]], dsts=[T["ld%d" % t][:, p * BW:(p + 1) * BW]]))
+                inc += len(mine)
+            sem = "snd%d" % (3 * t + k)
+            emit("g", lambda: g.remote_dma_fused(trs, local_sem=T.sem[sem]), [R("gg", (e - 1) * BW, e * BW) for e in es], [], sem=sem, inc=inc, dma=True)
+            sent[sem] = inc
+        arrived = 0
+        for e in range(1, 8):
+            src = (rank - e) % N
+            soff = [x for x in range(1, 8) if topo.chip(T.cores[(src + x) % N]) != topo.chip(T.cores[src])]
+            snear = [x for x in range(1, 8) if x not in soff]
+            arrived += len(engines_of(src, soff[0:4] if e in soff[0:4] else soff[4:] + snear, e))
+        hist["ld%d" % t] = [(0, 1 << 20, True, "r", "arr%d" % t, arrived, {}, True)]
+
+    ghosts(0)
+    send(0)
+    iota(R("j7"), [[0, 16], [1, 8]], 0, 0)
+    iota(R("j3"), [[1, 8], [0, 8]], 0, 0)
+    iota(R("jm3"), [[0, 16], [1, 16]], 0, 0)
+    iota(R("c113"), [[113, 8]], 0, 0)
+
+    tc(R("rep"), R("ji", 0, 50))
+    tc(R("wl", 0, 9), R("wni", 0, 9))
+    ms(R("wf"), 0.0)
+    tc(R("wf", 0, 27), R("wni"))
+    tt(R("wq", 0, 144), R("wf", 0, 32), R("mask", 0, 144), MUL, ind=R("rep", 0, 9))
+
+    def setup_hops():
+        tc(col("wt"), R("wti"))
+        tt(col("wtl"), col("wt"), col("rl"), MUL)
+        act(R("wz"), R("cm"), COPY, scale=col("wtl"))
+        ts(col("neg"), col("r15"), -1.0, None, MUL)
+        ts(col("half"), col("rl"), 0.5, None, MUL)
+        ts(col("q0"), col("rl"), -0.25, None, MUL)
+        for t in range(RO):
+            ts(col("st%d" % t), col("r15"), float(T0 + t), None, MUL)
+            tt(col("nb%d" % t), col("st%d" % t), col("q0"), ADD)
+        for t in (1, 2):
+            tc(R("wl", 10 * t + 1, 10 * t + 10), R("wni", 9 * t, 9 * t + 9))
+        tc(R("idh"), R("idf"))
+        ts(R("rs8"), R("j7"), 0.0, None, GT)
+        ts(R("ec"), R("j7"), -1.0, 7.0, MUL, ADD)
+        ts(R("onf"), R("j7"), 7.0, 99.0, EQ, MUL)
+        tt(R("ec"), R("ec"), R("onf"), ADD)
+        ts(R("tril"), R("jf"), col("p"), None, GT)
+        ts(R("gm"), R("j3"), col("g"), None, EQ)
+        ts(R("trw"), R("jm3"), col("q"), 1.5, LT, MUL)
+        ts(R("tru"), R("jm3"), col("q"), -0.5, LE, MUL)
+        tt(R("tri3"), R("trw"), R("tru"), ADD)
+        ts(R("base"), R("jf", 0, 32), 16.0, col("q"), MUL, ADD)
+        ts(R("basm"), R("base"), float(-OWN), None, ADD)
+        for h in (0, 1):
+            ts(R("ucode", 8 * h, 8 * h + 8), R("jf", 0, 8), 0.0, float(S - 2048 + 128 * h), MUL, ADD)
+        ts(R("ucode"), R("ucode"), col("p"), None, ADD)
+        ts(R("uc2"), R("ucode"), 2048.0, None, ADD)
+        tc(col("q8"), R("ci", 3, 4))
+        ts(R("rk"), R("jf", 0, 8), 2.0, col("q8"), MUL, ADD)
+        tc(R("rep8"), R("rk"))
+        ts(R("zi"), R("ji", 0, 16), 8.0, 7.0, MUL, ADD)
+        tc(R("rep87"), R("zi"))
+
+    def setup_later():
+        for t in (1, 2):
+            w0 = 8 * ((9 * t) // 8)
+            for lo, n in ((0, 8), (8, 1)):
+                ts(R("rpi", 0, n), R("ji", 0, n), float(9 * t - w0 + lo), None, ADD)
+                tc(R("rki", 0, n), R("rpi", 0, n))
+                tt(R("wq", 144 * t + 16 * lo, 144 * t + 16 * lo + 16 * n), R("wf", w0, 32), R("mask", 0, 16 * n), MUL, ind=R("rki", 0, n))
+        tc(R("sdf", 0, 49), R("sdi"))
+        ms(R("sdf", 49, 56), 0.0)
+        for lo in range(0, 49, 16):
+            hi = min(49, lo + 16)
+            tt(R("sdx", 16 * lo, 16 * hi), R("sdf"), R("mask", 0, 16 * (hi - lo)), MUL, ind=R("rep", lo, hi))
+        ms(R("sdw", 0, 784, 113), float(NULL))
+        ts(R("rsa"), R("jmf", 0, 112), 0.0, None, GT)
+        for lo, hi in ((0, 4 * G), (4 * G, 7 * G)):
+            mm(R("q2", 0, hi - lo), R("blk"), R("sdx", lo, hi), True, True)
+            for e in range(lo // G, hi // G):
+                act(R("sdw", 113 * e + 1, 113 * e + 113), R("q2", e * G - lo, (e + 1) * G - lo), COPY)
+
+    def stream(X, t):
+        h = 0 if X == "A" else 1
+        nc = (4, 5)[h] if t == 0 else 8
+        c0 = 0 if h == 0 else (4 if t == 0 else 8)
+        return {"X": X, "h": h, "nl": 16 * nc, "nc": nc, "c0": c0, "l0": 16 * c0, "hop": 1, "t": t}
+
+    def start(st):
+        X, t, h, nl = st["X"], st["t"], st["h"], st["nl"]
+        if t == 0:
+            st["list"] = R("wl", st["c0"], st["c0"] + st["nc"])
+            src = R("wq", st["l0"], st["l0"] + nl)
+        elif h == 1:
+            st["list"] = R("wl", 10 * t + 2, 10 * t + 10)
+            src = R("wq", 144 * t + 16, 144 * t + 144)
+        else:
+            tt(R("rk", 0, 7), R("ld%d" % t, G, 7 * BW, BW), R("c113", 0, 7), ADD)
+            tc(R("rki", 0, 7), R("rk", 0, 7))
+            tt(R("qa", 0, 112), R("sdw", 0, 791), R("mask", 0, 112), MUL, ind=R("rki", 0, 7))
+            tc(R("lA", 7, 8), R("wl", 10 * t + 1, 10 * t + 2))
+            scan(R("qc", 0, 112), R("rsa"), R("qa", 0, 112), 0.0, MUL, ADD)
+            tc(R("lA", 0, 7), R("qc", 15, 112, 16))
+            act(R("qa", 112, 128), R("wq", 144 * t, 144 * t + 16), COPY)
+            st["list"] = R("lA")
+            src = R("qa")
+        mm(R("acc" + X, 408, 416, rows=nl), src, R("cm"), True, True)
+        nbg(st)
+        tc(R("idp", 8 * h, 8 * h + 8, rows=nl), R("acc" + X, 408, 416, rows=nl))
+
+    def nbg(st):
+        X, nl = st["X"], st["nl"]
+        tc(R("off" + X, 0, nl), R("nbw"), ind=st["list"])
+
+    def compv(st):
+        X, nl = st["X"], st["nl"]
+        ts(R("cp" + X, 0, nl), R("off" + X, 0, nl), col("nb"), None, ADD)
+
+    def bgat(st):
+        X, h, nl, l0 = st["X"], st["h"], st["nl"], st["l0"]
+        bb = R("b", l0, l0 + nl)
+        ts(bb, R("f", OWN, FW), col("b2"), None, ADD, ind=st["list"])
+        for j in range(RR):
+            mm(R("bp" + X, j, RR * nl, RR), R("idb"), bb, True, True)
+        mm(R("acc" + X, 128, 392, rows=nl), bb, R("wb"), True, False)
+        mm(R("acc" + X, 384, 392, rows=nl), R("ones", 0, nl, rows=9), R("k9", rows=9), False, False)
+        mm(R("acc" + X, 0, 128, rows=nl), R("cp" + X, 0, nl), R("idf"), False, False)
+        if st["hop"] == H:
+            mm(R("q1", 8 * h, 8 * h + 8, rows=nl), bb, R("wz"), True, True)
+
+    def chunk(st, k):
+        n2 = 64 if st["nl"] == 128 else 32
+        return (0, n2) if k == 0 else (n2, st["nl"])
+
+    def agat(st, k):
+        X = st["X"]
+        lo, hi = chunk(st, k)
+        act(R("a" + X, 16 * lo, 16 * hi), R("f", OWN, FW), IDEN, bias=col("b2"), ind=R("off" + X, lo, hi))
+
+    def amm(st):
+        X, nl = st["X"], st["nl"]
+        for n in range(NV):
+            mm(R("acc" + X, n, 384, 16, rows=nl), R("a" + X, n, 16 * nl, 16), R("wa"), False, False)
+
+    def maxes(st, k, ns):
+        X, nl = st["X"], st["nl"]
+        lo, hi = chunk(st, k)
+        for n in ns:
+            tt(R("m" + X, RR * (n * nl + lo), RR * (n * nl + hi)), R("a" + X, 16 * lo + n, 16 * hi, NC), R("bp" + X, RR * lo, RR * hi), MAX)
+            if k == 1:
+                for j in range(RR):
+                    mm(R("acc" + X, n + NC * j, 384, 16, rows=nl), R("m" + X, RR * n * nl + j, RR * (n + 1) * nl, RR), R("wm"), False,
+                       n == NC - 1 and j == RR - 1)
+
+    def tail(st):
+        X, h, nl, hop = st["X"], st["h"], st["nl"], st["hop"]
+        acc = "acc" + X
+        hh = (8 * h, 8 * h + 8)
+        tc(R("t1" + X, rows=nl), R(acc, 128, 256, rows=nl))
+        tt(R("u" + X, rows=nl), R("t1" + X, rows=nl), R(acc, 256, 384, rows=nl), MIN)
+        tt(R("k" + X, rows=nl), R("u" + X, rows=nl), R(acc, 0, 128, rows=nl), MIN)
+        tt(R("sf" + X, rows=nl), R("idp" if hop == 1 else "id%d" % (1 - hop % 2), hh[0], hh[1], rows=nl), R(acc, 384, 392, rows=nl), ADD)
+        scan(R("sc" + X, rows=nl), R("rsm", rows=nl), R("k" + X, rows=nl), -1e29, ADD, MAX)
+        if hop == 1:
+            ts(R("alive", hh[0], hh[1], rows=nl), R(acc, 384, 392, rows=nl), 1.5 * K17 - OFS, None, GE)
+        tt(R("vi", hh[0], hh[1], rows=nl), R("sc" + X, 15, 128, 16, rows=nl), R("sf" + X, rows=nl), MAX)
+        ts(R("id%d" % (hop % 2), hh[0], hh[1], rows=nl), R("vi", hh[0], hh[1], rows=nl), 8191, None, AND)
+        if hop < H:
+            tt(R("xx", 128 * h, 128 * h + 128), R("id%d" % (hop % 2), hh[0], hh[1]), R("mask", 0, 128), MUL, ind=R("rep", 0, 8))
+            mm(R(acc, 400, 400 + st["nc"]), R("xx", 128 * h, 128 * h + 128, rows=nl), R("cm", 0, st["nc"], rows=nl), True, True)
+
+    def nextlist(st):
+        X, hop, nc = st["X"], st["hop"], st["nc"]
+        tc(R("l" + X, 0, nc), R("acc" + X, 400, 400 + nc))
+        st["list"] = R("l" + X, 0, nc)
+        nbg(st)
+        if hop == H - 1:
+            tc(R("sL", st["c0"], st["c0"] + nc), R("acc" + X, 400, 400 + nc))
+        st["hop"] = hop + 1
+
+    def places(t, sts):
+        tc(R("zi"), R("q1", 0, 16))
+        ts(R("zm"), R("zi"), 4095, None, AND)
+        tt(R("zq"), R("zm"), R("zm"), MUL)
+        if t:
+            ts(R("zi"), R("zq"), float(97 * 32 * t), None, ADD)
+        ts(R("zh"), R("zi" if t else "zq"), 5, 4095, SHR, AND)
+        ts(R("zg"), R("zh"), float(S), float(-S), GE, MUL)
+        tt(R("dT"), R("zh"), R("zg"), ADD)
+        tt(R("dx"), R("dT"), R("mask", 0, 256), MUL, ind=R("rep", 0, 16))
+        for st in sts:
+            mm(R("q1", 16 + st["c0"], 16 + st["c0"] + st["nc"]), R("dx", 128 * st["h"], 128 * st["h"] + 128, rows=st["nl"]),
+               R("cm", 0, st["nc"], rows=st["nl"]), True, True)
+
+    def places2(t, sts):
+        nc = sum(st["nc"] for st in sts)
+        L = 16 * nc
+        tc(R("dLi", 0, nc), R("q1", 16, 16 + nc))
+        tc(R("dl", 0, nc), R("dLi", 0, nc))
+        act(R("fd", 0, L), R("f", OWN, OWN + S), COPY, ind=R("dl", 0, nc))
+        ts(R("dLm", 0, nc), R("dLi", 0, nc), M - 1, None, AND)
+        tc(R("dlm", 0, nc), R("dLm", 0, nc))
+        act(R("uu", 0, L), R("pl"), COPY, ind=R("dlm", 0, nc))
+        ts(R("dLc", 0, nc), R("dLi", 0, nc), -2048.0, None, ADD)
+        tt(R("dmu"), R("dT"), R("uc2"), SUB)
+        ts(R("se"), R("id1"), float(S), None, LT)
+        tt(R("se"), R("se"), R("alive"), MUL)
+        tt(R("dmu"), R("dmu"), R("se"), MUL)
+        tt(R("a12", 0, nc), R("dLi", 0, nc), R("basm", 0, nc), SUB)
+        tt(R("a12", nc, 2 * nc), R("sL", 0, nc), R("basm", nc, 2 * nc), SUB)
+
+    def places3(t, sts):
+        nc = sum(st["nc"] for st in sts)
+        L = 16 * nc
+        for st in sts:
+            mm(R("q1", 32 + 8 * st["h"], 40 + 8 * st["h"], rows=st["nl"]), R("fd", st["l0"], st["l0"] + st["nl"]), R("ws"), True, True)
+        mm(R("q2", 0, L), R("idb"), R("uu", 0, L), True, False)
+        mm(R("q2", 0, L), R("idb"), R("b", 0, L), False, True)
+        ts(R("em"), R("q1", 32, 48), 0.0, None, LT)
+        tt(R("dmu"), R("em"), R("dmu"), MUL)
+
+    def moves(t, sts):
+        nc = sum(st["nc"] for st in sts)
+        L = 16 * nc
+        act(R("uv", 0, L), R("q2", 0, L), IDEN, bias=col("nb%d" % t), scale=col("half"))
+        act(R("val", L, 2 * L), R("b", 0, L), IDEN, bias=col("neg"), scale=col("rl"))
+        tt(R("se"), R("id0"), R("id1"), EQ)
+        tt(R("dc"), R("se"), R("dmu"), MUL)
+        tt(R("dc"), R("dc"), R("ucode"), ADD)
+        tc(R("ex"), R("dc"), ind=R("rep", 0, 16))
+        for st in sts:
+            mm(R("q2", st["l0"], st["l0"] + st["nl"]), R("ex", 128 * st["h"], 128 * st["h"] + 128, rows=st["nl"]), R("idh", 0, st["nl"], rows=st["nl"]), True, True)
+        ts(R("val", 0, L), R("uv", 0, L), MAGIC, -MAGIC, ADD, ADD)
+        tc(R("da", 0, L), R("q2", 0, L))
+        for c in range(nc - 1, -1, -1):
+            ts(R("e3", extra=(c, slice(256 - 16 * c, 272))), R("da", 0, 16 * c + 16), R("dLc", c, c + 1), None, EQ)
+            if c:
+                act(R("trash", 0, 16 * c), R("e3", extra=(c, slice(256 - 16 * c, 256))), COPY, accum=R("cnt", c, c + 1))
+        sl = slice(0, nc)
+        tt(R("dg", extra=(sl, slice(0, 16))), R("e3", extra=(sl, slice(256, 272))), R("tri3", extra=(sl, slice(0, 16))), MUL)
+        for w in (8, 4, 2, 1):
+            src = "dg" if w == 8 else "dgs"
+            tt(R("dgs", extra=(sl, slice(0, w))), R(src, extra=(sl, slice(0, w))), R(src, extra=(sl, slice(w, 2 * w))), ADD)
+
+    def moves2(t, sts):
+        nc = sum(st["nc"] for st in sts)
+        L = 16 * nc
+        tt(R("fl", 0, nc), R("cnt", 0, nc), R("dgs", extra=(slice(0, nc), 0)), ADD)
+        for k in (0, nc):
+            ts(R("w2", k, k + nc), R("fl", 0, nc), -0.25, None, LT)
+        tt(R("of", 0, 2 * nc), R("w2", 0, 2 * nc), R("a12", 0, 2 * nc), MUL)
+        tt(R("of", 0, 2 * nc), R("of", 0, 2 * nc), R("base", 0, 2 * nc), ADD)
+        tc(R("ofl", 0, 2 * nc), R("of", 0, 2 * nc))
+        tc(R("f", 0, OWN + S), R("val", 0, 2 * L), oind=R("ofl", 0, 2 * nc))
+
+    def requests(sts, part):
+        if part == 0:
+            ts(R("ebi"), R("id0"), 1.0 / G, 1.0 - (S + (G - 1) / 2) / G, MUL, ADD)
+            tt(R("eb"), R("ebi"), R("alive"), MUL)
+            ts(R("kq"), R("ebi"), float(-G), float(-(S - G - 1)), MUL, ADD)
+            tt(R("kq"), R("kq"), R("id0"), ADD)
+            tt(R("on"), R("eb"), R("ec"), EQ, ind=R("rep8"))
+            for st in sts:
+                nl, h = st["nl"], st["h"]
+                if h == 0:
+                    mm(R("q3", 0, 64, rows=nl), R("tril", 0, nl, rows=nl), R("on", 0, 64, rows=nl), True, True)
+                else:
+                    n0 = sts[0]["nl"]
+                    mm(R("q3", 64, 128, rows=nl), R("tril", 0, nl, rows=nl), R("on", 64, 128, rows=nl), True, False)
+                    mm(R("q3", 64, 128, rows=nl), R("ones", 0, nl, rows=n0), R("on", 0, 64, rows=n0), False, True)
+        elif part == 1:
+            tt(R("qb"), R("on"), R("q3", 0, 128), MUL)
+            scan(R("qs"), R("rs8"), R("qb"), 0.0, MUL, ADD)
+            tt(R("mh"), R("qs"), R("jmf"), EQ, ind=R("rep87"))
+            tt(R("ek"), R("kq"), R("on"), MUL, ind=R("rep8"))
+            for st in sts:
+                nl, h = st["nl"], st["h"]
+                mm(R("q3", 128, 192), R("mh", 128 * h, 128 * h + 128, rows=nl), R("ek", 64 * h, 64 * h + 64, rows=nl), h == 0, h == 1)
+        else:
+            tt(R("rq"), R("gm"), R("q3", 128, 192), MUL)
+            tt(R("rq", 0, 32), R("rq", 0, 32), R("rq", 32, 64), ADD)
+            tt(R("rq", 0, 16), R("rq", 0, 16), R("rq", 16, 32), ADD)
+            tt(R("gg", G, 7 * BW, BW), R("rq", 0, 7), R("rq", 8, 15), ADD)
+
+    def landed(t):
+        for e in range(1, 8):
+            o, i = R("f", OWN + S + (e - 1) * G, OWN + S + e * G), R("ld%d" % t, (7 - e) * BW, (7 - e) * BW + G)
+            if e in (2, 4, 6):
+                act(o, i, COPY)
+            else:
+                tc(o, i)
+
+    for t in range(RO):
+        A, B = stream("A", t), stream("B", t)
+        sts = (A, B)
+        order = (A, B) if t == 0 else (B, A)
+        if t == 1:
+            setup_later()
+        start(order[0])
+        compv(order[0])
+        if t == 0:
+            setup_hops()
+        landed(t)
+        for slot in range(2 * H):
+            X, Y = order[slot % 2], order[1 - slot % 2]
+            last = slot == 2 * H - 1
+            if slot:
+                compv(X)
+            bgat(X)
+            agat(X, 0)
+            if slot == 0:
+                start(Y)
+                maxes(X, 0, range(NC))
+            else:
+                tail(Y)
+                maxes(X, 0, range(0, K1))
+                if last:
+                    places(t, sts)
+                else:
+                    nextlist(Y)
+                maxes(X, 0, range(K1, NC))
+            agat(X, 1)
+            amm(X)
+            if last:
+                places2(t, sts)
+            maxes(X, 1, range(NC))
+        places3(t, sts)
+        tail(order[1])
+        moves(t, sts)
+        if t + 1 < RO:
+            requests(sts, 0)
+        moves2(t, sts)
+        if t + 1 < RO:
+            requests(sts, 1)
+            ghosts(t + 1)
+            requests(sts, 2)
+            send(t + 1)
+    emit("y", lambda: g.sync.dma_start(T.y[:], T.f[:, OWN:OWN + S]).then_inc(T.sem["d11"], 16), [R("f", OWN, OWN + S)], [], sem="d11", inc=16, dma=True)
+    g.sync.wait_ge(T.sem["d11"], 16)
+    for q in ("v", "s", "p", "g"):
+        g.wait_ge(T.sem[semof[q]], cnt[q])
+    for name, val in sorted(sent.items()):
+        g.wait_ge(T.sem[name], val)
+    for i in range(dman[0]):
+        g.wait_ge(T.sem["d%d" % i], 16)

@@ -4,7 +4,7 @@ from concourse.mybir import dt, AluOpType, AxisListType, ActivationFunctionType
 ADD, SUB, MUL, MAX, MIN = AluOpType.add, AluOpType.subtract, AluOpType.mult, AluOpType.max, AluOpType.min
 GE, GT, LE, LT, EQ = AluOpType.is_ge, AluOpType.is_gt, AluOpType.is_le, AluOpType.is_lt, AluOpType.is_equal
 SHR, AND = AluOpType.arith_shift_right, AluOpType.bitwise_and
-IDEN, COPY = ActivationFunctionType.Identity, ActivationFunctionType.Copy
+IDEN, COPY, RELU, EXP = ActivationFunctionType.Identity, ActivationFunctionType.Copy, ActivationFunctionType.Relu, ActivationFunctionType.Exp
 
 N, S, G, CAP, WN, M, RO, H, T0 = 8, 3328, 112, 16, 144, 512, 3, 4, 192
 OWN = 512
@@ -12,59 +12,114 @@ NULL = S + (N - 1) * G
 FW = OWN + NULL + 16
 BW = 120
 K17 = 17 * 8192
-OFS = 99 * K17
+MID = 97
 NV = 16
 RR = 4
 NC = NV // RR
 MAGIC = 12582912.0
-K1 = 2
+PEN = float(2 ** 26)
+DECAY = 1.04
+CHUNKS = {128: (48, 48, 32), 80: (48, 32), 64: (32, 32)}
 
 SCRATCH = {}
 for _n, _w, _t in (
-        ("f", FW, "bfloat16"), ("nbw", NULL + 16, "int32"), ("pl", M, "bfloat16"), ("wti", 1, "int32"), ("wni", 27, "int32"), ("sdi", 49, "int32"),
+        ("f", FW, "bfloat16"), ("nbw", NULL + 16, "int32"), ("pl", OWN + S, "bfloat16"), ("wti", 1, "int32"), ("wni", 27, "int32"), ("sdi", 49, "int32"),
         ("sdp", 56, "uint16"), ("sdf", 56, "float32"), ("sdw", 800, "float32"), ("sdx", 784, "float32"), ("wl", 30, "uint16"), ("rep", 50, "uint16"),
-        ("wq", 432, "float32"), ("jf", 128, "float32"), ("jmf", 256, "float32"), ("j4", 128, "float32"), ("j7", 128, "float32"), ("j3", 64, "float32"),
-        ("ji", 64, "int32"), ("cols", 40, "float32"), ("idf", 128, "float32"), ("idh", 128, "float16"), ("idb", 128, "bfloat16"),
-        ("mask", 256, "float32"), ("rep8", 8, "uint16"), ("rep87", 16, "uint16"), ("blk", 128, "float32"), ("wm", 24, "bfloat16"),
-        ("wa", 24, "bfloat16"), ("wb", 264, "bfloat16"), ("wz", 8, "bfloat16"), ("ws", 8, "bfloat16"), ("rsm", 128, "float32"), ("rsa", 112, "float32"),
-        ("rs8", 128, "float32"), ("tril", 128, "bfloat16"), ("ones", 128, "bfloat16"), ("k9", 8, "bfloat16"), ("ec", 128, "float32"), ("onf", 128, "float32"),
-        ("gm", 64, "float32"), ("b", 256, "bfloat16"), ("xx", 256, "float32"), ("dx", 256, "float32"), ("dl", 16, "uint16"), ("dlm", 16, "uint16"),
-        ("fd", 256, "bfloat16"), ("uu", 256, "bfloat16"), ("uv", 256, "float32"), ("val", 512, "bfloat16"), ("ex", 256, "float16"), ("da", 256, "float16"),
-        ("trash", 256, "bfloat16"), ("ofl", 32, "uint16"), ("on", 128, "bfloat16"), ("qb", 128, "float32"), ("qs", 128, "float32"),
-        ("mh", 256, "bfloat16"), ("ek", 128, "bfloat16"), ("rq", 64, "float32"), ("gg", 7 * BW, "bfloat16"), ("ld0", 7 * BW, "bfloat16"),
-        ("ld1", 7 * BW, "bfloat16"), ("ld2", 7 * BW, "bfloat16"), ("rki", 8, "uint16"), ("qa", 128, "float32"), ("qc", 128, "float32")):
+        ("wq", 432, "float32"), ("jf", 128, "float32"), ("jmf", 256, "float32"), ("jm1", 256, "float32"), ("j4", 128, "float32"), ("j7", 128, "float32"),
+        ("j16", 64, "float32"), ("ji", 64, "int32"), ("cols", 40, "float32"), ("idf", 128, "float32"), ("idh", 128, "float16"), ("idb", 128, "bfloat16"),
+        ("nid", 128, "bfloat16"), ("mask", 256, "float32"), ("rep8", 8, "uint16"), ("rep87", 16, "uint16"), ("gl", 2, "uint16"), ("blk", 128, "float32"),
+        ("wa", 24, "bfloat16"), ("wb", 256, "bfloat16"), ("mpen", 128, "bfloat16"), ("wz", 8, "bfloat16"), ("ws", 8, "bfloat16"), ("ww", 80, "bfloat16"), ("wwf", 64, "float32"),
+        ("cm2", 8, "bfloat16"), ("rsm", 128, "float32"), ("rsa", 128, "float32"), ("rs8", 128, "float32"), ("tril", 128, "bfloat16"), ("ones", 128, "bfloat16"),
+        ("mhalf", 256, "bfloat16"), ("ec", 128, "float32"), ("onf", 128, "float32"), ("b", 256, "bfloat16"), ("xx", 256, "float32"), ("dx", 256, "float32"),
+        ("x1", 256, "float32"), ("x2", 256, "bfloat16"), ("dl", 16, "uint16"), ("fb", 32, "bfloat16"), ("fd", 256, "bfloat16"), ("uu", 256, "bfloat16"),
+        ("uv", 256, "float32"), ("val", 512, "bfloat16"), ("ex", 256, "float16"), ("da", 256, "float16"), ("ofl", 32, "uint16"), ("on", 128, "bfloat16"),
+        ("qs", 128, "float32"), ("mh", 256, "float16"), ("ek", 128, "float16"), ("rq", 64, "float32"), ("gg", 16 * BW, "bfloat16"), ("ld0", 7 * BW, "bfloat16"),
+        ("ld1", 7 * BW, "bfloat16"), ("ld2", 7 * BW, "bfloat16"), ("rki", 8, "uint16"), ("rkj", 8, "uint16"), ("qa", 128, "float32"), ("qc", 128, "float32")):
     SCRATCH[_n] = ("sbuf", [128, _w], _t)
 for _x in "AB":
     for _n, _w, _t in (("l", 8, "uint16"), ("off", 128, "uint16"), ("a", 2048, "bfloat16"), ("m", 2048, "bfloat16"), ("cp", 128, "float32"),
-                       ("t1", 128, "float32"), ("u", 128, "float32"), ("k", 128, "float32"), ("sc", 128, "float32")):
+                       ("th", 128, "float32"), ("u", 128, "float32"), ("k", 128, "float32"), ("sc", 128, "float32")):
         SCRATCH[_n + _x] = ("sbuf", [128, _w], _t)
-for _n, _t in (("jm3", "float32"), ("dg", "bfloat16"), ("dgs", "float32"), ("trw", "float32"), ("tru", "float32")):
-    SCRATCH[_n] = ("sbuf", [128, 16, 16], _t)
-SCRATCH["e3"] = ("sbuf", [128, 16, 272], "bfloat16")
-for _n in ("accA", "accB", "bpA", "bpB", "q1", "q2", "q3"):
+SCRATCH["e3"] = ("sbuf", [128, 16 * 256], "bfloat16")
+for _n in ("a1A", "a1B", "a2A", "a2B", "bpA", "bpB", "q1", "q2"):
     SCRATCH[_n] = ("psum", [128, 512], "float32")
-SCRATCH["tri3"] = ("psum", [128, 16, 16], "float32")
 PSUMS = [k for k in SCRATCH if SCRATCH[k][0] == "psum"]
 ALIAS = {}
 for _buf, _t, _names in (
-        ("tf", "float32", (("sL", 16), ("idp", 16), ("alive", 16), ("dT", 16), ("em", 16), ("dmu", 16), ("dc", 16), ("cnt", 16), ("eb", 16), ("kq", 16), ("se", 16),
-                           ("ucode", 16), ("uc2", 16), ("dLc", 16), ("c113", 8), ("rk", 8), ("cm", 8), ("sfA", 8), ("sfB", 8), ("fl", 16), ("base", 32),
-                           ("basm", 32), ("w2", 32), ("of", 32), ("a12", 32), ("wf", 32))),
-        ("ti", "int32", (("vi", 16), ("id0", 16), ("id1", 16), ("zi", 16), ("zm", 16), ("zq", 16), ("zh", 16), ("zg", 16), ("dLi", 16), ("dLm", 16),
-                         ("ebi", 16), ("rpi", 8), ("ci", 8)))):
+        ("tf", "float32", (("dT", 16), ("cand", 16), ("first", 16), ("eb", 16), ("idm", 16), ("ce", 16), ("c112", 8), ("rk", 8), ("rl8", 8), ("cm", 8), ("sfA", 8),
+                           ("sfB", 8), ("base", 32), ("of", 32), ("a12", 32), ("wf", 32))),
+        ("ti", "int32", (("vi", 16), ("id0", 16), ("id1", 16), ("zi", 16), ("zm", 16), ("zq", 16), ("zh", 16), ("zg", 16), ("ebi", 16), ("rpi", 8), ("ci", 8),
+                         ("z7", 16)))):
     _o = 0
     for _n, _w in _names:
         ALIAS[_n] = (_buf, _o, _w)
         _o += _w
     SCRATCH[_buf] = ("sbuf", [128, _o], _t)
-SEMAPHORES = ["sv", "ss", "sp", "sg"] + ["d%d" % i for i in range(12)] + ["arr0", "arr1", "arr2"] + ["snd%d" % i for i in range(9)]
+SEMAPHORES = ["sv", "ss", "sp", "sg"] + ["d%d" % i for i in range(12)] + ["arr%d" % i for i in range(6)] + ["snd%d" % i for i in range(6)]
+
+CYC, GATHER, SCATTER, PECYC, WAKE = 0.00090, 1.45, 3.0, 0.00055, 0.12
+FILL = 0.12
 
 
-def R(name, lo=None, hi=None, step=None, rows=128, extra=None):
+def R(name, lo=None, hi=None, step=None, rows=128):
     if name in ALIAS:
         buf, o, w = ALIAS[name]
-        return (buf, o + (0 if lo is None else lo), o + (w if hi is None else hi), step, rows, extra)
-    return (name, lo, hi, step, rows, extra)
+        return (buf, o + (0 if lo is None else lo), o + (w if hi is None else hi), step, rows)
+    if lo is None:
+        return (name, 0, SCRATCH[name][1][1], None, rows)
+    return (name, lo, hi, step, rows)
+
+
+def width(r):
+    return len(range(r[1], r[2], r[3] or 1))
+
+
+def narrow(*rs):
+    return all(SCRATCH[r[0]][2] in ("bfloat16", "float16", "uint16") for r in rs)
+
+
+def in_order(ops):
+    n = len(ops)
+    users = [[] for _ in range(n)]
+    for i, o in enumerate(ops):
+        for d in o["deps"]:
+            users[d].append(i)
+    prio = [0.0] * n
+    for i in range(n - 1, -1, -1):
+        o = ops[i]
+        prio[i] = o["occ"] + max([o["lat"]] + [prio[u] + (o["lat"] if ops[u]["deps"][i] else 0.0) for u in users[i]])
+    left = [len(o["deps"]) for o in ops]
+    ready_at = [0.0] * n
+    cand = {}
+    for i, o in enumerate(ops):
+        cand.setdefault(o["q"], [])
+        if not left[i]:
+            cand[o["q"]].append(i)
+    free = {q: 0.0 for q in cand}
+    out = []
+    while len(out) < n:
+        q = min((x for x in cand if cand[x]), key=lambda x: max(free[x], min(ready_at[i] for i in cand[x])))
+        now = max(free[q], min(ready_at[i] for i in cand[q]))
+        here = sorted((i for i in cand[q] if ready_at[i] <= now), key=lambda i: (-prio[i], i))
+        top = max(cand[q], key=lambda i: (prio[i], -i))
+        pick = None
+        for i in here:
+            go = max(now + prio[i], max(now + ops[i]["occ"], ready_at[top]) + prio[top])
+            hold = max(ready_at[top] + prio[top], ready_at[top] + ops[top]["occ"] + prio[i])
+            if i == top or go <= hold + FILL:
+                pick = i
+                break
+        if pick is None:
+            pick, now = top, ready_at[top]
+        cand[q].remove(pick)
+        out.append((now, len(out), pick))
+        free[q] = now + ops[pick]["occ"]
+        for u in users[pick]:
+            ready_at[u] = max(ready_at[u], free[q] + (ops[pick]["lat"] if ops[u]["deps"][pick] else 0.0))
+            left[u] -= 1
+            if not left[u]:
+                cand[ops[u]["q"]].append(u)
+    return [i for _, _, i in out]
 
 
 def rank_program(g, core, T, topo):
@@ -73,135 +128,122 @@ def rank_program(g, core, T, topo):
         return
     qs = {"v": g.vector, "s": g.scalar, "p": g.tensor, "g": g, "y": g.sync}
     semof = {"v": "sv", "s": "ss", "p": "sp", "g": "sg"}
-    cnt = {"v": 0, "s": 0, "p": 0, "g": 0}
-    known = {"v": {}, "s": {}, "p": {}, "g": {}, "y": {}}
+    ops = []
     hist = {}
     dman = [0]
-    sent = {}
+    turn = []
 
     def ap(r):
-        name, lo, hi, step, rows, extra = r
-        t = T[name]
-        if extra is not None:
-            return t[(slice(0, rows),) + extra]
-        if lo is None:
-            return t[:] if rows == 128 else t[0:rows]
-        return t[0:rows, lo:hi] if step is None else t[0:rows, lo:hi:step]
+        name, lo, hi, step, rows = r
+        return T[name][0:rows, lo:hi] if step is None else T[name][0:rows, lo:hi:step]
 
-    def span(r):
-        name, lo, hi, step, rows, extra = r
-        if extra is not None and not isinstance(extra[0], slice):
-            return name, 1000 * extra[0], 1000 * extra[0] + 1000
-        if name in PSUMS or lo is None:
-            return name, 0, 1 << 20
-        return name, lo, hi
-
-    def emit(q, fn, reads, writes, sem=None, inc=1, dma=False):
-        acc = [(span(r), False) for r in reads] + [(span(r), True) for r in writes]
-        deps = []
-        for (name, lo, hi), w in acc:
-            for rec in hist.get(name, ()):
-                if rec[1] <= lo or rec[0] >= hi:
-                    continue
-                same = rec[3] == q and not dma and not rec[7]
-                if same and name in PSUMS and q == "p":
-                    need = False
-                elif name in PSUMS and not same:
-                    need = True
-                else:
-                    need = rec[2] or w
-                if need:
-                    deps.append(rec)
-        deps.sort(key=lambda rec: -len(rec[6]) * 100000 - rec[5])
-        kn = known[q]
-        for rec in deps:
-            if kn.get(rec[4], 0) >= rec[5]:
-                continue
-            val = rec[5]
-            for o in deps:
-                if o[4] == rec[4]:
-                    val = max(val, o[5])
-            qs[q].wait_ge(T.sem[rec[4]], val)
-            kn[rec[4]] = val
-            for o in deps:
-                if o[4] == rec[4] and o[5] <= val:
-                    for k, v in o[6].items():
-                        if kn.get(k, 0) < v:
-                            kn[k] = v
-        ins = fn()
-        if sem is None:
-            sem = semof[q]
-            cnt[q] += 1
-            val = cnt[q]
-            ins.then_inc(T.sem[sem], 1)
-        else:
-            val = inc
-        snap = dict(kn)
-        snap[sem] = val
-        for (name, lo, hi), w in acc:
+    def record(q, fn, reads, writes, occ, lat=WAKE, sem=None, inc=1, after=()):
+        me = len(ops)
+        deps = {d: True for d in after}
+        acc = [(r, False) for r in reads] + [(r, True) for r in writes]
+        for r, w in acc:
+            name, bank = r[0], r[0] in PSUMS
+            for lo, hi, ow, oq, o in hist.get(name, ()):
+                if bank and oq == q == "p":
+                    deps.setdefault(o, False)
+                elif (bank and oq != q) or ((w or ow) and lo < r[2] and r[1] < hi):
+                    deps[o] = True
+        for r, w in acc:
+            name, bank = r[0], r[0] in PSUMS
             lst = hist.get(name, [])
-            if w:
-                lst = [rec for rec in lst if not (rec[0] >= lo and rec[1] <= hi)]
-            else:
-                lst = [rec for rec in lst if not (not rec[2] and rec[3] == q and rec[4] == sem and rec[0] >= lo and rec[1] <= hi)]
-            lst.append((lo, hi, w, q, sem, val, snap, dma))
-            hist[name] = lst
-        return ins
+            if bank and q == "p":
+                lst = []
+            elif bank and lst and lst[-1][3] != q:
+                lst = [x for x in lst if x[3] == lst[-1][3]]
+            elif w and not bank and r[3] is None and r[4] == 128:
+                lst = [x for x in lst if not (x[0] >= r[1] and x[1] <= r[2])]
+            hist[name] = lst + [(r[1], r[2], w, q if sem is None else None, me)]
+        ops.append({"q": q, "fn": fn, "deps": deps, "occ": occ, "lat": lat, "sem": sem, "inc": inc})
+        return me
 
-    def dma(q, out, in_, outr, inr):
+    def emit_all():
+        cnt = {q: 0 for q in semof}
+        known = {q: {} for q in qs}
+        done = {}
+        for i in in_order(ops):
+            o = ops[i]
+            q = o["q"]
+            if o["fn"] is None:
+                done[i] = (o["sem"], o["inc"], {})
+                continue
+            need = {}
+            for d, wait in o["deps"].items():
+                if wait and done[d][1] > need.get(done[d][0], (0,))[0]:
+                    need[done[d][0]] = (done[d][1], done[d][2])
+            kn = known[q]
+            for sem in sorted(need, key=lambda s: -len(need[s][1])):
+                val, snap = need[sem]
+                if kn.get(sem, 0) >= val:
+                    continue
+                qs[q].wait_ge(T.sem[sem], val)
+                kn[sem] = val
+                for k, v in snap.items():
+                    if kn.get(k, 0) < v:
+                        kn[k] = v
+            ins = o["fn"]()
+            if o["sem"] is None:
+                cnt[q] += 1
+                ins.then_inc(T.sem[semof[q]], 1)
+                done[i] = (semof[q], cnt[q], dict(kn))
+            else:
+                done[i] = (o["sem"], o["inc"], dict(kn))
+        for q in semof:
+            g.wait_ge(T.sem[semof[q]], cnt[q])
+        for o in ops:
+            if o["sem"] is not None and known["g"].get(o["sem"], 0) < o["inc"]:
+                g.wait_ge(T.sem[o["sem"]], o["inc"])
+
+    def dma(q, out, in_, outr, inr, lat, after=()):
         sem = "d%d" % dman[0]
         dman[0] += 1
-        emit(q, lambda: qs[q].dma_start(out, in_).then_inc(T.sem[sem], 16), inr, outr, sem=sem, inc=16, dma=True)
+        return record(q, lambda: qs[q].dma_start(out, in_).then_inc(T.sem[sem], 16), inr, outr, 0.05, lat, sem, 16, after)
+
+    def vcost(out, ins, ind, both=False):
+        if ind:
+            return 0.05 + width(out) * GATHER * CYC
+        return 0.02 + max(64, width(out) * (2 if both else 0.5 if narrow(out, *ins) else 1)) * CYC
+
+    def src(r, ind):
+        return ap(r).indirect(ap(ind)) if ind else ap(r)
 
     def ts(out, in0, s1, s2, o0, o1=None, ind=None):
         rd = [in0] + [x for x in (s1, s2, ind) if isinstance(x, tuple)]
-        a1 = ap(s1) if isinstance(s1, tuple) else s1
-        a2 = ap(s2) if isinstance(s2, tuple) else s2
-        i0 = ap(in0).indirect(ap(ind)) if ind else ap(in0)
-        if o1 is None:
-            emit("v", lambda: g.vector.tensor_scalar(ap(out), i0, a1, None, o0), rd, [out])
-        else:
-            emit("v", lambda: g.vector.tensor_scalar(ap(out), i0, a1, a2, o0, o1), rd, [out])
+        a = [ap(x) if isinstance(x, tuple) else x for x in (s1, s2)] + ([o0] if o1 is None else [o0, o1])
+        record("v", lambda: g.vector.tensor_scalar(ap(out), src(in0, ind), *a), rd, [out], vcost(out, [in0], ind))
 
     def tt(out, in0, in1, op, ind=None):
-        i0 = ap(in0).indirect(ap(ind)) if ind else ap(in0)
-        emit("v", lambda: g.vector.tensor_tensor(ap(out), i0, ap(in1), op), [in0, in1] + ([ind] if ind else []), [out])
+        both = in0[0] not in PSUMS and in1[0] not in PSUMS
+        record("v", lambda: g.vector.tensor_tensor(ap(out), src(in0, ind), ap(in1), op), [in0, in1] + ([ind] if ind else []), [out],
+               vcost(out, [("tf",)], ind, both))
 
     def tc(out, in_, ind=None, oind=None):
-        i0 = ap(in_).indirect(ap(ind)) if ind else ap(in_)
-        o = ap(out).indirect(ap(oind)) if oind else ap(out)
-        emit("v", lambda: g.vector.tensor_copy(o, i0), [in_] + ([ind] if ind else []) + ([oind] if oind else []), [out])
+        cost = 0.05 + width(in_) * SCATTER * CYC if oind else vcost(out, [in_], ind)
+        record("v", lambda: g.vector.tensor_copy(src(out, oind), src(in_, ind)), [in_] + [x for x in (ind, oind) if x], [out], cost)
 
     def scan(out, d0, d1, init, o0, o1):
-        emit("v", lambda: g.vector.tensor_tensor_scan(ap(out), ap(d0), ap(d1), init, o0, o1), [d0, d1], [out])
+        record("v", lambda: g.vector.tensor_tensor_scan(ap(out), ap(d0), ap(d1), init, o0, o1), [d0, d1], [out], vcost(out, [d0, d1], None))
 
     def ms(out, c):
-        emit("v", lambda: g.vector.memset(ap(out), c), [], [out])
+        record("v", lambda: g.vector.memset(ap(out), c), [], [out], vcost(out, [], None))
 
-    def act(out, in_, func, bias=None, scale=None, ind=None, accum=None):
-        i0 = ap(in_).indirect(ap(ind)) if ind else ap(in_)
-        kw = {}
-        rd = [in_] + ([ind] if ind else [])
-        wr = [out]
-        if bias is not None:
-            kw["bias"] = ap(bias)
-            rd.append(bias)
-        if scale is not None:
-            kw["scale"] = ap(scale)
-            rd.append(scale)
-        if accum is not None:
-            kw["accum_out"] = ap(accum)
-            wr.append(accum)
-        emit("s", lambda: g.scalar.activation(ap(out), i0, func, **kw), rd, wr)
+    def act(out, in_, func, bias=None, scale=None, ind=None, more=0.0):
+        kw = {k: (ap(v) if isinstance(v, tuple) else v) for k, v in (("bias", bias), ("scale", scale)) if v is not None}
+        rd = [in_] + [x for x in (ind, bias, scale) if isinstance(x, tuple)]
+        cost = 0.065 + width(out) * GATHER * CYC if ind else 0.02 + max(64, width(out)) * CYC
+        record("s", lambda: g.scalar.activation(ap(out), src(in_, ind), func, **kw), rd, [out], cost + more)
 
     def mm(out, lhsT, rhs, start, stop):
-        emit("p", lambda: g.tensor.matmul(ap(out), ap(lhsT), ap(rhs), start, stop), [lhsT, rhs], [out])
+        cost = max(min(64, width(lhsT)), width(rhs)) * (1 if narrow(lhsT) else 4) * PECYC
+        record("p", lambda: g.tensor.matmul(ap(out), ap(lhsT), ap(rhs), start, stop), [lhsT, rhs], [out], cost)
 
     def iota(out, pattern, base, cmul, flt=True):
-        if flt:
-            emit("g", lambda: g.iota(ap(out), pattern, base, cmul, allow_small_or_imprecise_dtypes=True), [], [out])
-        else:
-            emit("g", lambda: g.iota(ap(out), pattern, base, cmul), [], [out])
+        kw = {"allow_small_or_imprecise_dtypes": True} if flt else {}
+        record("g", lambda: g.iota(ap(out), pattern, base, cmul, **kw), [], [out], 0.13 + 2 * width(out) * CYC)
 
     COL = {}
 
@@ -211,14 +253,16 @@ def rank_program(g, core, T, topo):
         return R("cols", COL[name], COL[name] + 1)
 
     hx = S // 2
-    dma("y", T.sdi[:], T.snd[:], [R("sdi")], [])
-    dma("s", T.f[:, OWN + hx:OWN + S], T.x0[:, hx:S], [R("f", OWN + hx, OWN + S)], [])
-    dma("y", T.f[:, OWN:OWN + hx], T.x0[:, 0:hx], [R("f", OWN, OWN + hx)], [])
-    dma("s", T.wti[:], T.wt[:], [R("wti")], [])
-    dma("y", T.wni[:], T.wants[:], [R("wni")], [])
-    dma("s", T.nbw[:, hx:S], T.nb[:, hx:S], [R("nbw", hx, S)], [])
-    dma("y", T.nbw[:, 0:hx], T.nb[:, 0:hx], [R("nbw", 0, hx)], [])
-    dma("y", T.pl[:], T.pull[:], [R("pl")], [])
+    d0 = dma("y", T.sdi[:], T.snd[:], [R("sdi")], [], 2.0)
+    d1 = dma("s", T.f[:, OWN + hx:OWN + S], T.x0[:, hx:S], [R("f", OWN + hx, OWN + S)], [], 5.5)
+    d2 = dma("y", T.f[:, OWN:OWN + hx], T.x0[:, 0:hx], [R("f", OWN, OWN + hx)], [], 5.5)
+    last = {"y": d2, "s": d1}
+    ops[d2]["deps"][d0] = False
+    for q, o, i, r, lat in (("s", T.wti[:], T.wt[:], R("wti"), 6.0), ("y", T.wni[:], T.wants[:], R("wni"), 6.0), ("y", T.pl[:, 0:M], T.pull[:], R("pl", 0, M), 6.5),
+                            ("s", T.nbw[:, hx:S], T.nb[:, hx:S], R("nbw", hx, S), 14.0), ("y", T.nbw[:, 0:hx], T.nb[:, 0:hx], R("nbw", 0, hx), 14.0)):
+        d = dma(q, o, i, [r], [], lat)
+        ops[d]["deps"][last[q]] = False
+        last[q] = d
 
     iota(R("ci", 0, 1), [[0, 1]], 0, 1, False)
     iota(R("jf"), [[1, 128]], 0, 0)
@@ -226,72 +270,109 @@ def rank_program(g, core, T, topo):
     iota(R("j4"), [[1, 8], [0, 16]], 0, 0)
     iota(R("ji"), [[1, 64]], 0, 0, False)
     iota(R("nbw", S, NULL + 1), [[1, NULL + 1 - S]], S, 0, False)
-
-    ms(R("gg"), 0.0)
+    iota(R("j7"), [[0, 16], [1, 8]], 0, 0)
+    iota(R("j16"), [[16, 8], [0, 8]], 0, 0)
+    iota(R("c112"), [[G, 8]], 0, 0)
+    ms(R("gg", 0, 7 * BW), 0.0)
     for nm in ("id0", "id1"):
         ms(R(nm), 0)
-    ms(R("alive"), 0.0)
-    ms(R("cnt"), 0.0)
-    ms(R("q1", 0, 64), 0.0)
-    ms(R("q3", 0, 128), 0.0)
+    for r in (R("cand"), R("fb"), R("q1", 0, 96), R("bpA", 256, 384), R("f", 0, OWN)):
+        ms(r, 0.0)
+    for c in range(1, 16):
+        ms(R("e3", 256 * c + (0 if c < 8 else 64 if c == 8 else 128), 256 * c + 16 * c), 0.0)
     ms(R("f", OWN + NULL, FW), -1.0)
     ms(R("ones"), 1.0)
-    ms(R("k9"), -11.0 * K17)
-    ms(R("wm", 0, 8), 0.0)
-    ms(R("wa", 16, 24), 0.0)
+    ms(R("mhalf"), -0.5)
     ts(R("ci", 1, 2), R("ci", 0, 1), 15, None, AND)
     ts(R("ci", 2, 3), R("ci", 0, 1), 4, None, SHR)
-    tc(col("p"), R("ci", 0, 1))
-    tc(col("q"), R("ci", 1, 2))
-    tc(col("g"), R("ci", 2, 3))
     ts(R("ci", 3, 4), R("ci", 1, 2), 3, None, SHR)
+    for k, nm in enumerate(("p", "q", "g", "q8")):
+        tc(col(nm), R("ci", k, k + 1))
     for e in range(7):
         tc(R("sdp", 8 * e, 8 * e + 7), R("sdi", 7 * e, 7 * e + 7))
-    P34, P26 = float(2 ** 34), float(2 ** 26)
     ts(col("r15"), col("q"), 15.0, None, EQ)
     ts(col("rl"), col("q"), 15.0, None, LT)
-    ts(col("b2"), col("r15"), 2.0, None, MUL)
-    ts(col("nb"), col("q"), -8192.0, -8192.0 - OFS, MUL, ADD)
-    ts(col("k17"), col("r15"), float(K17), None, MUL)
-    ts(col("t34"), col("rl"), P34, None, MUL)
-    ts(col("m34"), col("rl"), -P34, None, MUL)
-    ts(col("m26"), col("r15"), -P26, None, MUL)
-    tt(col("mt2"), col("m34"), col("m26"), ADD)
+    for nm, of, c in (("mid", "r15", -MID), ("k17", "r15", K17), ("neg", "r15", -1), ("full", "r15", -4 * PEN), ("nrl", "rl", -1), ("mag", "rl", -MAGIC),
+                      ("big", "rl", 2 * PEN), ("nbig", "rl", -2 * PEN)):
+        ts(col(nm), col(of), float(c), None, MUL)
+    ts(col("nb"), col("q"), -8192.0, -8192.0, MUL, ADD)
+    for t in range(RO):
+        ts(col("vb%d" % t), col("r15"), float(T0 + t), col("mag"), MUL, ADD)
     ts(R("cm"), R("jf", 0, 8), col("g"), None, EQ)
     ts(R("idf"), R("jf"), col("p"), None, EQ)
     ts(R("blk"), R("j4"), col("g"), None, EQ)
-    act(R("idb"), R("idf"), COPY)
-    for k in (1, 2):
-        act(R("wm", 8 * k, 8 * k + 8), R("cm"), COPY, scale=col("t34"))
-    act(R("wa", 0, 8), R("cm"), COPY, scale=col("k17"))
-    act(R("wa", 8, 16), R("cm"), COPY, scale=col("m34"))
-    act(R("wb", 0, 128), R("blk"), COPY, scale=col("m26"))
-    act(R("wb", 128, 256), R("blk"), COPY, scale=col("mt2"))
-    act(R("wb", 256, 264), R("cm"), COPY, scale=col("k17"))
-    act(R("ws"), R("cm"), COPY, scale=col("r15"))
     ts(R("mask"), R("jmf"), col("q"), None, EQ)
-    ts(R("rsm"), R("jmf", 0, 128), 0.0, -1e29, EQ, MUL)
+    ts(R("rsm"), R("jmf", 0, 128), 0.0, -2 * PEN, EQ, MUL)
+    ts(R("rsa"), R("jmf", 0, 128), 0.0, None, GT)
+    ts(R("jm1"), R("jmf"), 1024.0, None, ADD)
+    tc(R("idh"), R("idf"))
+    tc(col("wt"), R("wti"))
+    tt(col("wtl"), col("wt"), col("rl"), MUL)
+    act(R("idb"), R("idf"), COPY)
+    act(R("nid"), R("idf"), COPY, scale=-PEN)
+    act(R("wa", 0, 8), R("cm"), COPY, scale=col("rl"))
+    act(R("wa", 8, 16), R("cm"), COPY, scale=col("k17"))
+    act(R("wa", 16, 24), R("cm"), COPY, scale=col("big"))
+    act(R("wb", 0, 128), R("blk"), COPY, scale=col("nrl"))
+    act(R("wb", 128, 256), R("blk"), COPY, scale=col("nbig"))
+    ms(R("mpen"), -PEN)
+    act(R("ws"), R("cm"), COPY, scale=col("full"))
+    act(R("wz"), R("cm"), COPY, scale=col("wtl"))
+    act(R("cm2"), R("cm"), COPY, scale=2.0)
+    for k in range(1, 8):
+        hi = min(M * (k + 1), OWN + S)
+        act(R("pl", M * k, hi), R("pl", 0, hi - M * k), COPY)
+    ts(col("wq"), col("q"), -DECAY, 62.0, MUL, ADD)
+    ts(col("wp"), col("p"), -DECAY, 62.74, MUL, ADD)
+    act(R("wwf"), R("j16"), EXP, bias=col("wq"), scale=-DECAY, more=1.3)
+    act(col("thr"), col("wp"), EXP)
+    ts(R("onf", 0, 64), R("j7", 0, 64), col("g"), None, EQ)
+    tt(R("ww", 0, 64), R("wwf"), R("onf", 0, 64), MUL)
+    act(R("ww", 64, 72), R("cm"), COPY, scale=float(2 ** 95))
+    ts(R("rs8"), R("j7"), 0.0, None, GT)
+    ts(R("ec"), R("j7"), -1.0, 7.0, MUL, ADD)
+    ts(R("onf"), R("j7"), 7.0, 50.0, EQ, MUL)
+    tt(R("ec"), R("ec"), R("onf"), ADD)
+    ts(R("onf"), R("jf"), col("p"), None, GT)
+    ts(R("qs"), R("idf"), 1024.0, None, MUL)
+    tt(R("tril"), R("onf"), R("qs"), ADD)
+    ts(R("ce"), R("jf", 0, 16), float(-G), float(6 * G), MUL, ADD)
+    ts(R("ce"), R("ce"), 0.0, None, MAX)
+    ts(col("g8"), col("g"), 8.0, None, MUL)
+    ts(R("gl", 0, 1), col("q"), 7.0, col("g8"), MIN, ADD)
+    ts(R("base"), R("jf", 0, 32), 16.0, col("q"), MUL, ADD)
+    tc(R("rep"), R("ji", 0, 50))
+    ts(R("rep8"), R("jf", 0, 8), 2.0, col("q8"), MUL, ADD)
+    ts(R("rep87"), R("jf", 0, 16), 8.0, 7.0, MUL, ADD)
+    tc(R("wl", 0, 9), R("wni", 0, 9))
+    for t in (1, 2):
+        tc(R("wl", 10 * t + 1, 10 * t + 10), R("wni", 9 * t, 9 * t + 9))
+    ms(R("wf"), 0.0)
+    tc(R("wf", 0, 27), R("wni"))
+    for lo in range(0, 27, 8):
+        hi = min(27, lo + 8)
+        tt(R("wq", 16 * lo, 16 * hi), R("wf"), R("mask", 0, 16 * (hi - lo)), MUL, ind=R("rep", lo, hi))
+    tc(R("sdf", 0, 49), R("sdi"))
+    ms(R("sdf", 49, 56), 0.0)
+    for lo in range(0, 49, 8):
+        hi = min(49, lo + 8)
+        tt(R("sdx", 16 * lo, 16 * hi), R("sdf"), R("mask", 0, 16 * (hi - lo)), MUL, ind=R("rep", lo, hi))
+    ms(R("sdw", 0, 1), float(NULL))
+    for lo, hi in ((0, 4 * G), (4 * G, 7 * G)):
+        mm(R("q2", 0, hi - lo), R("blk"), R("sdx", lo, hi), True, True)
+        act(R("sdw", 1 + lo, 1 + hi), R("q2", 0, hi - lo), COPY)
 
-    off = [e for e in range(1, 8) if topo.chip(T.cores[(rank + e) % N]) != topo.chip(core)]
-    near = [e for e in range(1, 8) if e not in off]
-    calls = [off[0:4], off[4:] + near]
+    def calls_of(r):
+        off = [e for e in range(1, N) if topo.chip(T.cores[(r + e) % N]) != topo.chip(T.cores[r])]
+        return [off[0:4], off[4:] + [e for e in range(1, N) if e not in off]]
 
-    def ghosts(t):
-        order = calls[0] + calls[1]
-        for e in order:
-            o, w, i = R("gg", (e - 1) * BW, (e - 1) * BW + G), R("f", OWN, OWN + S), R("sdp", 8 * (e - 1), 8 * e - 1)
-            if e == order[-1] or (t == 0 and e in order[-3:]):
-                tc(o, w, ind=i)
-            else:
-                act(o, w, COPY, ind=i)
-
-    def engines_of(src, es, e):
-        me = T.cores[src]
-        away = [x for x in es if topo.chip(T.cores[(src + x) % N]) != topo.chip(me)]
+    def engines_of(r, es):
+        me = T.cores[r]
+        away = [x for x in es if topo.chip(T.cores[(r + x) % N]) != topo.chip(me)]
         out = {}
         used = []
         for x in away + [y for y in es if y not in away]:
-            eng = topo.engines(me, T.cores[(src + x) % N])
+            eng = topo.engines(me, T.cores[(r + x) % N])
             free = [y for y in eng if y not in used]
             room = len(eng) // len(away) if x in away else len(free)
             n = 1
@@ -299,360 +380,221 @@ def rank_program(g, core, T, topo):
                 n *= 2
             out[x] = free[0:n]
             used = used + out[x]
-        return out[e]
+        return out
 
-    def send(t):
+    def exchange(t):
+        calls = calls_of(rank)
+        for k, e in enumerate(calls[0] + calls[1]):
+            o, w, i = R("gg", (e - 1) * BW, (e - 1) * BW + G), R("f", OWN, OWN + S), R("sdp", 8 * (e - 1), 8 * e - 1)
+            if k % 2:
+                tc(o, w, ind=i)
+            else:
+                act(o, w, COPY, ind=i)
+        sent = []
         for k, es in enumerate(calls):
+            eng = engines_of(rank, es)
             trs = []
-            inc = 0
             for e in es:
-                dst = T.cores[(rank + e) % N]
-                mine = engines_of(rank, es, e)
-                rid, pid, se = topo.addr(dst)
-                mk = 0
-                for x in mine:
-                    mk += 1 << x
-                p = 7 - e
-                trs.append(RemoteDMATransfer(dst_ids=[DstId(rid=rid, pnc=pid)], dma_engine_mask=mk, remote_sem=T.sem["arr%d" % t],
-                                             srcs=[T.gg[:, (e - 1) * BW:e * BW]], dsts=[T["ld%d" % t][:, p * BW:(p + 1) * BW]]))
-                inc += len(mine)
-            sem = "snd%d" % (3 * t + k)
-            emit("g", lambda: g.remote_dma_fused(trs, local_sem=T.sem[sem]), [R("gg", (e - 1) * BW, e * BW) for e in es], [], sem=sem, inc=inc, dma=True)
-            sent[sem] = inc
-        arrived = 0
-        for e in range(1, 8):
-            src = (rank - e) % N
-            soff = [x for x in range(1, 8) if topo.chip(T.cores[(src + x) % N]) != topo.chip(T.cores[src])]
-            snear = [x for x in range(1, 8) if x not in soff]
-            arrived += len(engines_of(src, soff[0:4] if e in soff[0:4] else soff[4:] + snear, e))
-        hist["ld%d" % t] = [(0, 1 << 20, True, "r", "arr%d" % t, arrived, {}, True)]
-
-    ghosts(0)
-    send(0)
-    iota(R("j7"), [[0, 16], [1, 8]], 0, 0)
-    iota(R("j3"), [[1, 8], [0, 8]], 0, 0)
-    iota(R("jm3"), [[0, 16], [1, 16]], 0, 0)
-    iota(R("c113"), [[113, 8]], 0, 0)
-
-    tc(R("rep"), R("ji", 0, 50))
-    tc(R("wl", 0, 9), R("wni", 0, 9))
-    ms(R("wf"), 0.0)
-    tc(R("wf", 0, 27), R("wni"))
-    tt(R("wq", 0, 144), R("wf", 0, 32), R("mask", 0, 144), MUL, ind=R("rep", 0, 9))
-
-    def setup_hops():
-        tc(col("wt"), R("wti"))
-        tt(col("wtl"), col("wt"), col("rl"), MUL)
-        act(R("wz"), R("cm"), COPY, scale=col("wtl"))
-        ts(col("neg"), col("r15"), -1.0, None, MUL)
-        ts(col("half"), col("rl"), 0.5, None, MUL)
-        ts(col("q0"), col("rl"), -0.25, None, MUL)
-        for t in range(RO):
-            ts(col("st%d" % t), col("r15"), float(T0 + t), None, MUL)
-            tt(col("nb%d" % t), col("st%d" % t), col("q0"), ADD)
-        for t in (1, 2):
-            tc(R("wl", 10 * t + 1, 10 * t + 10), R("wni", 9 * t, 9 * t + 9))
-        tc(R("idh"), R("idf"))
-        ts(R("rs8"), R("j7"), 0.0, None, GT)
-        ts(R("ec"), R("j7"), -1.0, 7.0, MUL, ADD)
-        ts(R("onf"), R("j7"), 7.0, 99.0, EQ, MUL)
-        tt(R("ec"), R("ec"), R("onf"), ADD)
-        ts(R("tril"), R("jf"), col("p"), None, GT)
-        ts(R("gm"), R("j3"), col("g"), None, EQ)
-        ts(R("trw"), R("jm3"), col("q"), 1.5, LT, MUL)
-        ts(R("tru"), R("jm3"), col("q"), -0.5, LE, MUL)
-        tt(R("tri3"), R("trw"), R("tru"), ADD)
-        ts(R("base"), R("jf", 0, 32), 16.0, col("q"), MUL, ADD)
-        ts(R("basm"), R("base"), float(-OWN), None, ADD)
-        for h in (0, 1):
-            ts(R("ucode", 8 * h, 8 * h + 8), R("jf", 0, 8), 0.0, float(S - 2048 + 128 * h), MUL, ADD)
-        ts(R("ucode"), R("ucode"), col("p"), None, ADD)
-        ts(R("uc2"), R("ucode"), 2048.0, None, ADD)
-        tc(col("q8"), R("ci", 3, 4))
-        ts(R("rk"), R("jf", 0, 8), 2.0, col("q8"), MUL, ADD)
-        tc(R("rep8"), R("rk"))
-        ts(R("zi"), R("ji", 0, 16), 8.0, 7.0, MUL, ADD)
-        tc(R("rep87"), R("zi"))
-
-    def setup_later():
-        for t in (1, 2):
-            w0 = 8 * ((9 * t) // 8)
-            for lo, n in ((0, 8), (8, 1)):
-                ts(R("rpi", 0, n), R("ji", 0, n), float(9 * t - w0 + lo), None, ADD)
-                tc(R("rki", 0, n), R("rpi", 0, n))
-                tt(R("wq", 144 * t + 16 * lo, 144 * t + 16 * lo + 16 * n), R("wf", w0, 32), R("mask", 0, 16 * n), MUL, ind=R("rki", 0, n))
-        tc(R("sdf", 0, 49), R("sdi"))
-        ms(R("sdf", 49, 56), 0.0)
-        for lo in range(0, 49, 16):
-            hi = min(49, lo + 16)
-            tt(R("sdx", 16 * lo, 16 * hi), R("sdf"), R("mask", 0, 16 * (hi - lo)), MUL, ind=R("rep", lo, hi))
-        ms(R("sdw", 0, 784, 113), float(NULL))
-        ts(R("rsa"), R("jmf", 0, 112), 0.0, None, GT)
-        for lo, hi in ((0, 4 * G), (4 * G, 7 * G)):
-            mm(R("q2", 0, hi - lo), R("blk"), R("sdx", lo, hi), True, True)
-            for e in range(lo // G, hi // G):
-                act(R("sdw", 113 * e + 1, 113 * e + 113), R("q2", e * G - lo, (e + 1) * G - lo), COPY)
+                rid, pid, se = topo.addr(T.cores[(rank + e) % N])
+                there = calls_of(rank)
+                trs.append(RemoteDMATransfer(dst_ids=[DstId(rid=rid, pnc=pid)], dma_engine_mask=sum(1 << x for x in eng[e]), remote_sem=T.sem["arr%d" % (2 * t + k)],
+                                             srcs=[T.gg[:, (e - 1) * BW:e * BW]], dsts=[T["ld%d" % t][:, (7 - e) * BW:(8 - e) * BW]]))
+            sem = "snd%d" % (2 * t + k)
+            sent.append(record("g", lambda trs=trs, sem=sem: g.remote_dma_fused(trs, local_sem=T.sem[sem]), [R("gg", (e - 1) * BW, e * BW) for e in es], [],
+                               2.5 if t + k == 0 else 0.6, 5.0, sem, sum(len(x) for x in eng.values()), ()))
+        ops[sent[1]]["deps"].setdefault(sent[0], False)
+        for k in (0, 1):
+            es = [e for e in range(1, N) if e in calls_of((rank - e) % N)[k]]
+            n = sum(len(engines_of((rank - e) % N, calls_of((rank - e) % N)[k])[e]) for e in es)
+            record("r", None, [], [R("ld%d" % t, (7 - e) * BW, (8 - e) * BW) for e in es], 0.0, 0.0, "arr%d" % (2 * t + k), n, [sent[k]])
+            for j, e in enumerate(es):
+                o, i = R("f", OWN + S + (e - 1) * G, OWN + S + e * G), R("ld%d" % t, (7 - e) * BW, (7 - e) * BW + G)
+                if j % 2:
+                    act(o, i, COPY)
+                else:
+                    tc(o, i)
 
     def stream(X, t):
         h = 0 if X == "A" else 1
         nc = (4, 5)[h] if t == 0 else 8
         c0 = 0 if h == 0 else (4 if t == 0 else 8)
-        return {"X": X, "h": h, "nl": 16 * nc, "nc": nc, "c0": c0, "l0": 16 * c0, "hop": 1, "t": t}
+        return {"X": X, "h": h, "nl": 16 * nc, "nc": nc, "c0": c0, "l0": 16 * c0, "t": t}
 
     def start(st):
-        X, t, h, nl = st["X"], st["t"], st["h"], st["nl"]
+        t, h, nl = st["t"], st["h"], st["nl"]
         if t == 0:
             st["list"] = R("wl", st["c0"], st["c0"] + st["nc"])
-            src = R("wq", st["l0"], st["l0"] + nl)
+            st["diag"] = R("wq", st["l0"], st["l0"] + nl)
         elif h == 1:
             st["list"] = R("wl", 10 * t + 2, 10 * t + 10)
-            src = R("wq", 144 * t + 16, 144 * t + 144)
+            st["diag"] = R("wq", 144 * t + 16, 144 * t + 144)
         else:
-            tt(R("rk", 0, 7), R("ld%d" % t, G, 7 * BW, BW), R("c113", 0, 7), ADD)
-            tc(R("rki", 0, 7), R("rk", 0, 7))
-            tt(R("qa", 0, 112), R("sdw", 0, 791), R("mask", 0, 112), MUL, ind=R("rki", 0, 7))
-            tc(R("lA", 7, 8), R("wl", 10 * t + 1, 10 * t + 2))
-            scan(R("qc", 0, 112), R("rsa"), R("qa", 0, 112), 0.0, MUL, ADD)
-            tc(R("lA", 0, 7), R("qc", 15, 112, 16))
             act(R("qa", 112, 128), R("wq", 144 * t, 144 * t + 16), COPY)
+            tt(R("rk", 0, 7), R("ld%d" % t, G, 7 * BW, BW), R("c112", 0, 7), ADD)
+            tc(R("rki", 0, 7), R("rk", 0, 7))
+            tt(R("qa", 0, 112), R("sdw", 0, 785), R("mask", 0, 112), MUL, ind=R("rki", 0, 7))
+            scan(R("qc"), R("rsa"), R("qa"), 0.0, MUL, ADD)
+            tc(R("lA"), R("qc", 15, 128, 16))
             st["list"] = R("lA")
-            src = R("qa")
-        mm(R("acc" + X, 408, 416, rows=nl), src, R("cm"), True, True)
-        nbg(st)
-        tc(R("idp", 8 * h, 8 * h + 8, rows=nl), R("acc" + X, 408, 416, rows=nl))
+            st["diag"] = R("qa")
 
-    def nbg(st):
-        X, nl = st["X"], st["nl"]
+    def look(st, hop, ncs):
+        X, h, nl, l0, nc = st["X"], st["h"], st["nl"], st["l0"], st["nc"]
+        a1, a2, hh = "a1" + X, "a2" + X, (8 * h, 8 * h + 8)
+        win, bb, me = R("f", OWN, FW), R("b", l0, l0 + nl), R(a1, 256, 264, rows=nl)
         tc(R("off" + X, 0, nl), R("nbw"), ind=st["list"])
-
-    def compv(st):
-        X, nl = st["X"], st["nl"]
+        ts(bb, win, col("mid"), None, ADD, ind=st["list"])
         ts(R("cp" + X, 0, nl), R("off" + X, 0, nl), col("nb"), None, ADD)
-
-    def bgat(st):
-        X, h, nl, l0 = st["X"], st["h"], st["nl"], st["l0"]
-        bb = R("b", l0, l0 + nl)
-        ts(bb, R("f", OWN, FW), col("b2"), None, ADD, ind=st["list"])
         for j in range(RR):
             mm(R("bp" + X, j, RR * nl, RR), R("idb"), bb, True, True)
-        mm(R("acc" + X, 128, 392, rows=nl), bb, R("wb"), True, False)
-        mm(R("acc" + X, 384, 392, rows=nl), R("ones", 0, nl, rows=9), R("k9", rows=9), False, False)
-        mm(R("acc" + X, 0, 128, rows=nl), R("cp" + X, 0, nl), R("idf"), False, False)
-        if st["hop"] == H:
-            mm(R("q1", 8 * h, 8 * h + 8, rows=nl), bb, R("wz"), True, True)
-
-    def chunk(st, k):
-        n2 = 64 if st["nl"] == 128 else 32
-        return (0, n2) if k == 0 else (n2, st["nl"])
-
-    def agat(st, k):
-        X = st["X"]
-        lo, hi = chunk(st, k)
-        act(R("a" + X, 16 * lo, 16 * hi), R("f", OWN, FW), IDEN, bias=col("b2"), ind=R("off" + X, lo, hi))
-
-    def amm(st):
-        X, nl = st["X"], st["nl"]
-        for n in range(NV):
-            mm(R("acc" + X, n, 384, 16, rows=nl), R("a" + X, n, 16 * nl, 16), R("wa"), False, False)
-
-    def maxes(st, k, ns):
-        X, nl = st["X"], st["nl"]
-        lo, hi = chunk(st, k)
-        for n in ns:
-            tt(R("m" + X, RR * (n * nl + lo), RR * (n * nl + hi)), R("a" + X, 16 * lo + n, 16 * hi, NC), R("bp" + X, RR * lo, RR * hi), MAX)
-            if k == 1:
-                for j in range(RR):
-                    mm(R("acc" + X, n + NC * j, 384, 16, rows=nl), R("m" + X, RR * n * nl + j, RR * (n + 1) * nl, RR), R("wm"), False,
-                       n == NC - 1 and j == RR - 1)
-
-    def tail(st):
-        X, h, nl, hop = st["X"], st["h"], st["nl"], st["hop"]
-        acc = "acc" + X
-        hh = (8 * h, 8 * h + 8)
-        tc(R("t1" + X, rows=nl), R(acc, 128, 256, rows=nl))
-        tt(R("u" + X, rows=nl), R("t1" + X, rows=nl), R(acc, 256, 384, rows=nl), MIN)
-        tt(R("k" + X, rows=nl), R("u" + X, rows=nl), R(acc, 0, 128, rows=nl), MIN)
-        tt(R("sf" + X, rows=nl), R("idp" if hop == 1 else "id%d" % (1 - hop % 2), hh[0], hh[1], rows=nl), R(acc, 384, 392, rows=nl), ADD)
-        scan(R("sc" + X, rows=nl), R("rsm", rows=nl), R("k" + X, rows=nl), -1e29, ADD, MAX)
+        mm(R(a1, 0, 128, rows=nl), bb, R("wb", 0, 128), True, False)
+        mm(me, bb, R("wa", 8, 16), False, False)
         if hop == 1:
-            ts(R("alive", hh[0], hh[1], rows=nl), R(acc, 384, 392, rows=nl), 1.5 * K17 - OFS, None, GE)
-        tt(R("vi", hh[0], hh[1], rows=nl), R("sc" + X, 15, 128, 16, rows=nl), R("sf" + X, rows=nl), MAX)
+            mm(me, st["diag"], R("cm"), False, False)
+        mm(R(a2, 0, 128, rows=nl), bb, R("wb", 128, 256), True, False)
+        mm(R(a2, 0, 128, rows=nl), R("ones", 0, nl, rows=1), R("mpen", rows=1), False, False)
+        mm(R(a1, 128, 256, rows=nl), R("cp" + X, 0, nl), R("idf"), False, False)
+        if hop == H:
+            mm(R("q1", hh[0], hh[1], rows=nl), bb, R("wz"), True, True)
+        lo = 0
+        for w in CHUNKS[nl]:
+            hi = lo + w
+            act(R("a" + X, 16 * lo, 16 * hi), win, IDEN, bias=col("mid"), ind=R("off" + X, lo, hi))
+            if turn:
+                ops[-1]["deps"].setdefault(turn.pop(), False)
+            turn.append(len(ops) - 1)
+            for n in range(NC):
+                tt(R("m" + X, RR * (n * nl + lo), RR * (n * nl + hi)), R("a" + X, 16 * lo + n, 16 * hi, NC), R("bp" + X, RR * lo, RR * hi), MAX)
+            lo = hi
+        for n in range(NV):
+            mm(R(a1, n, 256, 16, rows=nl), R("a" + X, n, 16 * nl, 16), R("wa", 0, 16), False, n == NV - 1)
+        act(R("th" + X, rows=nl), R(a1, 0, 128, rows=nl), RELU, scale=2 * PEN)
+        if hop == 1:
+            ts(R("fb", hh[0], hh[1], rows=nl), me, -(MID + 0.5) * K17, 100.0, LT, MUL)
+        else:
+            tt(R("sf" + X, rows=nl), R("id%d" % (1 - hop % 2), hh[0], hh[1], rows=nl), me, ADD)
+        for n in range(NC):
+            for j in range(RR):
+                mm(R(a2, n + NC * j, 128, 16, rows=nl), R("m" + X, RR * n * nl + j, RR * (n + 1) * nl, RR), R("wa", 16, 24), False, n == NC - 1 and j == RR - 1)
+        tt(R("u" + X, rows=nl), R(a2, 0, 128, rows=nl), R("th" + X, rows=nl), SUB)
+        tt(R("k" + X, rows=nl), R("u" + X, rows=nl), R(a1, 128, 256, rows=nl), MIN)
+        scan(R("sc" + X, rows=nl), R("rsm", rows=nl), R("k" + X, rows=nl), 0.0, ADD, MAX)
+        if hop == H and st["t"] == RO - 1:
+            return
+        tt(R("vi", hh[0], hh[1], rows=nl), R("sc" + X, 15, 128, 16, rows=nl), me if hop == 1 else R("sf" + X, rows=nl), MAX)
         ts(R("id%d" % (hop % 2), hh[0], hh[1], rows=nl), R("vi", hh[0], hh[1], rows=nl), 8191, None, AND)
         if hop < H:
             tt(R("xx", 128 * h, 128 * h + 128), R("id%d" % (hop % 2), hh[0], hh[1]), R("mask", 0, 128), MUL, ind=R("rep", 0, 8))
-            mm(R(acc, 400, 400 + st["nc"]), R("xx", 128 * h, 128 * h + 128, rows=nl), R("cm", 0, st["nc"], rows=nl), True, True)
-
-    def nextlist(st):
-        X, hop, nc = st["X"], st["hop"], st["nc"]
-        tc(R("l" + X, 0, nc), R("acc" + X, 400, 400 + nc))
-        st["list"] = R("l" + X, 0, nc)
-        nbg(st)
+            mm(R(a2, 128, 128 + nc), R("xx", 128 * h, 128 * h + 128, rows=nl), R("cm", 0, nc, rows=nl), True, True)
+            tc(R("l" + X, 0, nc), R(a2, 128, 128 + nc))
+            st["list"] = R("l" + X, 0, nc)
         if hop == H - 1:
-            tc(R("sL", st["c0"], st["c0"] + nc), R("acc" + X, 400, 400 + nc))
-        st["hop"] = hop + 1
+            ts(R("a12", ncs + st["c0"], ncs + st["c0"] + nc), R("l" + X, 0, nc), float(OWN), None, ADD)
 
-    def places(t, sts):
+    def places(t, sts, F):
+        nc = sum(st["nc"] for st in sts)
+        L = 16 * nc
         tc(R("zi"), R("q1", 0, 16))
         ts(R("zm"), R("zi"), 4095, None, AND)
         tt(R("zq"), R("zm"), R("zm"), MUL)
         if t:
             ts(R("zi"), R("zq"), float(97 * 32 * t), None, ADD)
         ts(R("zh"), R("zi" if t else "zq"), 5, 4095, SHR, AND)
-        ts(R("zg"), R("zh"), float(S), float(-S), GE, MUL)
+        ts(R("zg"), R("zh"), float(S), float(S), LT, MUL)
         tt(R("dT"), R("zh"), R("zg"), ADD)
-        tt(R("dx"), R("dT"), R("mask", 0, 256), MUL, ind=R("rep", 0, 16))
+        tt(R("dx"), R("dT"), R("mask"), MUL, ind=R("rep", 0, 16))
         for st in sts:
             mm(R("q1", 16 + st["c0"], 16 + st["c0"] + st["nc"]), R("dx", 128 * st["h"], 128 * st["h"] + 128, rows=st["nl"]),
                R("cm", 0, st["nc"], rows=st["nl"]), True, True)
-
-    def places2(t, sts):
-        nc = sum(st["nc"] for st in sts)
-        L = 16 * nc
-        tc(R("dLi", 0, nc), R("q1", 16, 16 + nc))
-        tc(R("dl", 0, nc), R("dLi", 0, nc))
-        act(R("fd", 0, L), R("f", OWN, OWN + S), COPY, ind=R("dl", 0, nc))
-        ts(R("dLm", 0, nc), R("dLi", 0, nc), M - 1, None, AND)
-        tc(R("dlm", 0, nc), R("dLm", 0, nc))
-        act(R("uu", 0, L), R("pl"), COPY, ind=R("dlm", 0, nc))
-        ts(R("dLc", 0, nc), R("dLi", 0, nc), -2048.0, None, ADD)
-        tt(R("dmu"), R("dT"), R("uc2"), SUB)
-        ts(R("se"), R("id1"), float(S), None, LT)
-        tt(R("se"), R("se"), R("alive"), MUL)
-        tt(R("dmu"), R("dmu"), R("se"), MUL)
-        tt(R("a12", 0, nc), R("dLi", 0, nc), R("basm", 0, nc), SUB)
-        tt(R("a12", nc, 2 * nc), R("sL", 0, nc), R("basm", nc, 2 * nc), SUB)
-
-    def places3(t, sts):
-        nc = sum(st["nc"] for st in sts)
-        L = 16 * nc
+        ts(R("dl", 0, nc), R("q1", 16, 16 + nc), float(OWN - S), None, ADD)
+        ts(R("a12", 0, nc), R("q1", 16, 16 + nc), float(OWN - S), None, ADD)
+        act(R("fd", 0, L), R("f", 0, OWN + S), IDEN, bias=col("r15"), ind=R("dl", 0, nc))
+        act(R("uu", 0, L), R("pl"), COPY, ind=R("dl", 0, nc))
+        ts(R("fb", 16, 32), R("id1"), float(S), 8.0, GE, MUL)
         for st in sts:
-            mm(R("q1", 32 + 8 * st["h"], 40 + 8 * st["h"], rows=st["nl"]), R("fd", st["l0"], st["l0"] + st["nl"]), R("ws"), True, True)
-        mm(R("q2", 0, L), R("idb"), R("uu", 0, L), True, False)
-        mm(R("q2", 0, L), R("idb"), R("b", 0, L), False, True)
-        ts(R("em"), R("q1", 32, 48), 0.0, None, LT)
-        tt(R("dmu"), R("em"), R("dmu"), MUL)
-
-    def moves(t, sts):
-        nc = sum(st["nc"] for st in sts)
-        L = 16 * nc
-        act(R("uv", 0, L), R("q2", 0, L), IDEN, bias=col("nb%d" % t), scale=col("half"))
-        act(R("val", L, 2 * L), R("b", 0, L), IDEN, bias=col("neg"), scale=col("rl"))
-        tt(R("se"), R("id0"), R("id1"), EQ)
-        tt(R("dc"), R("se"), R("dmu"), MUL)
-        tt(R("dc"), R("dc"), R("ucode"), ADD)
-        tc(R("ex"), R("dc"), ind=R("rep", 0, 16))
+            h, nl, l0 = st["h"], st["nl"], st["l0"]
+            o = R("q1", 32 + 8 * h, 40 + 8 * h, rows=nl)
+            mm(o, R("b", l0, l0 + nl), R("wa", 8, 16), True, False)
+            for k in (0, 16):
+                mm(o, R("nid", 0, nl, rows=nl), R("fb", k + 8 * h, k + 8 * h + 8, rows=nl), False, False)
+            mm(o, R("fd", l0, l0 + nl), R("ws"), False, True)
+        ts(R("ex"), R("dT"), float(-S - 2048), None, ADD, ind=R("rep", 0, 16))
         for st in sts:
             mm(R("q2", st["l0"], st["l0"] + st["nl"]), R("ex", 128 * st["h"], 128 * st["h"] + 128, rows=st["nl"]), R("idh", 0, st["nl"], rows=st["nl"]), True, True)
-        ts(R("val", 0, L), R("uv", 0, L), MAGIC, -MAGIC, ADD, ADD)
         tc(R("da", 0, L), R("q2", 0, L))
-        for c in range(nc - 1, -1, -1):
-            ts(R("e3", extra=(c, slice(256 - 16 * c, 272))), R("da", 0, 16 * c + 16), R("dLc", c, c + 1), None, EQ)
-            if c:
-                act(R("trash", 0, 16 * c), R("e3", extra=(c, slice(256 - 16 * c, 256))), COPY, accum=R("cnt", c, c + 1))
-        sl = slice(0, nc)
-        tt(R("dg", extra=(sl, slice(0, 16))), R("e3", extra=(sl, slice(256, 272))), R("tri3", extra=(sl, slice(0, 16))), MUL)
-        for w in (8, 4, 2, 1):
-            src = "dg" if w == 8 else "dgs"
-            tt(R("dgs", extra=(sl, slice(0, w))), R(src, extra=(sl, slice(0, w))), R(src, extra=(sl, slice(w, 2 * w))), ADD)
+        bp = "bp" + F
+        mm(R(bp, 0, L), R("idb"), R("uu", 0, L), True, False)
+        mm(R(bp, 0, L), R("idb"), R("b", 0, L), False, False)
+        mm(R(bp, 0, L), R("ones", rows=1), R("mhalf", 0, L, rows=1), False, True)
+        act(R("uv", 0, L), R(bp, 0, L), IDEN, bias=MAGIC, scale=0.5)
+        act(R("val", 0, L), R("uv", 0, L), IDEN, bias=col("vb%d" % t), scale=col("rl"))
+        act(R("val", L, 2 * L), R("b", 0, L), IDEN, bias=col("neg"), scale=col("rl"))
 
-    def moves2(t, sts):
+    def rivals(st, sts, F):
+        X, h, nl, nc, c0 = st["X"], st["h"], st["nl"], st["nc"], st["c0"]
+        L = sum(x["nl"] for x in sts)
+        rows = max(x["nl"] for x in sts)
+        tt(R("cand", 8 * h, 8 * h + 8, rows=nl), R("sc" + X, 15, 128, 16, rows=nl), R("q1", 32 + 8 * h, 40 + 8 * h, rows=nl), LE)
+        tt(R("x1", 128 * h, 128 * h + 128), R("cand", 8 * h, 8 * h + 8), R("dx", 128 * h, 128 * h + 128), MUL, ind=R("rep", 0, 8))
+        mm(R("a2" + F, 136 + c0, 136 + c0 + nc), R("x1", 128 * h, 128 * h + 128, rows=nl), R("cm", 0, nc, rows=nl), True, True)
+        for c in range(c0, c0 + nc):
+            ts(R("e3", 256 * c + 16 * c, 256 * c + L), R("da", 16 * c, L), float(S + 2048), R("a2" + F, 136 + c, 137 + c), ADD, EQ)
+            for o in sts[h:]:
+                w = R("ww", 8 * (c - c0), 8 * (c - c0) + 8) if o is st else R("ww", 64, 72)
+                mm(R("q2", 8 * o["h"], 8 * o["h"] + 8, rows=rows), R("e3", 256 * c + o["l0"], 256 * c + o["l0"] + rows), w,
+                   X == F and c == c0 and o is st, X != F and c == c0 + nc - 1 and o is sts[-1])
+
+    def moves(sts):
         nc = sum(st["nc"] for st in sts)
-        L = 16 * nc
-        tt(R("fl", 0, nc), R("cnt", 0, nc), R("dgs", extra=(slice(0, nc), 0)), ADD)
-        for k in (0, nc):
-            ts(R("w2", k, k + nc), R("fl", 0, nc), -0.25, None, LT)
-        tt(R("of", 0, 2 * nc), R("w2", 0, 2 * nc), R("a12", 0, 2 * nc), MUL)
-        tt(R("of", 0, 2 * nc), R("of", 0, 2 * nc), R("base", 0, 2 * nc), ADD)
+        mm(R("q1", 64, 64 + 2 * nc), R("idf"), R("base", 0, 2 * nc), True, False)
+        ts(R("first"), R("q2", 0, 16), col("thr"), None, LT)
+        tt(R("x2"), R("first"), R("x1"), MUL, ind=R("rep", 0, 16))
+        for st in sts:
+            for k in (0, nc):
+                o = 64 + k + st["c0"]
+                mm(R("q1", o, o + st["nc"]), R("x2", 128 * st["h"], 128 * st["h"] + 128, rows=st["nl"]), R("cm2", 0, st["nc"], rows=st["nl"]), False,
+                   st["h"] == 1 and k == nc)
+        tt(R("of", 0, 2 * nc), R("a12", 0, 2 * nc), R("q1", 64, 64 + 2 * nc), MIN)
         tc(R("ofl", 0, 2 * nc), R("of", 0, 2 * nc))
-        tc(R("f", 0, OWN + S), R("val", 0, 2 * L), oind=R("ofl", 0, 2 * nc))
+        tc(R("f", 0, OWN + S), R("val", 0, 32 * nc), oind=R("ofl", 0, 2 * nc))
 
-    def requests(sts, part):
-        if part == 0:
-            ts(R("ebi"), R("id0"), 1.0 / G, 1.0 - (S + (G - 1) / 2) / G, MUL, ADD)
-            tt(R("eb"), R("ebi"), R("alive"), MUL)
-            ts(R("kq"), R("ebi"), float(-G), float(-(S - G - 1)), MUL, ADD)
-            tt(R("kq"), R("kq"), R("id0"), ADD)
-            tt(R("on"), R("eb"), R("ec"), EQ, ind=R("rep8"))
-            for st in sts:
-                nl, h = st["nl"], st["h"]
-                if h == 0:
-                    mm(R("q3", 0, 64, rows=nl), R("tril", 0, nl, rows=nl), R("on", 0, 64, rows=nl), True, True)
-                else:
-                    n0 = sts[0]["nl"]
-                    mm(R("q3", 64, 128, rows=nl), R("tril", 0, nl, rows=nl), R("on", 64, 128, rows=nl), True, False)
-                    mm(R("q3", 64, 128, rows=nl), R("ones", 0, nl, rows=n0), R("on", 0, 64, rows=n0), False, True)
-        elif part == 1:
-            tt(R("qb"), R("on"), R("q3", 0, 128), MUL)
-            scan(R("qs"), R("rs8"), R("qb"), 0.0, MUL, ADD)
-            tt(R("mh"), R("qs"), R("jmf"), EQ, ind=R("rep87"))
-            tt(R("ek"), R("kq"), R("on"), MUL, ind=R("rep8"))
-            for st in sts:
-                nl, h = st["nl"], st["h"]
-                mm(R("q3", 128, 192), R("mh", 128 * h, 128 * h + 128, rows=nl), R("ek", 64 * h, 64 * h + 64, rows=nl), h == 0, h == 1)
-        else:
-            tt(R("rq"), R("gm"), R("q3", 128, 192), MUL)
-            tt(R("rq", 0, 32), R("rq", 0, 32), R("rq", 32, 64), ADD)
-            tt(R("rq", 0, 16), R("rq", 0, 16), R("rq", 16, 32), ADD)
-            tt(R("gg", G, 7 * BW, BW), R("rq", 0, 7), R("rq", 8, 15), ADD)
+    def requests(sts, F):
+        ts(R("ebi"), R("id0"), 1.0 / G, 1.0 - (S + (G - 1) / 2) / G, MUL, ADD)
+        tt(R("eb"), R("ebi"), R("fb", 0, 16), ADD)
+        ts(R("idm"), R("id0"), float(1 - S), None, ADD)
+        tt(R("on"), R("eb"), R("ec"), EQ, ind=R("rep8"))
+        A, B = sts
+        bp = "bp" + F
+        mm(R(bp, 256, 320, rows=A["nl"]), R("tril", 0, A["nl"], rows=A["nl"]), R("on", 0, 64, rows=A["nl"]), True, True)
+        mm(R(bp, 320, 384, rows=B["nl"]), R("tril", 0, B["nl"], rows=B["nl"]), R("on", 64, 128, rows=B["nl"]), True, False)
+        mm(R(bp, 320, 384, rows=B["nl"]), R("ones", 0, B["nl"], rows=A["nl"]), R("on", 0, 64, rows=A["nl"]), False, True)
+        scan(R("qs"), R("rs8"), R(bp, 256, 384), 0.0, MUL, MAX)
+        tt(R("ek"), R("idm"), R("on"), MUL, ind=R("rep8"))
+        tt(R("mh"), R("qs"), R("jm1"), EQ, ind=R("rep87"))
+        for st in sts:
+            nl, h = st["nl"], st["h"]
+            mm(R("a1" + F, 0, 64), R("mh", 128 * h, 128 * h + 128, rows=nl), R("ek", 64 * h, 64 * h + 64, rows=nl), h == 0, h == 1)
+        act(R("rq"), R("a1" + F, 0, 64), COPY)
+        tt(R("gg", G, 16 * BW, BW), R("rq"), R("ce"), SUB, ind=R("gl", 0, 1))
 
-    def landed(t):
-        for e in range(1, 8):
-            o, i = R("f", OWN + S + (e - 1) * G, OWN + S + e * G), R("ld%d" % t, (7 - e) * BW, (7 - e) * BW + G)
-            if e in (2, 4, 6):
-                act(o, i, COPY)
-            else:
-                tc(o, i)
-
+    exchange(0)
     for t in range(RO):
-        A, B = stream("A", t), stream("B", t)
-        sts = (A, B)
-        order = (A, B) if t == 0 else (B, A)
-        if t == 1:
-            setup_later()
-        start(order[0])
-        compv(order[0])
-        if t == 0:
-            setup_hops()
-        landed(t)
-        for slot in range(2 * H):
-            X, Y = order[slot % 2], order[1 - slot % 2]
-            last = slot == 2 * H - 1
-            if slot:
-                compv(X)
-            bgat(X)
-            agat(X, 0)
-            if slot == 0:
-                start(Y)
-                maxes(X, 0, range(NC))
-            else:
-                tail(Y)
-                maxes(X, 0, range(0, K1))
-                if last:
-                    places(t, sts)
-                else:
-                    nextlist(Y)
-                maxes(X, 0, range(K1, NC))
-            agat(X, 1)
-            amm(X)
-            if last:
-                places2(t, sts)
-            maxes(X, 1, range(NC))
-        places3(t, sts)
-        tail(order[1])
-        moves(t, sts)
+        sts = (stream("A", t), stream("B", t))
+        order = sts if t == 0 else sts[::-1]
+        F = order[0]["X"]
+        ncs = sum(st["nc"] for st in sts)
+        for st in order:
+            start(st)
+        for hop in range(1, H + 1):
+            for st in order:
+                look(st, hop, ncs)
+        places(t, sts, F)
+        for st in order:
+            rivals(st, sts, F)
         if t + 1 < RO:
-            requests(sts, 0)
-        moves2(t, sts)
+            requests(sts, F)
+        moves(sts)
         if t + 1 < RO:
-            requests(sts, 1)
-            ghosts(t + 1)
-            requests(sts, 2)
-            send(t + 1)
-    emit("y", lambda: g.sync.dma_start(T.y[:], T.f[:, OWN:OWN + S]).then_inc(T.sem["d11"], 16), [R("f", OWN, OWN + S)], [], sem="d11", inc=16, dma=True)
-    g.sync.wait_ge(T.sem["d11"], 16)
-    for q in ("v", "s", "p", "g"):
-        g.wait_ge(T.sem[semof[q]], cnt[q])
-    for name, val in sorted(sent.items()):
-        g.wait_ge(T.sem[name], val)
-    for i in range(dman[0]):
-        g.wait_ge(T.sem["d%d" % i], 16)
+            exchange(t + 1)
+    dma("y", T.y[:], T.f[:, OWN:OWN + S], [], [R("f", OWN, OWN + S)], 5.0)
+    emit_all()

@@ -4,6 +4,7 @@ from concourse.mybir import dt, AluOpType, AxisListType, ActivationFunctionType
 ADD, SUB, MUL, MAX, MIN = AluOpType.add, AluOpType.subtract, AluOpType.mult, AluOpType.max, AluOpType.min
 GE, GT, LE, LT, EQ = AluOpType.is_ge, AluOpType.is_gt, AluOpType.is_le, AluOpType.is_lt, AluOpType.is_equal
 SHR, AND = AluOpType.arith_shift_right, AluOpType.bitwise_and
+ABS = ActivationFunctionType.Abs
 IDEN, COPY, RELU, EXP = ActivationFunctionType.Identity, ActivationFunctionType.Copy, ActivationFunctionType.Relu, ActivationFunctionType.Exp
 
 N, S, G, CAP, WN, M, RO, H, T0 = 8, 3328, 112, 16, 144, 512, 3, 4, 192
@@ -19,20 +20,21 @@ NC = NV // RR
 MAGIC = 12582912.0
 PEN = float(2 ** 26)
 DECAY = 1.04
-CHUNKS = {128: (48, 48, 32), 80: (48, 32), 64: (32, 32)}
+CHUNKS = {128: (32, 48, 48), 80: (48, 32), 64: (32, 32)}
+OPENING = {128: (48, 48, 32), 64: (32, 32)}
 
 SCRATCH = {}
 for _n, _w, _t in (
         ("f", FW, "bfloat16"), ("nbw", NULL + 16, "int32"), ("pl", OWN + S, "bfloat16"), ("wti", 1, "int32"), ("wni", 27, "int32"), ("sdi", 49, "int32"),
         ("sdp", 56, "uint16"), ("sdf", 56, "float32"), ("sdw", 800, "float32"), ("sdx", 784, "float32"), ("wl", 30, "uint16"), ("rep", 50, "uint16"),
         ("wq", 432, "float32"), ("jf", 128, "float32"), ("jmf", 256, "float32"), ("jm1", 256, "float32"), ("j4", 128, "float32"), ("j7", 128, "float32"),
-        ("j16", 64, "float32"), ("ji", 64, "int32"), ("cols", 40, "float32"), ("idf", 128, "float32"), ("idh", 128, "float16"), ("idb", 128, "bfloat16"),
-        ("nid", 128, "bfloat16"), ("mask", 256, "float32"), ("rep8", 8, "uint16"), ("rep87", 16, "uint16"), ("gl", 2, "uint16"), ("blk", 128, "float32"),
+        ("j16", 64, "float32"), ("ji", 64, "int32"), ("cols", 40, "float32"), ("idf", 128, "float32"), ("mask1", 144, "float32"), ("rep1", 10, "uint16"), ("idb", 128, "bfloat16"),
+        ("nid", 128, "bfloat16"), ("nidf", 128, "float32"), ("da4", 256, "float32"), ("far", 512, "float32"), ("nco", 8, "float32"), ("mask", 256, "float32"), ("rep8", 8, "uint16"), ("rep87", 16, "uint16"), ("gl", 2, "uint16"), ("blk", 128, "float32"),
         ("wa", 24, "bfloat16"), ("wb", 256, "bfloat16"), ("mpen", 128, "bfloat16"), ("wz", 8, "bfloat16"), ("ws", 8, "bfloat16"), ("ww", 80, "bfloat16"), ("wwf", 64, "float32"),
         ("cm2", 8, "bfloat16"), ("rsm", 128, "float32"), ("rsa", 128, "float32"), ("rs8", 128, "float32"), ("tril", 128, "bfloat16"), ("ones", 128, "bfloat16"),
-        ("mhalf", 256, "bfloat16"), ("ec", 128, "float32"), ("onf", 128, "float32"), ("b", 256, "bfloat16"), ("xx", 256, "float32"), ("dx", 256, "float32"),
+        ("mhalf", 256, "bfloat16"), ("ec", 128, "float32"), ("onf", 128, "float32"), ("b", 256, "bfloat16"), ("xx", 288, "float32"), ("dx", 256, "float32"),
         ("x1", 256, "float32"), ("x2", 256, "bfloat16"), ("dl", 16, "uint16"), ("fb", 32, "bfloat16"), ("fd", 256, "bfloat16"), ("uu", 256, "bfloat16"),
-        ("uv", 256, "float32"), ("val", 512, "bfloat16"), ("ex", 256, "float16"), ("da", 256, "float16"), ("ofl", 32, "uint16"), ("on", 128, "bfloat16"),
+        ("uv", 256, "float32"), ("val", 512, "bfloat16"), ("ramp", OWN + S, "float32"), ("da", 256, "float16"), ("ofl", 32, "uint16"), ("on", 128, "bfloat16"),
         ("qs", 128, "float32"), ("mh", 256, "float16"), ("ek", 128, "float16"), ("rq", 64, "float32"), ("gg", 16 * BW, "bfloat16"), ("ld0", 7 * BW, "bfloat16"),
         ("ld1", 7 * BW, "bfloat16"), ("ld2", 7 * BW, "bfloat16"), ("rki", 8, "uint16"), ("rkj", 8, "uint16"), ("qa", 128, "float32"), ("qc", 128, "float32")):
     SCRATCH[_n] = ("sbuf", [128, _w], _t)
@@ -55,10 +57,13 @@ for _buf, _t, _names in (
         ALIAS[_n] = (_buf, _o, _w)
         _o += _w
     SCRATCH[_buf] = ("sbuf", [128, _o], _t)
-SEMAPHORES = ["sv", "ss", "sp", "sg"] + ["d%d" % i for i in range(12)] + ["arr%d" % i for i in range(6)] + ["snd%d" % i for i in range(6)]
+SEMAPHORES = ["sv", "ss", "sp", "sg", "go"] + ["d%d" % i for i in range(12)] + ["arr%d" % i for i in range(6)] + ["snd%d" % i for i in range(6)]
 
-CYC, GATHER, SCATTER, PECYC, WAKE = 0.00090, 1.45, 3.0, 0.00055, 0.12
-FILL = 0.12
+CYC, GATHER, SCATTER, PECYC, WAKE = 0.00090, 1.55, 3.0, 0.00045, 0.13
+TAIL, EARLY = 1.0, 3.0
+SCOLS = 6
+NEAR = 2
+FILL = 0.14
 
 
 def R(name, lo=None, hi=None, step=None, rows=128):
@@ -78,6 +83,26 @@ def narrow(*rs):
     return all(SCRATCH[r[0]][2] in ("bfloat16", "float16", "uint16") for r in rs)
 
 
+def meet(r, lo, hi, step):
+    if r[2] <= lo or hi <= r[1]:
+        return False
+    if (r[3] is None) == (step is None):
+        return True
+    (a, b, s), (c, d) = ((lo, hi, step), r[1:3]) if step else (r[1:4], (lo, hi))
+    return a + max(0, -((a - c) // s)) * s < min(b, d)
+
+
+def topological(ops, users):
+    left = [len(o["deps"]) for o in ops]
+    out = [i for i, x in enumerate(left) if not x]
+    for i in out:
+        for u in users[i]:
+            left[u] -= 1
+            if not left[u]:
+                out.append(u)
+    return out
+
+
 def in_order(ops):
     n = len(ops)
     users = [[] for _ in range(n)]
@@ -85,9 +110,10 @@ def in_order(ops):
         for d in o["deps"]:
             users[d].append(i)
     prio = [0.0] * n
-    for i in range(n - 1, -1, -1):
+    for i in topological(ops, users)[::-1]:
         o = ops[i]
         prio[i] = o["occ"] + max([o["lat"]] + [prio[u] + (o["lat"] if ops[u]["deps"][i] else 0.0) for u in users[i]])
+    prio = [p + o["early"] for p, o in zip(prio, ops)]
     left = [len(o["deps"]) for o in ops]
     ready_at = [0.0] * n
     cand = {}
@@ -106,11 +132,12 @@ def in_order(ops):
         for i in here:
             go = max(now + prio[i], max(now + ops[i]["occ"], ready_at[top]) + prio[top])
             hold = max(ready_at[top] + prio[top], ready_at[top] + ops[top]["occ"] + prio[i])
-            if i == top or go <= hold + FILL:
+            if i == top or go <= hold + (0.0 if ops[i]["lazy"] else FILL):
                 pick = i
                 break
         if pick is None:
-            pick, now = top, ready_at[top]
+            free[q] = min(ready_at[top], now + 0.03)
+            continue
         cand[q].remove(pick)
         out.append((now, len(out), pick))
         free[q] = now + ops[pick]["occ"]
@@ -143,10 +170,10 @@ def rank_program(g, core, T, topo):
         acc = [(r, False) for r in reads] + [(r, True) for r in writes]
         for r, w in acc:
             name, bank = r[0], r[0] in PSUMS
-            for lo, hi, ow, oq, o in hist.get(name, ()):
+            for lo, hi, ow, oq, o, st in hist.get(name, ()):
                 if bank and oq == q == "p":
                     deps.setdefault(o, False)
-                elif (bank and oq != q) or ((w or ow) and lo < r[2] and r[1] < hi):
+                elif (bank and oq != q) or ((w or ow) and meet(r, lo, hi, st)):
                     deps[o] = True
         for r, w in acc:
             name, bank = r[0], r[0] in PSUMS
@@ -157,8 +184,8 @@ def rank_program(g, core, T, topo):
                 lst = [x for x in lst if x[3] == lst[-1][3]]
             elif w and not bank and r[3] is None and r[4] == 128:
                 lst = [x for x in lst if not (x[0] >= r[1] and x[1] <= r[2])]
-            hist[name] = lst + [(r[1], r[2], w, q if sem is None else None, me)]
-        ops.append({"q": q, "fn": fn, "deps": deps, "occ": occ, "lat": lat, "sem": sem, "inc": inc})
+            hist[name] = lst + [(r[1], r[2], w, q if sem is None else None, me, r[3])]
+        ops.append({"q": q, "fn": fn, "deps": deps, "occ": occ, "lat": lat, "sem": sem, "inc": inc, "early": 0.0, "lazy": False})
         return me
 
     def emit_all():
@@ -243,7 +270,9 @@ def rank_program(g, core, T, topo):
 
     def iota(out, pattern, base, cmul, flt=True):
         kw = {"allow_small_or_imprecise_dtypes": True} if flt else {}
-        record("g", lambda: g.iota(ap(out), pattern, base, cmul, **kw), [], [out], 0.13 + 2 * width(out) * CYC)
+        i = record("g", lambda: g.iota(ap(out), pattern, base, cmul, **kw), [], [out], 0.13 + 2 * width(out) * CYC)
+        if ops[i - 1]["q"] == "g":
+            ops[i]["deps"][i - 1] = False
 
     COL = {}
 
@@ -273,10 +302,12 @@ def rank_program(g, core, T, topo):
     iota(R("j7"), [[0, 16], [1, 8]], 0, 0)
     iota(R("j16"), [[16, 8], [0, 8]], 0, 0)
     iota(R("c112"), [[G, 8]], 0, 0)
+    for lo in range(0, OWN + S, 256):
+        iota(R("ramp", lo, lo + 256), [[1, 256]], lo - OWN - 2048, 0)
     ms(R("gg", 0, 7 * BW), 0.0)
     for nm in ("id0", "id1"):
         ms(R(nm), 0)
-    for r in (R("cand"), R("fb"), R("q1", 0, 96), R("bpA", 256, 384), R("f", 0, OWN)):
+    for r in (R("cand"), R("fb"), R("q1", 0, 96), R("q2", 0, 16), R("bpA", 256, 384), R("f", 0, OWN)):
         ms(r, 0.0)
     for c in range(1, 16):
         ms(R("e3", 256 * c + (0 if c < 8 else 64 if c == 8 else 128), 256 * c + 16 * c), 0.0)
@@ -305,11 +336,11 @@ def rank_program(g, core, T, topo):
     ts(R("rsm"), R("jmf", 0, 128), 0.0, -2 * PEN, EQ, MUL)
     ts(R("rsa"), R("jmf", 0, 128), 0.0, None, GT)
     ts(R("jm1"), R("jmf"), 1024.0, None, ADD)
-    tc(R("idh"), R("idf"))
     tc(col("wt"), R("wti"))
     tt(col("wtl"), col("wt"), col("rl"), MUL)
     act(R("idb"), R("idf"), COPY)
     act(R("nid"), R("idf"), COPY, scale=-PEN)
+    act(R("nidf"), R("idf"), COPY, scale=-1.0)
     act(R("wa", 0, 8), R("cm"), COPY, scale=col("rl"))
     act(R("wa", 8, 16), R("cm"), COPY, scale=col("k17"))
     act(R("wa", 16, 24), R("cm"), COPY, scale=col("big"))
@@ -342,6 +373,10 @@ def rank_program(g, core, T, topo):
     ts(R("gl", 0, 1), col("q"), 7.0, col("g8"), MIN, ADD)
     ts(R("base"), R("jf", 0, 32), 16.0, col("q"), MUL, ADD)
     tc(R("rep"), R("ji", 0, 50))
+    tc(R("rep1", 0, 8), R("ji", 0, 8))
+    ts(R("rep1", 8, 9), col("q"), 7.0, None, MIN)
+    act(R("mask1", 0, 128), R("mask", 0, 128), COPY)
+    ms(R("mask1", 128, 144), 1.0)
     ts(R("rep8"), R("jf", 0, 8), 2.0, col("q8"), MUL, ADD)
     ts(R("rep87"), R("jf", 0, 16), 8.0, 7.0, MUL, ADD)
     tc(R("wl", 0, 9), R("wni", 0, 9))
@@ -374,7 +409,7 @@ def rank_program(g, core, T, topo):
         for x in away + [y for y in es if y not in away]:
             eng = topo.engines(me, T.cores[(r + x) % N])
             free = [y for y in eng if y not in used]
-            room = len(eng) // len(away) if x in away else len(free)
+            room = len(eng) // len(away) if x in away else NEAR
             n = 1
             while n * 2 <= room:
                 n *= 2
@@ -384,7 +419,7 @@ def rank_program(g, core, T, topo):
 
     def exchange(t):
         calls = calls_of(rank)
-        for k, e in enumerate(calls[0] + calls[1]):
+        for k, e in enumerate(sum(calls, [])):
             o, w, i = R("gg", (e - 1) * BW, (e - 1) * BW + G), R("f", OWN, OWN + S), R("sdp", 8 * (e - 1), 8 * e - 1)
             if k % 2:
                 tc(o, w, ind=i)
@@ -402,8 +437,9 @@ def rank_program(g, core, T, topo):
             sem = "snd%d" % (2 * t + k)
             sent.append(record("g", lambda trs=trs, sem=sem: g.remote_dma_fused(trs, local_sem=T.sem[sem]), [R("gg", (e - 1) * BW, e * BW) for e in es], [],
                                2.5 if t + k == 0 else 0.6, 5.0, sem, sum(len(x) for x in eng.values()), ()))
-        ops[sent[1]]["deps"].setdefault(sent[0], False)
-        for k in (0, 1):
+        for k in range(1, len(calls)):
+            ops[sent[k]]["deps"].setdefault(sent[k - 1], False)
+        for k in range(len(calls)):
             es = [e for e in range(1, N) if e in calls_of((rank - e) % N)[k]]
             n = sum(len(engines_of((rank - e) % N, calls_of((rank - e) % N)[k])[e]) for e in es)
             record("r", None, [], [R("ld%d" % t, (7 - e) * BW, (8 - e) * BW) for e in es], 0.0, 0.0, "arr%d" % (2 * t + k), n, [sent[k]])
@@ -418,7 +454,7 @@ def rank_program(g, core, T, topo):
         h = 0 if X == "A" else 1
         nc = (4, 5)[h] if t == 0 else 8
         c0 = 0 if h == 0 else (4 if t == 0 else 8)
-        return {"X": X, "h": h, "nl": 16 * nc, "nc": nc, "c0": c0, "l0": 16 * c0, "t": t}
+        return {"X": X, "h": h, "nl": 16 * nc, "nc": nc, "c0": c0, "l0": 16 * c0, "t": t, "own": t == 0 or h == 1, "opens": (t == 0) == (h == 0)}
 
     def start(st):
         t, h, nl = st["t"], st["h"], st["nl"]
@@ -443,53 +479,73 @@ def rank_program(g, core, T, topo):
         a1, a2, hh = "a1" + X, "a2" + X, (8 * h, 8 * h + 8)
         win, bb, me = R("f", OWN, FW), R("b", l0, l0 + nl), R(a1, 256, 264, rows=nl)
         tc(R("off" + X, 0, nl), R("nbw"), ind=st["list"])
-        ts(bb, win, col("mid"), None, ADD, ind=st["list"])
+        ops[-1]["early"] = TAIL
+        ts(bb, R("f", OWN, OWN + S) if hop == 1 and st["own"] else win, col("mid"), None, ADD, ind=st["list"])
+        ops[-1]["early"] = EARLY
         ts(R("cp" + X, 0, nl), R("off" + X, 0, nl), col("nb"), None, ADD)
+        if hop == 1 and st["own"]:
+            for o in ops[-3:]:
+                o["early"], o["lazy"] = 0.0, True
         for j in range(RR):
             mm(R("bp" + X, j, RR * nl, RR), R("idb"), bb, True, True)
         mm(R(a1, 0, 128, rows=nl), bb, R("wb", 0, 128), True, False)
         mm(me, bb, R("wa", 8, 16), False, False)
         if hop == 1:
             mm(me, st["diag"], R("cm"), False, False)
+        else:
+            mm(me, R("idf", 0, nl, rows=nl), R("xx", 144 * h + 128, 144 * h + 136, rows=nl), False, False)
         mm(R(a2, 0, 128, rows=nl), bb, R("wb", 128, 256), True, False)
         mm(R(a2, 0, 128, rows=nl), R("ones", 0, nl, rows=1), R("mpen", rows=1), False, False)
         mm(R(a1, 128, 256, rows=nl), R("cp" + X, 0, nl), R("idf"), False, False)
         if hop == H:
             mm(R("q1", hh[0], hh[1], rows=nl), bb, R("wz"), True, True)
         lo = 0
-        for w in CHUNKS[nl]:
+        opening = hop == 1 and st["opens"]
+        for w in (OPENING if opening else CHUNKS)[nl]:
             hi = lo + w
-            act(R("a" + X, 16 * lo, 16 * hi), win, IDEN, bias=col("mid"), ind=R("off" + X, lo, hi))
-            if turn:
-                ops[-1]["deps"].setdefault(turn.pop(), False)
-            turn.append(len(ops) - 1)
+            if opening and lo == 0:
+                ts(R("a" + X, 16 * lo, 16 * hi), win, col("mid"), None, ADD, ind=R("off" + X, lo, hi))
+            else:
+                act(R("a" + X, 16 * lo, 16 * hi), win, IDEN, bias=col("mid"), ind=R("off" + X, lo, hi))
+                if turn:
+                    ops[-1]["deps"].setdefault(turn.pop(), False)
+                turn.append(len(ops) - 1)
             for n in range(NC):
                 tt(R("m" + X, RR * (n * nl + lo), RR * (n * nl + hi)), R("a" + X, 16 * lo + n, 16 * hi, NC), R("bp" + X, RR * lo, RR * hi), MAX)
             lo = hi
         for n in range(NV):
             mm(R(a1, n, 256, 16, rows=nl), R("a" + X, n, 16 * nl, 16), R("wa", 0, 16), False, n == NV - 1)
+        spare = st["t"] == 0 or (hop == H and not st["opens"])
         act(R("th" + X, rows=nl), R(a1, 0, 128, rows=nl), RELU, scale=2 * PEN)
+        if spare:
+            act(R("u" + X, rows=nl), R(a1, 128, 256, rows=nl), COPY)
         if hop == 1:
             ts(R("fb", hh[0], hh[1], rows=nl), me, -(MID + 0.5) * K17, 100.0, LT, MUL)
-        else:
-            tt(R("sf" + X, rows=nl), R("id%d" % (1 - hop % 2), hh[0], hh[1], rows=nl), me, ADD)
         for n in range(NC):
             for j in range(RR):
                 mm(R(a2, n + NC * j, 128, 16, rows=nl), R("m" + X, RR * n * nl + j, RR * (n + 1) * nl, RR), R("wa", 16, 24), False, n == NC - 1 and j == RR - 1)
-        tt(R("u" + X, rows=nl), R(a2, 0, 128, rows=nl), R("th" + X, rows=nl), SUB)
-        tt(R("k" + X, rows=nl), R("u" + X, rows=nl), R(a1, 128, 256, rows=nl), MIN)
+            if spare and n == NC - 2:
+                mm(R(a2, 0, 128, rows=nl), R("nidf", 0, nl, rows=nl), R("th" + X, rows=nl), False, False)
+        chain = len(ops)
+        if spare:
+            tt(R("k" + X, rows=nl), R("u" + X, rows=nl), R(a2, 0, 128, rows=nl), MIN)
+        else:
+            tt(R("u" + X, rows=nl), R(a2, 0, 128, rows=nl), R("th" + X, rows=nl), SUB)
+            tt(R("k" + X, rows=nl), R("u" + X, rows=nl), R(a1, 128, 256, rows=nl), MIN)
         scan(R("sc" + X, rows=nl), R("rsm", rows=nl), R("k" + X, rows=nl), 0.0, ADD, MAX)
         if hop == H and st["t"] == RO - 1:
             return
-        tt(R("vi", hh[0], hh[1], rows=nl), R("sc" + X, 15, 128, 16, rows=nl), me if hop == 1 else R("sf" + X, rows=nl), MAX)
+        tt(R("vi", hh[0], hh[1], rows=nl), R("sc" + X, 15, 128, 16, rows=nl), me, MAX)
         ts(R("id%d" % (hop % 2), hh[0], hh[1], rows=nl), R("vi", hh[0], hh[1], rows=nl), 8191, None, AND)
         if hop < H:
-            tt(R("xx", 128 * h, 128 * h + 128), R("id%d" % (hop % 2), hh[0], hh[1]), R("mask", 0, 128), MUL, ind=R("rep", 0, 8))
-            mm(R(a2, 128, 128 + nc), R("xx", 128 * h, 128 * h + 128, rows=nl), R("cm", 0, nc, rows=nl), True, True)
+            tt(R("xx", 144 * h, 144 * h + 144), R("id%d" % (hop % 2), hh[0], hh[1]), R("mask1"), MUL, ind=R("rep1", 0, 9))
+            mm(R(a2, 128, 128 + nc), R("xx", 144 * h, 144 * h + 128, rows=nl), R("cm", 0, nc, rows=nl), True, True)
             tc(R("l" + X, 0, nc), R(a2, 128, 128 + nc))
             st["list"] = R("l" + X, 0, nc)
+        for o in ops[chain:]:
+            o["early"] = TAIL
         if hop == H - 1:
-            ts(R("a12", ncs + st["c0"], ncs + st["c0"] + nc), R("l" + X, 0, nc), float(OWN), None, ADD)
+            act(R("a12", ncs + st["c0"], ncs + st["c0"] + nc), R(a2, 128, 128 + nc), IDEN, bias=float(OWN))
 
     def places(t, sts, F):
         nc = sum(st["nc"] for st in sts)
@@ -507,7 +563,7 @@ def rank_program(g, core, T, topo):
             mm(R("q1", 16 + st["c0"], 16 + st["c0"] + st["nc"]), R("dx", 128 * st["h"], 128 * st["h"] + 128, rows=st["nl"]),
                R("cm", 0, st["nc"], rows=st["nl"]), True, True)
         ts(R("dl", 0, nc), R("q1", 16, 16 + nc), float(OWN - S), None, ADD)
-        ts(R("a12", 0, nc), R("q1", 16, 16 + nc), float(OWN - S), None, ADD)
+        act(R("a12", 0, nc), R("q1", 16, 16 + nc), IDEN, bias=float(OWN - S))
         act(R("fd", 0, L), R("f", 0, OWN + S), IDEN, bias=col("r15"), ind=R("dl", 0, nc))
         act(R("uu", 0, L), R("pl"), COPY, ind=R("dl", 0, nc))
         ts(R("fb", 16, 32), R("id1"), float(S), 8.0, GE, MUL)
@@ -518,10 +574,8 @@ def rank_program(g, core, T, topo):
             for k in (0, 16):
                 mm(o, R("nid", 0, nl, rows=nl), R("fb", k + 8 * h, k + 8 * h + 8, rows=nl), False, False)
             mm(o, R("fd", l0, l0 + nl), R("ws"), False, True)
-        ts(R("ex"), R("dT"), float(-S - 2048), None, ADD, ind=R("rep", 0, 16))
-        for st in sts:
-            mm(R("q2", st["l0"], st["l0"] + st["nl"]), R("ex", 128 * st["h"], 128 * st["h"] + 128, rows=st["nl"]), R("idh", 0, st["nl"], rows=st["nl"]), True, True)
-        tc(R("da", 0, L), R("q2", 0, L))
+        act(R("da4", 0, L), R("ramp"), COPY, ind=R("dl", 0, nc))
+        tc(R("da", 0, L), R("da4", 0, L))
         bp = "bp" + F
         mm(R(bp, 0, L), R("idb"), R("uu", 0, L), True, False)
         mm(R(bp, 0, L), R("idb"), R("b", 0, L), False, False)
@@ -537,8 +591,16 @@ def rank_program(g, core, T, topo):
         tt(R("cand", 8 * h, 8 * h + 8, rows=nl), R("sc" + X, 15, 128, 16, rows=nl), R("q1", 32 + 8 * h, 40 + 8 * h, rows=nl), LE)
         tt(R("x1", 128 * h, 128 * h + 128), R("cand", 8 * h, 8 * h + 8), R("dx", 128 * h, 128 * h + 128), MUL, ind=R("rep", 0, 8))
         mm(R("a2" + F, 136 + c0, 136 + c0 + nc), R("x1", 128 * h, 128 * h + 128, rows=nl), R("cm", 0, nc, rows=nl), True, True)
+        if X == F:
+            act(R("nco", 0, nc), R("a2" + F, 136 + c0, 136 + c0 + nc), IDEN, bias=float(S + 2048), scale=-1.0)
         for c in range(c0, c0 + nc):
-            ts(R("e3", 256 * c + 16 * c, 256 * c + L), R("da", 16 * c, L), float(S + 2048), R("a2" + F, 136 + c, 137 + c), ADD, EQ)
+            same = R("e3", 256 * c + 16 * c, 256 * c + L)
+            if X == F and c >= c0 + nc - SCOLS:
+                far = R("far", 256 * (c % 2) + 16 * c, 256 * (c % 2) + L)
+                act(far, R("da4", 16 * c, L), ABS, bias=R("nco", c - c0, c - c0 + 1))
+                act(same, far, RELU, bias=1.0, scale=-1.0)
+            else:
+                ts(same, R("da", 16 * c, L), float(S + 2048), R("a2" + F, 136 + c, 137 + c), ADD, EQ)
             for o in sts[h:]:
                 w = R("ww", 8 * (c - c0), 8 * (c - c0) + 8) if o is st else R("ww", 64, 72)
                 mm(R("q2", 8 * o["h"], 8 * o["h"] + 8, rows=rows), R("e3", 256 * c + o["l0"], 256 * c + o["l0"] + rows), w,
@@ -577,6 +639,8 @@ def rank_program(g, core, T, topo):
         act(R("rq"), R("a1" + F, 0, 64), COPY)
         tt(R("gg", G, 16 * BW, BW), R("rq"), R("ce"), SUB, ind=R("gl", 0, 1))
 
+    for o in ops:
+        o["lazy"] = True
     exchange(0)
     for t in range(RO):
         sts = (stream("A", t), stream("B", t))

@@ -20,8 +20,9 @@ NC = NV // RR
 MAGIC = 12582912.0
 PEN = float(2 ** 26)
 DECAY = 1.04
-CHUNKS = {128: (32, 48, 48), 80: (48, 32), 64: (32, 32)}
-OPENING = {128: (48, 48, 32), 64: (32, 32)}
+CHUNKS = {128: (32, 32, 32, 32), 80: (32, 32, 16), 64: (32, 32)}
+PARTS = {128: ((0, 96), (96, 128)), 80: ((0, 64), (64, 80)), 64: ((0, 32), (32, 64))}
+OPENING = {128: (32, 32, 32, 32), 64: (32, 32)}
 
 SCRATCH = {}
 for _n, _w, _t in (
@@ -59,11 +60,11 @@ for _buf, _t, _names in (
     SCRATCH[_buf] = ("sbuf", [128, _o], _t)
 SEMAPHORES = ["sv", "ss", "sp", "sg", "go"] + ["d%d" % i for i in range(12)] + ["arr%d" % i for i in range(6)] + ["snd%d" % i for i in range(6)]
 
-CYC, GATHER, SCATTER, PECYC, WAKE = 0.00090, 1.55, 3.0, 0.00045, 0.13
+CYC, GATHER, SCATTER, PECYC, WAKE = 0.00090, 1.45, 3.8, 0.00050, 0.17
 TAIL, EARLY = 1.0, 3.0
-SCOLS = 6
+SCOLS = 4
 NEAR = 2
-FILL = 0.14
+FILL = 0.12
 
 
 def R(name, lo=None, hi=None, step=None, rows=128):
@@ -146,7 +147,48 @@ def in_order(ops):
             left[u] -= 1
             if not left[u]:
                 cand[ops[u]["q"]].append(u)
-    return [i for _, _, i in out]
+    start = [0.0] * n
+    for now, _, i in out:
+        start[i] = now
+    late = justify(ops, [{u: ops[u]["deps"][i] for u in users[i]} for i in range(n)], [-(start[i] + ops[i]["occ"]) for i in range(n)], True)
+    start = justify(ops, [o["deps"] for o in ops], [-(late[i] + ops[i]["occ"]) for i in range(n)], False)
+    rank = {i: k for k, i in enumerate(topological(ops, users))}
+    return sorted(range(n), key=lambda i: (start[i], rank[i]))
+
+
+def justify(ops, before, key, backward):
+    n = len(ops)
+    after = [[] for _ in range(n)]
+    for i in range(n):
+        for d in before[i]:
+            after[d].append(i)
+    left = [len(before[i]) for i in range(n)]
+    pool = sorted(((key[i], i) for i in range(n) if not left[i]), reverse=True)
+    busy = {}
+    start = [0.0] * n
+    while pool:
+        i = pool.pop()[1]
+        o = ops[i]
+        t = o["lat"] if backward and not before[i] else 0.0
+        for d, wait in before[i].items():
+            t = max(t, start[d] + ops[d]["occ"] + ((o if backward else ops[d])["lat"] if wait else 1e-6))
+        line = busy.setdefault(o["q"], [])
+        k = len(line)
+        while k and line[k - 1][1] > t:
+            k -= 1
+        while k < len(line) and line[k][0] < t + o["occ"]:
+            t = max(t, line[k][1])
+            k += 1
+        line.insert(k, (t, t + o["occ"]))
+        start[i] = t
+        for u in after[i]:
+            left[u] -= 1
+            if not left[u]:
+                j = len(pool)
+                while j and pool[j - 1] < (key[u], u):
+                    j -= 1
+                pool.insert(j, (key[u], u))
+    return start
 
 
 def rank_program(g, core, T, topo):
@@ -162,7 +204,8 @@ def rank_program(g, core, T, topo):
 
     def ap(r):
         name, lo, hi, step, rows = r
-        return T[name][0:rows, lo:hi] if step is None else T[name][0:rows, lo:hi:step]
+        p0, p1 = rows if isinstance(rows, tuple) else (0, rows)
+        return T[name][p0:p1, lo:hi] if step is None else T[name][p0:p1, lo:hi:step]
 
     def record(q, fn, reads, writes, occ, lat=WAKE, sem=None, inc=1, after=()):
         me = len(ops)
@@ -233,7 +276,7 @@ def rank_program(g, core, T, topo):
     def vcost(out, ins, ind, both=False):
         if ind:
             return 0.05 + width(out) * GATHER * CYC
-        return 0.02 + max(64, width(out) * (2 if both else 0.5 if narrow(out, *ins) else 1)) * CYC
+        return max(64, width(out) * (2 if both else 0.5 if narrow(out, *ins) else 1)) * CYC
 
     def src(r, ind):
         return ap(r).indirect(ap(ind)) if ind else ap(r)
@@ -283,12 +326,12 @@ def rank_program(g, core, T, topo):
 
     hx = S // 2
     d0 = dma("y", T.sdi[:], T.snd[:], [R("sdi")], [], 2.0)
-    d1 = dma("s", T.f[:, OWN + hx:OWN + S], T.x0[:, hx:S], [R("f", OWN + hx, OWN + S)], [], 5.5)
-    d2 = dma("y", T.f[:, OWN:OWN + hx], T.x0[:, 0:hx], [R("f", OWN, OWN + hx)], [], 5.5)
+    d1 = dma("s", T.f[:, OWN + hx:OWN + S], T.x0[:, hx:S], [R("f", OWN + hx, OWN + S)], [], 3.0)
+    d2 = dma("y", T.f[:, OWN:OWN + hx], T.x0[:, 0:hx], [R("f", OWN, OWN + hx)], [], 3.0)
     last = {"y": d2, "s": d1}
     ops[d2]["deps"][d0] = False
     for q, o, i, r, lat in (("s", T.wti[:], T.wt[:], R("wti"), 6.0), ("y", T.wni[:], T.wants[:], R("wni"), 6.0), ("y", T.pl[:, 0:M], T.pull[:], R("pl", 0, M), 6.5),
-                            ("s", T.nbw[:, hx:S], T.nb[:, hx:S], R("nbw", hx, S), 14.0), ("y", T.nbw[:, 0:hx], T.nb[:, 0:hx], R("nbw", 0, hx), 14.0)):
+                            ("s", T.nbw[:, hx:S], T.nb[:, hx:S], R("nbw", hx, S), 8.0), ("y", T.nbw[:, 0:hx], T.nb[:, 0:hx], R("nbw", 0, hx), 9.0)):
         d = dma(q, o, i, [r], [], lat)
         ops[d]["deps"][last[q]] = False
         last[q] = d
@@ -380,22 +423,29 @@ def rank_program(g, core, T, topo):
     ts(R("rep8"), R("jf", 0, 8), 2.0, col("q8"), MUL, ADD)
     ts(R("rep87"), R("jf", 0, 16), 8.0, 7.0, MUL, ADD)
     tc(R("wl", 0, 9), R("wni", 0, 9))
-    for t in (1, 2):
-        tc(R("wl", 10 * t + 1, 10 * t + 10), R("wni", 9 * t, 9 * t + 9))
     ms(R("wf"), 0.0)
     tc(R("wf", 0, 27), R("wni"))
-    for lo in range(0, 27, 8):
-        hi = min(27, lo + 8)
-        tt(R("wq", 16 * lo, 16 * hi), R("wf"), R("mask", 0, 16 * (hi - lo)), MUL, ind=R("rep", lo, hi))
-    tc(R("sdf", 0, 49), R("sdi"))
-    ms(R("sdf", 49, 56), 0.0)
-    for lo in range(0, 49, 8):
-        hi = min(49, lo + 8)
-        tt(R("sdx", 16 * lo, 16 * hi), R("sdf"), R("mask", 0, 16 * (hi - lo)), MUL, ind=R("rep", lo, hi))
-    ms(R("sdw", 0, 1), float(NULL))
-    for lo, hi in ((0, 4 * G), (4 * G, 7 * G)):
-        mm(R("q2", 0, hi - lo), R("blk"), R("sdx", lo, hi), True, True)
-        act(R("sdw", 1 + lo, 1 + hi), R("q2", 0, hi - lo), COPY)
+    tt(R("wq", 0, 160), R("wf"), R("mask", 0, 160), MUL, ind=R("rep", 0, 10))
+
+    def later_tables():
+        first, moved = len(ops), hist["ofl"][-1][4]
+        for t in (1, 2):
+            tc(R("wl", 10 * t + 1, 10 * t + 10), R("wni", 9 * t, 9 * t + 9))
+        for lo, hi in ((10, 18), (18, 27)):
+            tt(R("wq", 16 * lo, 16 * hi), R("wf"), R("mask", 0, 16 * (hi - lo)), MUL, ind=R("rep", lo, hi))
+        tc(R("sdf", 0, 49), R("sdi"))
+        ms(R("sdf", 49, 56), 0.0)
+        for lo in range(0, 49, 8):
+            hi = min(49, lo + 8)
+            tt(R("sdx", 16 * lo, 16 * hi), R("sdf"), R("mask", 0, 16 * (hi - lo)), MUL, ind=R("rep", lo, hi))
+        ms(R("sdw", 0, 1), float(NULL))
+        for lo, hi in ((0, 4 * G), (4 * G, 7 * G)):
+            mm(R("bpB", 0, hi - lo), R("blk"), R("sdx", lo, hi), True, True)
+            act(R("sdw", 1 + lo, 1 + hi), R("bpB", 0, hi - lo), COPY)
+        for o in ops[first:]:
+            o["lazy"] = True
+            if o["q"] == "v":
+                o["deps"].setdefault(moved, False)
 
     def calls_of(r):
         off = [e for e in range(1, N) if topo.chip(T.cores[(r + e) % N]) != topo.chip(T.cores[r])]
@@ -436,7 +486,7 @@ def rank_program(g, core, T, topo):
                                              srcs=[T.gg[:, (e - 1) * BW:e * BW]], dsts=[T["ld%d" % t][:, (7 - e) * BW:(8 - e) * BW]]))
             sem = "snd%d" % (2 * t + k)
             sent.append(record("g", lambda trs=trs, sem=sem: g.remote_dma_fused(trs, local_sem=T.sem[sem]), [R("gg", (e - 1) * BW, e * BW) for e in es], [],
-                               2.5 if t + k == 0 else 0.6, 5.0, sem, sum(len(x) for x in eng.values()), ()))
+                               2.5 if t + k == 0 else 0.6, 4.0, sem, sum(len(x) for x in eng.values()), ()))
         for k in range(1, len(calls)):
             ops[sent[k]]["deps"].setdefault(sent[k - 1], False)
         for k in range(len(calls)):
@@ -478,9 +528,14 @@ def rank_program(g, core, T, topo):
         X, h, nl, l0, nc = st["X"], st["h"], st["nl"], st["l0"], st["nc"]
         a1, a2, hh = "a1" + X, "a2" + X, (8 * h, 8 * h + 8)
         win, bb, me = R("f", OWN, FW), R("b", l0, l0 + nl), R(a1, 256, 264, rows=nl)
-        tc(R("off" + X, 0, nl), R("nbw"), ind=st["list"])
-        ops[-1]["early"] = TAIL
-        ts(bb, R("f", OWN, OWN + S) if hop == 1 and st["own"] else win, col("mid"), None, ADD, ind=st["list"])
+        ls = st["list"]
+        for c0, c1 in (((0, 2), (2, nc)) if hop > 1 else ((0, nc),)):
+            tc(R("off" + X, 16 * c0, 16 * c1), R("nbw"), ind=R(ls[0], ls[1] + c0, ls[1] + c1))
+            ops[-1]["early"] = TAIL
+        if st["own"] and (hop == 1 or st["t"] == 0):
+            ts(bb, R("f", OWN, OWN + S) if hop == 1 else win, col("mid"), None, ADD, ind=st["list"])
+        else:
+            act(bb, win, IDEN, bias=col("mid"), ind=st["list"])
         ops[-1]["early"] = EARLY
         ts(R("cp" + X, 0, nl), R("off" + X, 0, nl), col("nb"), None, ADD)
         if hop == 1 and st["own"]:
@@ -513,12 +568,18 @@ def rank_program(g, core, T, topo):
             for n in range(NC):
                 tt(R("m" + X, RR * (n * nl + lo), RR * (n * nl + hi)), R("a" + X, 16 * lo + n, 16 * hi, NC), R("bp" + X, RR * lo, RR * hi), MAX)
             lo = hi
-        for n in range(NV):
-            mm(R(a1, n, 256, 16, rows=nl), R("a" + X, n, 16 * nl, 16), R("wa", 0, 16), False, n == NV - 1)
+        for p0, p1 in PARTS[nl]:
+            for n in range(NV):
+                mm(R(a1, n, 256, 16, rows=(p0, p1)), R("a" + X, 16 * p0 + n, 16 * p1, 16), R("wa", 0, 16), False, n == NV - 1)
         spare = st["t"] == 0 or (hop == H and not st["opens"])
-        act(R("th" + X, rows=nl), R(a1, 0, 128, rows=nl), RELU, scale=2 * PEN)
         if spare:
+            act(R("th" + X, rows=nl), R(a1, 0, 128, rows=nl), RELU, scale=2 * PEN)
             act(R("u" + X, rows=nl), R(a1, 128, 256, rows=nl), COPY)
+        else:
+            ts(R("th" + X, rows=nl), R(a1, 0, 128, rows=nl), 0.0, 2 * PEN, MAX, MUL)
+        if st["t"] == 0 and hop < H:
+            turn[:] = [len(ops) - 1]
+            ops[-1]["deps"].setdefault(len(ops) - 2, False)
         if hop == 1:
             ts(R("fb", hh[0], hh[1], rows=nl), me, -(MID + 0.5) * K17, 100.0, LT, MUL)
         for n in range(NC):
@@ -527,12 +588,13 @@ def rank_program(g, core, T, topo):
             if spare and n == NC - 2:
                 mm(R(a2, 0, 128, rows=nl), R("nidf", 0, nl, rows=nl), R("th" + X, rows=nl), False, False)
         chain = len(ops)
-        if spare:
-            tt(R("k" + X, rows=nl), R("u" + X, rows=nl), R(a2, 0, 128, rows=nl), MIN)
-        else:
-            tt(R("u" + X, rows=nl), R(a2, 0, 128, rows=nl), R("th" + X, rows=nl), SUB)
-            tt(R("k" + X, rows=nl), R("u" + X, rows=nl), R(a1, 128, 256, rows=nl), MIN)
-        scan(R("sc" + X, rows=nl), R("rsm", rows=nl), R("k" + X, rows=nl), 0.0, ADD, MAX)
+        for lo, hi in ((0, 64), (64, 128)):
+            if spare:
+                tt(R("k" + X, lo, hi, rows=nl), R("u" + X, lo, hi, rows=nl), R(a2, lo, hi, rows=nl), MIN)
+            else:
+                tt(R("u" + X, lo, hi, rows=nl), R(a2, lo, hi, rows=nl), R("th" + X, lo, hi, rows=nl), SUB)
+                tt(R("k" + X, lo, hi, rows=nl), R("u" + X, lo, hi, rows=nl), R(a1, 128 + lo, 128 + hi, rows=nl), MIN)
+            scan(R("sc" + X, lo, hi, rows=nl), R("rsm", lo, hi, rows=nl), R("k" + X, lo, hi, rows=nl), 0.0, ADD, MAX)
         if hop == H and st["t"] == RO - 1:
             return
         tt(R("vi", hh[0], hh[1], rows=nl), R("sc" + X, 15, 128, 16, rows=nl), me, MAX)
@@ -558,7 +620,8 @@ def rank_program(g, core, T, topo):
         ts(R("zh"), R("zi" if t else "zq"), 5, 4095, SHR, AND)
         ts(R("zg"), R("zh"), float(S), float(S), LT, MUL)
         tt(R("dT"), R("zh"), R("zg"), ADD)
-        tt(R("dx"), R("dT"), R("mask"), MUL, ind=R("rep", 0, 16))
+        for k in (0, 1):
+            tt(R("dx", 128 * k, 128 * k + 128), R("dT", 8 * k, 8 * k + 8), R("mask", 0, 128), MUL, ind=R("rep", 0, 8))
         for st in sts:
             mm(R("q1", 16 + st["c0"], 16 + st["c0"] + st["nc"]), R("dx", 128 * st["h"], 128 * st["h"] + 128, rows=st["nl"]),
                R("cm", 0, st["nc"], rows=st["nl"]), True, True)
@@ -632,7 +695,8 @@ def rank_program(g, core, T, topo):
         mm(R(bp, 320, 384, rows=B["nl"]), R("ones", 0, B["nl"], rows=A["nl"]), R("on", 0, 64, rows=A["nl"]), False, True)
         scan(R("qs"), R("rs8"), R(bp, 256, 384), 0.0, MUL, MAX)
         tt(R("ek"), R("idm"), R("on"), MUL, ind=R("rep8"))
-        tt(R("mh"), R("qs"), R("jm1"), EQ, ind=R("rep87"))
+        for k in (0, 1):
+            tt(R("mh", 128 * k, 128 * k + 128), R("qs"), R("jm1", 0, 128), EQ, ind=R("rep87", 8 * k, 8 * k + 8))
         for st in sts:
             nl, h = st["nl"], st["h"]
             mm(R("a1" + F, 0, 64), R("mh", 128 * h, 128 * h + 128, rows=nl), R("ek", 64 * h, 64 * h + 64, rows=nl), h == 0, h == 1)
@@ -658,6 +722,8 @@ def rank_program(g, core, T, topo):
         if t + 1 < RO:
             requests(sts, F)
         moves(sts)
+        if t == 0:
+            later_tables()
         if t + 1 < RO:
             exchange(t + 1)
     dma("y", T.y[:], T.f[:, OWN:OWN + S], [], [R("f", OWN, OWN + S)], 5.0)

@@ -8,9 +8,10 @@ ABS = ActivationFunctionType.Abs
 IDEN, COPY, RELU, EXP = ActivationFunctionType.Identity, ActivationFunctionType.Copy, ActivationFunctionType.Relu, ActivationFunctionType.Exp
 
 N, S, G, CAP, WN, M, RO, H, T0 = 8, 3328, 112, 16, 144, 512, 3, 4, 192
-OWN = 512
+OWN = 0
 NULL = S + (N - 1) * G
-FW = OWN + NULL + 16
+WIN = NULL + 16
+FW = WIN + 512
 BW = 120
 K17 = 17 * 8192
 MID = 97
@@ -19,9 +20,12 @@ RR = 4
 NC = NV // RR
 MAGIC = 12582912.0
 PEN = float(2 ** 26)
+TOP = 14 * 2 ** 20
+HUGE = float(2 ** 95)
 DECAY = 1.04
 CHUNKS = {128: (32, 32, 32, 32), 80: (32, 32, 16), 64: (32, 32)}
-PARTS = {128: ((0, 96), (96, 128)), 80: ((0, 64), (64, 80)), 64: ((0, 32), (32, 64))}
+PARTS = {128: ((0, 64), (64, 96), (96, 128)), 80: ((0, 32), (32, 64), (64, 80)), 64: ((0, 32), (32, 64))}
+ZEARLY = 0.0
 OPENING = {128: (32, 32, 32, 32), 64: (32, 32)}
 
 SCRATCH = {}
@@ -29,30 +33,34 @@ for _n, _w, _t in (
         ("f", FW, "bfloat16"), ("nbw", NULL + 16, "int32"), ("pl", OWN + S, "bfloat16"), ("wti", 1, "int32"), ("wni", 27, "int32"), ("sdi", 49, "int32"),
         ("sdp", 56, "uint16"), ("sdf", 56, "float32"), ("sdw", 800, "float32"), ("sdx", 784, "float32"), ("wl", 30, "uint16"), ("rep", 50, "uint16"),
         ("wq", 432, "float32"), ("jf", 128, "float32"), ("jmf", 256, "float32"), ("jm1", 256, "float32"), ("j4", 128, "float32"), ("j7", 128, "float32"),
-        ("j16", 64, "float32"), ("ji", 64, "int32"), ("cols", 40, "float32"), ("idf", 128, "float32"), ("mask1", 144, "float32"), ("rep1", 10, "uint16"), ("idb", 128, "bfloat16"),
-        ("nid", 128, "bfloat16"), ("nidf", 128, "float32"), ("da4", 256, "float32"), ("far", 512, "float32"), ("nco", 8, "float32"), ("mask", 256, "float32"), ("rep8", 8, "uint16"), ("rep87", 16, "uint16"), ("gl", 2, "uint16"), ("blk", 128, "float32"),
-        ("wa", 24, "bfloat16"), ("wb", 256, "bfloat16"), ("mpen", 128, "bfloat16"), ("wz", 8, "bfloat16"), ("ws", 8, "bfloat16"), ("ww", 80, "bfloat16"), ("wwf", 64, "float32"),
-        ("cm2", 8, "bfloat16"), ("rsm", 128, "float32"), ("rsa", 128, "float32"), ("rs8", 128, "float32"), ("tril", 128, "bfloat16"), ("ones", 128, "bfloat16"),
+        ("j16", 8, "float32"), ("ji", 64, "int32"), ("cols", 40, "float32"), ("idf", 128, "float32"), ("mask1", 144, "float32"), ("rep1", 10, "uint16"), ("idb", 128, "bfloat16"),
+        ("nid", 128, "bfloat16"), ("hug", 128, "bfloat16"), ("da4", 256, "float32"), ("far", 512, "float32"), ("nco", 8, "float32"), ("mask", 256, "float32"), ("rep8", 8, "uint16"), ("rep87", 16, "uint16"), ("gl", 2, "uint16"), ("blk", 128, "float32"),
+        ("wa", 16, "bfloat16"), ("wm", 16, "bfloat16"), ("wn", 8, "bfloat16"), ("wz", 144, "bfloat16"), ("wk", 128, "bfloat16"), ("ws", 128, "bfloat16"), ("mn", 128, "bfloat16"),
+        ("ww", 9 * 128, "bfloat16"), ("wwf", 8, "float32"),
+        ("cm8", 8, "bfloat16"), ("rsa", 128, "float32"), ("rs8", 128, "float32"), ("tril", 128, "bfloat16"), ("ones", 128, "bfloat16"),
         ("mhalf", 256, "bfloat16"), ("ec", 128, "float32"), ("onf", 128, "float32"), ("b", 256, "bfloat16"), ("xx", 288, "float32"), ("dx", 256, "float32"),
-        ("x1", 256, "float32"), ("x2", 256, "bfloat16"), ("dl", 16, "uint16"), ("fb", 32, "bfloat16"), ("fd", 256, "bfloat16"), ("uu", 256, "bfloat16"),
+        ("x2", 256, "bfloat16"), ("dl", 32, "uint16"), ("fd", 256, "bfloat16"), ("uu", 256, "bfloat16"),
         ("uv", 256, "float32"), ("val", 512, "bfloat16"), ("ramp", OWN + S, "float32"), ("da", 256, "float16"), ("ofl", 32, "uint16"), ("on", 128, "bfloat16"),
         ("qs", 128, "float32"), ("mh", 256, "float16"), ("ek", 128, "float16"), ("rq", 64, "float32"), ("gg", 16 * BW, "bfloat16"), ("ld0", 7 * BW, "bfloat16"),
         ("ld1", 7 * BW, "bfloat16"), ("ld2", 7 * BW, "bfloat16"), ("rki", 8, "uint16"), ("rkj", 8, "uint16"), ("qa", 128, "float32"), ("qc", 128, "float32")):
     SCRATCH[_n] = ("sbuf", [128, _w], _t)
 for _x in "AB":
     for _n, _w, _t in (("l", 8, "uint16"), ("off", 128, "uint16"), ("a", 2048, "bfloat16"), ("m", 2048, "bfloat16"), ("cp", 128, "float32"),
-                       ("th", 128, "float32"), ("u", 128, "float32"), ("k", 128, "float32"), ("sc", 128, "float32")):
+                       ("nf", 128, "bfloat16"), ("gf", 128, "bfloat16"), ("tx", 128, "float32"), ("nx", 128, "bfloat16")):
         SCRATCH[_n + _x] = ("sbuf", [128, _w], _t)
+    SCRATCH["t" + _x] = ("sbuf", [128, 8, 18], "float32")
+    SCRATCH["s" + _x] = ("psum", [128, 8, 16, 4], "float32")
 SCRATCH["e3"] = ("sbuf", [128, 16 * 256], "bfloat16")
-for _n in ("a1A", "a1B", "a2A", "a2B", "bpA", "bpB", "q1", "q2"):
+SCRATCH["wb"] = ("sbuf", [128, 128], "bfloat16")
+SCRATCH["mc"] = ("sbuf", [128, 384], "bfloat16")
+SCRATCH["mt"] = ("sbuf", [128, 16], "bfloat16")
+for _n in ("kA", "kB", "bpA", "bpB", "q1", "q2"):
     SCRATCH[_n] = ("psum", [128, 512], "float32")
 PSUMS = [k for k in SCRATCH if SCRATCH[k][0] == "psum"]
 ALIAS = {}
 for _buf, _t, _names in (
-        ("tf", "float32", (("dT", 16), ("cand", 16), ("first", 16), ("eb", 16), ("idm", 16), ("ce", 16), ("c112", 8), ("rk", 8), ("rl8", 8), ("cm", 8), ("sfA", 8),
-                           ("sfB", 8), ("base", 32), ("of", 32), ("a12", 32), ("wf", 32))),
-        ("ti", "int32", (("vi", 16), ("id0", 16), ("id1", 16), ("zi", 16), ("zm", 16), ("zq", 16), ("zh", 16), ("zg", 16), ("ebi", 16), ("rpi", 8), ("ci", 8),
-                         ("z7", 16)))):
+        ("tf", "float32", (("dT", 16), ("idm", 16), ("ce", 16), ("c112", 8), ("cm", 8), ("base", 32), ("base2", 32), ("wf", 32))),
+        ("ti", "int32", (("vi", 16), ("id0", 16), ("id1", 16), ("zi", 16), ("zm", 16), ("zq", 16), ("zh", 16), ("zg", 16), ("ebi", 16), ("ci", 8)))):
     _o = 0
     for _n, _w in _names:
         ALIAS[_n] = (_buf, _o, _w)
@@ -60,9 +68,15 @@ for _buf, _t, _names in (
     SCRATCH[_buf] = ("sbuf", [128, _o], _t)
 SEMAPHORES = ["sv", "ss", "sp", "sg", "go"] + ["d%d" % i for i in range(12)] + ["arr%d" % i for i in range(6)] + ["snd%d" % i for i in range(6)]
 
-CYC, GATHER, SCATTER, PECYC, WAKE = 0.00090, 1.45, 3.8, 0.00050, 0.17
-TAIL, EARLY = 1.0, 3.0
-SCOLS = 4
+CYC, GATHER, SCATTER, PECYC, WAKE = 0.00083, 1.56, 3.8, 0.00042, 0.17
+TAIL, EARLY = 1.0, 1.5
+BV, MES = (True, False), (False, False)
+ALL8, ALL16, HALVES = (0, 8), (0, 16), ((0, 8),)
+CLOSING = {128: (32, 32, 32, 16, 16), 80: (32, 32, 16)}
+SCOLS = (0, 0)
+PASSES = 1
+CPS = False
+ONV = {}
 NEAR = 2
 FILL = 0.12
 
@@ -76,8 +90,16 @@ def R(name, lo=None, hi=None, step=None, rows=128):
     return (name, lo, hi, step, rows)
 
 
+def RN(name, *idx, rows=128):
+    dims = SCRATCH[name][1][1:]
+    n = total = 1
+    for d, i in zip(dims, idx):
+        n, total = n * (1 if isinstance(i, int) else i[1] - i[0]), total * d
+    return (name, 0, total, None, rows, tuple(i if isinstance(i, int) else slice(i[0], i[1]) for i in idx), n)
+
+
 def width(r):
-    return len(range(r[1], r[2], r[3] or 1))
+    return r[6] if len(r) > 5 else len(range(r[1], r[2], r[3] or 1))
 
 
 def narrow(*rs):
@@ -91,6 +113,13 @@ def meet(r, lo, hi, step):
         return True
     (a, b, s), (c, d) = ((lo, hi, step), r[1:3]) if step else (r[1:4], (lo, hi))
     return a + max(0, -((a - c) // s)) * s < min(b, d)
+
+
+def boxes_meet(a, b):
+    if not a or not b:
+        return True
+    ends = [[(i, i + 1) if isinstance(i, int) else (i.start, i.stop) for i in x[0]] for x in (a, b)]
+    return all(p[0] < q[1] and q[0] < p[1] for p, q in zip(*ends))
 
 
 def topological(ops, users):
@@ -150,8 +179,10 @@ def in_order(ops):
     start = [0.0] * n
     for now, _, i in out:
         start[i] = now
-    late = justify(ops, [{u: ops[u]["deps"][i] for u in users[i]} for i in range(n)], [-(start[i] + ops[i]["occ"]) for i in range(n)], True)
-    start = justify(ops, [o["deps"] for o in ops], [-(late[i] + ops[i]["occ"]) for i in range(n)], False)
+    back = [{u: ops[u]["deps"][i] for u in users[i]} for i in range(n)]
+    for _ in range(PASSES):
+        late = justify(ops, back, [-(start[i] + ops[i]["occ"]) for i in range(n)], True)
+        start = justify(ops, [o["deps"] for o in ops], [-(late[i] + ops[i]["occ"]) for i in range(n)], False)
     rank = {i: k for k, i in enumerate(topological(ops, users))}
     return sorted(range(n), key=lambda i: (start[i], rank[i]))
 
@@ -203,8 +234,10 @@ def rank_program(g, core, T, topo):
     turn = []
 
     def ap(r):
-        name, lo, hi, step, rows = r
+        name, lo, hi, step, rows = r[0:5]
         p0, p1 = rows if isinstance(rows, tuple) else (0, rows)
+        if len(r) > 5:
+            return T[name][(slice(p0, p1),) + r[5]]
         return T[name][p0:p1, lo:hi] if step is None else T[name][p0:p1, lo:hi:step]
 
     def record(q, fn, reads, writes, occ, lat=WAKE, sem=None, inc=1, after=()):
@@ -213,10 +246,10 @@ def rank_program(g, core, T, topo):
         acc = [(r, False) for r in reads] + [(r, True) for r in writes]
         for r, w in acc:
             name, bank = r[0], r[0] in PSUMS
-            for lo, hi, ow, oq, o, st in hist.get(name, ()):
+            for lo, hi, ow, oq, o, st, box in hist.get(name, ()):
                 if bank and oq == q == "p":
                     deps.setdefault(o, False)
-                elif (bank and oq != q) or ((w or ow) and meet(r, lo, hi, st)):
+                elif (bank and oq != q) or ((w or ow) and meet(r, lo, hi, st) and boxes_meet(r[5:6], box)):
                     deps[o] = True
         for r, w in acc:
             name, bank = r[0], r[0] in PSUMS
@@ -225,9 +258,9 @@ def rank_program(g, core, T, topo):
                 lst = []
             elif bank and lst and lst[-1][3] != q:
                 lst = [x for x in lst if x[3] == lst[-1][3]]
-            elif w and not bank and r[3] is None and r[4] == 128:
+            elif w and not bank and r[3] is None and r[4] == 128 and len(r) == 5:
                 lst = [x for x in lst if not (x[0] >= r[1] and x[1] <= r[2])]
-            hist[name] = lst + [(r[1], r[2], w, q if sem is None else None, me, r[3])]
+            hist[name] = lst + [(r[1], r[2], w, q if sem is None else None, me, r[3], r[5:6])]
         ops.append({"q": q, "fn": fn, "deps": deps, "occ": occ, "lat": lat, "sem": sem, "inc": inc, "early": 0.0, "lazy": False})
         return me
 
@@ -298,6 +331,13 @@ def rank_program(g, core, T, topo):
     def scan(out, d0, d1, init, o0, o1):
         record("v", lambda: g.vector.tensor_tensor_scan(ap(out), ap(d0), ap(d1), init, o0, o1), [d0, d1], [out], vcost(out, [d0, d1], None))
 
+    def red(out, in_, op):
+        record("v", lambda: g.vector.tensor_reduce(ap(out), ap(in_), AxisListType.X, op), [in_], [out], max(64, width(in_)) * CYC)
+
+    def gcopy(out, in_):
+        n = width(out)
+        record("g", lambda: g.affine_select(ap(out), ap(in_), [[0, n]], GE, 0.0, 0, 0), [in_], [out], 0.17 + 2 * n * CYC)
+
     def ms(out, c):
         record("v", lambda: g.vector.memset(ap(out), c), [], [out], vcost(out, [], None))
 
@@ -343,18 +383,19 @@ def rank_program(g, core, T, topo):
     iota(R("ji"), [[1, 64]], 0, 0, False)
     iota(R("nbw", S, NULL + 1), [[1, NULL + 1 - S]], S, 0, False)
     iota(R("j7"), [[0, 16], [1, 8]], 0, 0)
-    iota(R("j16"), [[16, 8], [0, 8]], 0, 0)
+    iota(R("j16"), [[16, 8]], 0, 0)
     iota(R("c112"), [[G, 8]], 0, 0)
     for lo in range(0, OWN + S, 256):
         iota(R("ramp", lo, lo + 256), [[1, 256]], lo - OWN - 2048, 0)
     ms(R("gg", 0, 7 * BW), 0.0)
-    for nm in ("id0", "id1"):
+    for nm in ("id0", "id1", "vi"):
         ms(R(nm), 0)
-    for r in (R("cand"), R("fb"), R("q1", 0, 96), R("q2", 0, 16), R("bpA", 256, 384), R("f", 0, OWN)):
+    ms(R("dl"), 0)
+    for r in (R("txA"), R("txB"), R("bpA", 256, 384), R("val", WN, WN + 16), R("wz")):
         ms(r, 0.0)
     for c in range(1, 16):
         ms(R("e3", 256 * c + (0 if c < 8 else 64 if c == 8 else 128), 256 * c + 16 * c), 0.0)
-    ms(R("f", OWN + NULL, FW), -1.0)
+    ms(R("f", NULL, WIN), -1.0)
     ms(R("ones"), 1.0)
     ms(R("mhalf"), -0.5)
     ts(R("ci", 1, 2), R("ci", 0, 1), 15, None, AND)
@@ -366,43 +407,47 @@ def rank_program(g, core, T, topo):
         tc(R("sdp", 8 * e, 8 * e + 7), R("sdi", 7 * e, 7 * e + 7))
     ts(col("r15"), col("q"), 15.0, None, EQ)
     ts(col("rl"), col("q"), 15.0, None, LT)
-    for nm, of, c in (("mid", "r15", -MID), ("k17", "r15", K17), ("neg", "r15", -1), ("full", "r15", -4 * PEN), ("nrl", "rl", -1), ("mag", "rl", -MAGIC),
+    for nm, of, c in (("mid", "r15", -MID), ("k17", "r15", K17), ("neg", "r15", -1), ("full", "r15", -PEN), ("mag", "rl", -MAGIC),
                       ("big", "rl", 2 * PEN), ("nbig", "rl", -2 * PEN)):
         ts(col(nm), col(of), float(c), None, MUL)
-    ts(col("nb"), col("q"), -8192.0, -8192.0, MUL, ADD)
     for t in range(RO):
         ts(col("vb%d" % t), col("r15"), float(T0 + t), col("mag"), MUL, ADD)
     ts(R("cm"), R("jf", 0, 8), col("g"), None, EQ)
     ts(R("idf"), R("jf"), col("p"), None, EQ)
     ts(R("blk"), R("j4"), col("g"), None, EQ)
     ts(R("mask"), R("jmf"), col("q"), None, EQ)
-    ts(R("rsm"), R("jmf", 0, 128), 0.0, -2 * PEN, EQ, MUL)
     ts(R("rsa"), R("jmf", 0, 128), 0.0, None, GT)
     ts(R("jm1"), R("jmf"), 1024.0, None, ADD)
     tc(col("wt"), R("wti"))
     tt(col("wtl"), col("wt"), col("rl"), MUL)
     act(R("idb"), R("idf"), COPY)
-    act(R("nid"), R("idf"), COPY, scale=-PEN)
-    act(R("nidf"), R("idf"), COPY, scale=-1.0)
-    act(R("wa", 0, 8), R("cm"), COPY, scale=col("rl"))
-    act(R("wa", 8, 16), R("cm"), COPY, scale=col("k17"))
-    act(R("wa", 16, 24), R("cm"), COPY, scale=col("big"))
-    act(R("wb", 0, 128), R("blk"), COPY, scale=col("nrl"))
-    act(R("wb", 128, 256), R("blk"), COPY, scale=col("nbig"))
-    ms(R("mpen"), -PEN)
-    act(R("ws"), R("cm"), COPY, scale=col("full"))
-    act(R("wz"), R("cm"), COPY, scale=col("wtl"))
-    act(R("cm2"), R("cm"), COPY, scale=2.0)
-    for k in range(1, 8):
+    act(R("hug"), R("idf"), COPY, scale=HUGE)
+    act(R("wa", 0, 16, 2), R("cm"), COPY, scale=col("nbig"))
+    act(R("wa", 1, 16, 2), R("cm"), COPY, scale=col("k17"))
+    for k in (0, 1):
+        act(R("wm", k, 16, 2), R("cm"), COPY, scale=col("big"))
+    act(R("wb"), R("blk"), COPY, scale=col("nbig"))
+    ms(R("mc", rows=1), -PEN)
+    ts(R("mc", 2, 384, 3, rows=1), R("jmf", 0, 128, rows=1), -8192.0, -8192.0, MUL, ADD)
+    ms(R("mt", rows=3), 0.0)
+    for k, c in enumerate((NULL % 4096, NULL - NULL % 4096, TOP)):
+        ms(R("mt", 1, 16, 2, rows=3 - k), float(c))
+    act(R("wn"), R("cm"), COPY, scale=col("full"))
+    act(R("wk"), R("blk"), COPY, scale=col("k17"))
+    act(R("ws"), R("blk"), COPY, scale=col("full"))
+    act(R("mn"), R("mask", 0, 128), IDEN, scale=PEN, bias=-PEN)
+    act(R("wz", 15, 143, 16), R("cm"), COPY, scale=col("wtl"))
+    act(R("cm8"), R("cm"), COPY, scale=8192.0)
+    for k in range(1, 7):
         hi = min(M * (k + 1), OWN + S)
         act(R("pl", M * k, hi), R("pl", 0, hi - M * k), COPY)
     ts(col("wq"), col("q"), -DECAY, 62.0, MUL, ADD)
     ts(col("wp"), col("p"), -DECAY, 62.74, MUL, ADD)
     act(R("wwf"), R("j16"), EXP, bias=col("wq"), scale=-DECAY, more=1.3)
     act(col("thr"), col("wp"), EXP)
-    ts(R("onf", 0, 64), R("j7", 0, 64), col("g"), None, EQ)
-    tt(R("ww", 0, 64), R("wwf"), R("onf", 0, 64), MUL)
-    act(R("ww", 64, 72), R("cm"), COPY, scale=float(2 ** 95))
+    for c in range(8):
+        act(R("ww", 128 * c, 128 * c + 128), R("blk"), COPY, scale=R("wwf", c, c + 1))
+    act(R("ww", 1024, 1152), R("blk"), COPY, scale=HUGE)
     ts(R("rs8"), R("j7"), 0.0, None, GT)
     ts(R("ec"), R("j7"), -1.0, 7.0, MUL, ADD)
     ts(R("onf"), R("j7"), 7.0, 50.0, EQ, MUL)
@@ -414,7 +459,10 @@ def rank_program(g, core, T, topo):
     ts(R("ce"), R("ce"), 0.0, None, MAX)
     ts(col("g8"), col("g"), 8.0, None, MUL)
     ts(R("gl", 0, 1), col("q"), 7.0, col("g8"), MIN, ADD)
-    ts(R("base"), R("jf", 0, 32), 16.0, col("q"), MUL, ADD)
+    ts(col("qb"), col("q"), float(WIN - 16 * 8192), None, ADD)
+    for nm in ("base", "base2"):
+        ts(R(nm), R("jf", 0, 32), 16.0, col("qb"), MUL, ADD)
+    ts(R("base", WN // 16, WN // 16 + 1), R("base2", WN // 16, WN // 16 + 1), float(16 * 8192), None, ADD)
     tc(R("rep"), R("ji", 0, 50))
     tc(R("rep1", 0, 8), R("ji", 0, 8))
     ts(R("rep1", 8, 9), col("q"), 7.0, None, MIN)
@@ -516,8 +564,7 @@ def rank_program(g, core, T, topo):
             st["diag"] = R("wq", 144 * t + 16, 144 * t + 144)
         else:
             act(R("qa", 112, 128), R("wq", 144 * t, 144 * t + 16), COPY)
-            tt(R("rk", 0, 7), R("ld%d" % t, G, 7 * BW, BW), R("c112", 0, 7), ADD)
-            tc(R("rki", 0, 7), R("rk", 0, 7))
+            tt(R("rki", 0, 7), R("ld%d" % t, G, 7 * BW, BW), R("c112", 0, 7), ADD)
             tt(R("qa", 0, 112), R("sdw", 0, 785), R("mask", 0, 112), MUL, ind=R("rki", 0, 7))
             scan(R("qc"), R("rsa"), R("qa"), 0.0, MUL, ADD)
             tc(R("lA"), R("qc", 15, 128, 16))
@@ -526,39 +573,53 @@ def rank_program(g, core, T, topo):
 
     def look(st, hop, ncs):
         X, h, nl, l0, nc = st["X"], st["h"], st["nl"], st["l0"], st["nc"]
-        a1, a2, hh = "a1" + X, "a2" + X, (8 * h, 8 * h + 8)
-        win, bb, me = R("f", OWN, FW), R("b", l0, l0 + nl), R(a1, 256, 264, rows=nl)
+        sq, hh = "s" + X, (8 * h, 8 * h + 8)
+        win, bb, me = R("f", 0, WIN), R("b", l0, l0 + nl), R("k" + X, 256, 272, 2, rows=nl)
         ls = st["list"]
+        named = hop < H or st["t"] < RO - 1
+        wide = 18 if hop == 1 else 17
+        first = len(ops)
         for c0, c1 in (((0, 2), (2, nc)) if hop > 1 else ((0, nc),)):
             tc(R("off" + X, 16 * c0, 16 * c1), R("nbw"), ind=R(ls[0], ls[1] + c0, ls[1] + c1))
             ops[-1]["early"] = TAIL
-        if st["own"] and (hop == 1 or st["t"] == 0):
-            ts(bb, R("f", OWN, OWN + S) if hop == 1 else win, col("mid"), None, ADD, ind=st["list"])
+        if st["own"] and hop == 1 or BV[st["t"] > 0]:
+            ts(bb, R("f", OWN, OWN + S) if hop == 1 and st["own"] else win, col("mid"), None, ADD, ind=st["list"])
         else:
             act(bb, win, IDEN, bias=col("mid"), ind=st["list"])
         ops[-1]["early"] = EARLY
-        ts(R("cp" + X, 0, nl), R("off" + X, 0, nl), col("nb"), None, ADD)
+        if named and st["t"] == 0 and (hop == 1 or CPS):
+            act(R("cp" + X, 0, nl), R("off" + X, 0, nl), COPY)
+        elif named:
+            gcopy(R("cp" + X, 0, nl), R("off" + X, 0, nl))
+        if hop == 1:
+            ts(R("nf" + X, 0, nl), bb, -MID - 0.5, None, GE)
         if hop == 1 and st["own"]:
-            for o in ops[-3:]:
+            for o in ops[first:]:
                 o["early"], o["lazy"] = 0.0, True
         for j in range(RR):
             mm(R("bp" + X, j, RR * nl, RR), R("idb"), bb, True, True)
-        mm(R(a1, 0, 128, rows=nl), bb, R("wb", 0, 128), True, False)
-        mm(me, bb, R("wa", 8, 16), False, False)
+        mm(RN(sq, ALL8, ALL16, (0, 3), rows=nl), R("ones", 0, nl, rows=1), R("mc", rows=1), True, False)
+        mm(RN(sq, ALL8, ALL16, 0, rows=nl), bb, R("wb"), False, False)
         if hop == 1:
+            mm(R("k" + X, 256, 272, rows=nl), R("ones", 0, nl, rows=3), R("mt", rows=3), True, False)
             mm(me, st["diag"], R("cm"), False, False)
+            mm(R("k" + X, 257, 272, 2, rows=nl), R("nf" + X, 0, nl), R("wn"), False, False)
         else:
-            mm(me, R("idf", 0, nl, rows=nl), R("xx", 144 * h + 128, 144 * h + 136, rows=nl), False, False)
-        mm(R(a2, 0, 128, rows=nl), bb, R("wb", 128, 256), True, False)
-        mm(R(a2, 0, 128, rows=nl), R("ones", 0, nl, rows=1), R("mpen", rows=1), False, False)
-        mm(R(a1, 128, 256, rows=nl), R("cp" + X, 0, nl), R("idf"), False, False)
-        if hop == H:
-            mm(R("q1", hh[0], hh[1], rows=nl), bb, R("wz"), True, True)
+            mm(me, R("idf", 0, nl, rows=nl), R("xx", 144 * h + 128, 144 * h + 136, rows=nl), True, False)
+        mm(me, bb, R("wa", 1, 16, 2), False, True)
+        own = (RN("t" + X, ALL8, (16, 18), rows=nl), R("k" + X, 256, 272, rows=nl)) if hop == 1 else (RN("t" + X, ALL8, 16, rows=nl), me)
+        if MES[st["t"] > 0]:
+            act(own[0], own[1], COPY)
+        else:
+            tc(own[0], own[1])
+        if named:
+            mm(RN(sq, ALL8, ALL16, 2, rows=nl), R("cp" + X, 0, nl), R("idf"), False, False)
         lo = 0
         opening = hop == 1 and st["opens"]
-        for w in (OPENING if opening else CHUNKS)[nl]:
+        closing = hop == H and not st["opens"]
+        for k, w in enumerate((OPENING if opening else CLOSING if closing else CHUNKS)[nl]):
             hi = lo + w
-            if opening and lo == 0:
+            if k == (0 if opening else ONV.get(nl)):
                 ts(R("a" + X, 16 * lo, 16 * hi), win, col("mid"), None, ADD, ind=R("off" + X, lo, hi))
             else:
                 act(R("a" + X, 16 * lo, 16 * hi), win, IDEN, bias=col("mid"), ind=R("off" + X, lo, hi))
@@ -570,124 +631,106 @@ def rank_program(g, core, T, topo):
             lo = hi
         for p0, p1 in PARTS[nl]:
             for n in range(NV):
-                mm(R(a1, n, 256, 16, rows=(p0, p1)), R("a" + X, 16 * p0 + n, 16 * p1, 16), R("wa", 0, 16), False, n == NV - 1)
-        spare = st["t"] == 0 or (hop == H and not st["opens"])
-        if spare:
-            act(R("th" + X, rows=nl), R(a1, 0, 128, rows=nl), RELU, scale=2 * PEN)
-            act(R("u" + X, rows=nl), R(a1, 128, 256, rows=nl), COPY)
-        else:
-            ts(R("th" + X, rows=nl), R(a1, 0, 128, rows=nl), 0.0, 2 * PEN, MAX, MUL)
-        if st["t"] == 0 and hop < H:
-            turn[:] = [len(ops) - 1]
-            ops[-1]["deps"].setdefault(len(ops) - 2, False)
-        if hop == 1:
-            ts(R("fb", hh[0], hh[1], rows=nl), me, -(MID + 0.5) * K17, 100.0, LT, MUL)
-        for n in range(NC):
-            for j in range(RR):
-                mm(R(a2, n + NC * j, 128, 16, rows=nl), R("m" + X, RR * n * nl + j, RR * (n + 1) * nl, RR), R("wa", 16, 24), False, n == NC - 1 and j == RR - 1)
-            if spare and n == NC - 2:
-                mm(R(a2, 0, 128, rows=nl), R("nidf", 0, nl, rows=nl), R("th" + X, rows=nl), False, False)
+                mm(RN(sq, ALL8, n, (1, 3), rows=(p0, p1)), R("a" + X, 16 * p0 + n, 16 * p1, 16), R("wa"), False, False)
+            for n in range(NC):
+                for j in range(RR):
+                    mm(RN(sq, ALL8, n + NC * j, (0, 2), rows=(p0, p1)), R("m" + X, RR * (n * nl + p0) + j, RR * (n * nl + p1), RR), R("wm"), False,
+                       n == NC - 1 and j == RR - 1)
         chain = len(ops)
-        for lo, hi in ((0, 64), (64, 128)):
-            if spare:
-                tt(R("k" + X, lo, hi, rows=nl), R("u" + X, lo, hi, rows=nl), R(a2, lo, hi, rows=nl), MIN)
-            else:
-                tt(R("u" + X, lo, hi, rows=nl), R(a2, lo, hi, rows=nl), R("th" + X, lo, hi, rows=nl), SUB)
-                tt(R("k" + X, lo, hi, rows=nl), R("u" + X, lo, hi, rows=nl), R(a1, 128 + lo, 128 + hi, rows=nl), MIN)
-            scan(R("sc" + X, lo, hi, rows=nl), R("rsm", lo, hi, rows=nl), R("k" + X, lo, hi, rows=nl), 0.0, ADD, MAX)
-        if hop == H and st["t"] == RO - 1:
-            return
-        tt(R("vi", hh[0], hh[1], rows=nl), R("sc" + X, 15, 128, 16, rows=nl), me, MAX)
-        ts(R("id%d" % (hop % 2), hh[0], hh[1], rows=nl), R("vi", hh[0], hh[1], rows=nl), 8191, None, AND)
+        for g0, g1 in HALVES:
+            red(RN("t" + X, (g0, g1), ALL16, rows=nl), RN(sq, (g0, g1), ALL16, (0, 3), rows=nl), MIN)
+        red(R("vi", hh[0], hh[1], rows=nl), RN("t" + X, ALL8, (0, wide), rows=nl), MAX)
+        if named:
+            ts(R("id%d" % (hop % 2), hh[0], hh[1], rows=nl), R("vi", hh[0], hh[1], rows=nl), 8191, None, AND)
         if hop < H:
             tt(R("xx", 144 * h, 144 * h + 144), R("id%d" % (hop % 2), hh[0], hh[1]), R("mask1"), MUL, ind=R("rep1", 0, 9))
-            mm(R(a2, 128, 128 + nc), R("xx", 144 * h, 144 * h + 128, rows=nl), R("cm", 0, nc, rows=nl), True, True)
-            tc(R("l" + X, 0, nc), R(a2, 128, 128 + nc))
-            st["list"] = R("l" + X, 0, nc)
+            mm(R("k" + X, 0, nc), R("xx", 144 * h, 144 * h + 128, rows=nl), R("cm", 0, nc, rows=nl), True, True)
+            at = ncs + ncs % 2 + st["c0"]
+            st["list"] = R("l" + X, 0, nc) if hop < H - 1 else R("dl", at, at + nc)
+            tc(st["list"], R("k" + X, 0, nc))
         for o in ops[chain:]:
             o["early"] = TAIL
-        if hop == H - 1:
-            act(R("a12", ncs + st["c0"], ncs + st["c0"] + nc), R(a2, 128, 128 + nc), IDEN, bias=float(OWN))
 
     def places(t, sts, F):
         nc = sum(st["nc"] for st in sts)
         L = 16 * nc
-        tc(R("zi"), R("q1", 0, 16))
-        ts(R("zm"), R("zi"), 4095, None, AND)
-        tt(R("zq"), R("zm"), R("zm"), MUL)
+        first = len(ops)
+        for q in range(16):
+            mm(R("q1", 0, nc), R("wz", 15 - q, 143 - q), R("b", q, L, 16), q == 0, q == 15)
+        zi, zm, zq, zh, zg = (R(x, 0, nc) for x in ("zi", "zm", "zq", "zh", "zg"))
+        tc(zi, R("q1", 0, nc))
+        ts(zm, zi, 4095, None, AND)
+        tt(zq, zm, zm, MUL)
         if t:
-            ts(R("zi"), R("zq"), float(97 * 32 * t), None, ADD)
-        ts(R("zh"), R("zi" if t else "zq"), 5, 4095, SHR, AND)
-        ts(R("zg"), R("zh"), float(S), float(S), LT, MUL)
-        tt(R("dT"), R("zh"), R("zg"), ADD)
-        for k in (0, 1):
-            tt(R("dx", 128 * k, 128 * k + 128), R("dT", 8 * k, 8 * k + 8), R("mask", 0, 128), MUL, ind=R("rep", 0, 8))
-        for st in sts:
-            mm(R("q1", 16 + st["c0"], 16 + st["c0"] + st["nc"]), R("dx", 128 * st["h"], 128 * st["h"] + 128, rows=st["nl"]),
-               R("cm", 0, st["nc"], rows=st["nl"]), True, True)
-        ts(R("dl", 0, nc), R("q1", 16, 16 + nc), float(OWN - S), None, ADD)
-        act(R("a12", 0, nc), R("q1", 16, 16 + nc), IDEN, bias=float(OWN - S))
-        act(R("fd", 0, L), R("f", 0, OWN + S), IDEN, bias=col("r15"), ind=R("dl", 0, nc))
+            ts(zi, zq, float(97 * 32 * t), None, ADD)
+        ts(zh, zi if t else zq, 5, 4095, SHR, AND)
+        ts(zg, zh, float(S), float(-S), GE, MUL)
+        tt(R("dl", 0, nc), zh, zg, ADD)
+        for o in ops[first + 16:]:
+            o["early"] = ZEARLY
+        gcopy(R("dT", 0, nc), R("dl", 0, nc))
+        act(R("fd", 0, L), R("f", 0, S), IDEN, bias=col("r15"), ind=R("dl", 0, nc))
         act(R("uu", 0, L), R("pl"), COPY, ind=R("dl", 0, nc))
-        ts(R("fb", 16, 32), R("id1"), float(S), 8.0, GE, MUL)
         for st in sts:
-            h, nl, l0 = st["h"], st["nl"], st["l0"]
-            o = R("q1", 32 + 8 * h, 40 + 8 * h, rows=nl)
-            mm(o, R("b", l0, l0 + nl), R("wa", 8, 16), True, False)
-            for k in (0, 16):
-                mm(o, R("nid", 0, nl, rows=nl), R("fb", k + 8 * h, k + 8 * h + 8, rows=nl), False, False)
+            X, nl, l0 = st["X"], st["nl"], st["l0"]
+            o = R("k" + X, 128, 256, rows=nl)
+            mm(o, R("b", l0, l0 + nl), R("wk"), True, False)
+            mm(o, R("idb", 0, nl, rows=nl), R("mn", rows=nl), False, False)
             mm(o, R("fd", l0, l0 + nl), R("ws"), False, True)
-        act(R("da4", 0, L), R("ramp"), COPY, ind=R("dl", 0, nc))
-        tc(R("da", 0, L), R("da4", 0, L))
+            act(R("tx" + X, rows=nl), o, IDEN, bias=float(S - 1))
+        act(R("da", 0, L), R("ramp"), COPY, ind=R("dl", 0, nc))
         bp = "bp" + F
         mm(R(bp, 0, L), R("idb"), R("uu", 0, L), True, False)
         mm(R(bp, 0, L), R("idb"), R("b", 0, L), False, False)
         mm(R(bp, 0, L), R("ones", rows=1), R("mhalf", 0, L, rows=1), False, True)
         act(R("uv", 0, L), R(bp, 0, L), IDEN, bias=MAGIC, scale=0.5)
         act(R("val", 0, L), R("uv", 0, L), IDEN, bias=col("vb%d" % t), scale=col("rl"))
-        act(R("val", L, 2 * L), R("b", 0, L), IDEN, bias=col("neg"), scale=col("rl"))
+        at = L + 16 * (nc % 2)
+        act(R("val", at, at + L), R("b", 0, L), IDEN, bias=col("neg"), scale=col("rl"))
 
     def rivals(st, sts, F):
         X, h, nl, nc, c0 = st["X"], st["h"], st["nl"], st["nc"], st["c0"]
         L = sum(x["nl"] for x in sts)
         rows = max(x["nl"] for x in sts)
-        tt(R("cand", 8 * h, 8 * h + 8, rows=nl), R("sc" + X, 15, 128, 16, rows=nl), R("q1", 32 + 8 * h, 40 + 8 * h, rows=nl), LE)
-        tt(R("x1", 128 * h, 128 * h + 128), R("cand", 8 * h, 8 * h + 8), R("dx", 128 * h, 128 * h + 128), MUL, ind=R("rep", 0, 8))
-        mm(R("a2" + F, 136 + c0, 136 + c0 + nc), R("x1", 128 * h, 128 * h + 128, rows=nl), R("cm", 0, nc, rows=nl), True, True)
-        if X == F:
-            act(R("nco", 0, nc), R("a2" + F, 136 + c0, 136 + c0 + nc), IDEN, bias=float(S + 2048), scale=-1.0)
+        nx, off = R("nx" + X, rows=nl), float(2048 + 15 * 8192)
+        mm(R("k" + X, 0, nc), R("idf"), R("dT", c0, c0 + nc), True, False)
+        tt(R("nx" + X), R("vi", 8 * h, 8 * h + 8), R("tx" + X), GT, ind=R("rep", 0, 8))
+        mm(R("k" + X, 0, nc), nx, R("cm8", 0, nc, rows=nl), False, True)
+        mm(R("q2", 128 * h, 128 * h + 128, rows=rows), R("hug", 0, rows, rows=nl), nx, X == F, False)
+        scols = SCOLS[X != F]
+        if scols:
+            act(R("nco", 0, nc), R("k" + X, 0, nc), IDEN, bias=off, scale=-1.0)
         for c in range(c0, c0 + nc):
             same = R("e3", 256 * c + 16 * c, 256 * c + L)
-            if X == F and c >= c0 + nc - SCOLS:
+            if c >= c0 + nc - scols:
                 far = R("far", 256 * (c % 2) + 16 * c, 256 * (c % 2) + L)
-                act(far, R("da4", 16 * c, L), ABS, bias=R("nco", c - c0, c - c0 + 1))
+                act(far, R("da", 16 * c, L), ABS, bias=R("nco", c - c0, c - c0 + 1))
                 act(same, far, RELU, bias=1.0, scale=-1.0)
             else:
-                ts(same, R("da", 16 * c, L), float(S + 2048), R("a2" + F, 136 + c, 137 + c), ADD, EQ)
+                ts(same, R("da", 16 * c, L), off, R("k" + X, c - c0, c - c0 + 1), ADD, EQ)
             for o in sts[h:]:
-                w = R("ww", 8 * (c - c0), 8 * (c - c0) + 8) if o is st else R("ww", 64, 72)
-                mm(R("q2", 8 * o["h"], 8 * o["h"] + 8, rows=rows), R("e3", 256 * c + o["l0"], 256 * c + o["l0"] + rows), w,
-                   X == F and c == c0 and o is st, X != F and c == c0 + nc - 1 and o is sts[-1])
+                w = R("ww", 128 * (c - c0), 128 * (c - c0) + 128) if o is st else R("ww", 1024, 1152)
+                mm(R("q2", 128 * o["h"], 128 * o["h"] + 128, rows=rows), R("e3", 256 * c + o["l0"], 256 * c + o["l0"] + rows), w,
+                   False, X != F and c == c0 + nc - 1 and o is sts[-1])
 
     def moves(sts):
         nc = sum(st["nc"] for st in sts)
-        mm(R("q1", 64, 64 + 2 * nc), R("idf"), R("base", 0, 2 * nc), True, False)
-        ts(R("first"), R("q2", 0, 16), col("thr"), None, LT)
-        tt(R("x2"), R("first"), R("x1"), MUL, ind=R("rep", 0, 16))
+        rows = max(x["nl"] for x in sts)
+        w = 2 * nc + nc % 2
+        mm(R("q1", 64, 64 + w), R("idf"), R("base2" if nc % 2 == 0 else "base", 0, w), True, False)
+        ts(R("x2", rows=rows), R("q2", 0, 256, rows=rows), R("cols", COL["thr"], COL["thr"] + 1, rows=rows), None, GE)
         for st in sts:
-            for k in (0, nc):
+            for k in (0, nc + nc % 2):
                 o = 64 + k + st["c0"]
-                mm(R("q1", o, o + st["nc"]), R("x2", 128 * st["h"], 128 * st["h"] + 128, rows=st["nl"]), R("cm2", 0, st["nc"], rows=st["nl"]), False,
-                   st["h"] == 1 and k == nc)
-        tt(R("of", 0, 2 * nc), R("a12", 0, 2 * nc), R("q1", 64, 64 + 2 * nc), MIN)
-        tc(R("ofl", 0, 2 * nc), R("of", 0, 2 * nc))
-        tc(R("f", 0, OWN + S), R("val", 0, 32 * nc), oind=R("ofl", 0, 2 * nc))
+                mm(R("q1", o, o + st["nc"]), R("x2", 128 * st["h"], 128 * st["h"] + 128, rows=st["nl"]), R("cm8", 0, st["nc"], rows=st["nl"]), False,
+                   st["h"] == 1 and k > 0)
+        tt(R("ofl", 0, w), R("dl", 0, w), R("q1", 64, 64 + w), MAX)
+        tc(R("f"), R("val", 0, 16 * w), oind=R("ofl", 0, w))
 
     def requests(sts, F):
         ts(R("ebi"), R("id0"), 1.0 / G, 1.0 - (S + (G - 1) / 2) / G, MUL, ADD)
-        tt(R("eb"), R("ebi"), R("fb", 0, 16), ADD)
         ts(R("idm"), R("id0"), float(1 - S), None, ADD)
-        tt(R("on"), R("eb"), R("ec"), EQ, ind=R("rep8"))
+        tt(R("on"), R("ebi"), R("ec"), EQ, ind=R("rep8"))
         A, B = sts
         bp = "bp" + F
         mm(R(bp, 256, 320, rows=A["nl"]), R("tril", 0, A["nl"], rows=A["nl"]), R("on", 0, 64, rows=A["nl"]), True, True)
@@ -699,8 +742,8 @@ def rank_program(g, core, T, topo):
             tt(R("mh", 128 * k, 128 * k + 128), R("qs"), R("jm1", 0, 128), EQ, ind=R("rep87", 8 * k, 8 * k + 8))
         for st in sts:
             nl, h = st["nl"], st["h"]
-            mm(R("a1" + F, 0, 64), R("mh", 128 * h, 128 * h + 128, rows=nl), R("ek", 64 * h, 64 * h + 64, rows=nl), h == 0, h == 1)
-        act(R("rq"), R("a1" + F, 0, 64), COPY)
+            mm(RN("s" + F, 0, ALL16, (0, 4)), R("mh", 128 * h, 128 * h + 128, rows=nl), R("ek", 64 * h, 64 * h + 64, rows=nl), h == 0, h == 1)
+        act(R("rq"), RN("s" + F, 0, ALL16, (0, 4)), COPY)
         tt(R("gg", G, 16 * BW, BW), R("rq"), R("ce"), SUB, ind=R("gl", 0, 1))
 
     for o in ops:

@@ -3,8 +3,9 @@ from concourse.mybir import dt, AluOpType, AxisListType, ActivationFunctionType
 
 ADD, SUB, MUL, MAX, MIN = AluOpType.add, AluOpType.subtract, AluOpType.mult, AluOpType.max, AluOpType.min
 GE, GT, LE, LT, EQ = AluOpType.is_ge, AluOpType.is_gt, AluOpType.is_le, AluOpType.is_lt, AluOpType.is_equal
+NE = AluOpType.not_equal
 SHR, AND = AluOpType.arith_shift_right, AluOpType.bitwise_and
-ABS = ActivationFunctionType.Abs
+SIGN = ActivationFunctionType.Sign
 IDEN, COPY, RELU, EXP = ActivationFunctionType.Identity, ActivationFunctionType.Copy, ActivationFunctionType.Relu, ActivationFunctionType.Exp
 
 N, S, G, CAP, WN, M, RO, H, T0 = 8, 3328, 112, 16, 144, 512, 3, 4, 192
@@ -21,10 +22,11 @@ NC = NV // RR
 MAGIC = 12582912.0
 PEN = float(2 ** 26)
 TOP = 14 * 2 ** 20
-HUGE = float(2 ** 95)
-DECAY = 1.04
+RIVAL = 32768.0
+LISTS = (((0, 4), (14, 8)), ((8, 16), (0, 24)))
 CHUNKS = {128: (32, 32, 32, 32), 80: (32, 32, 16), 64: (32, 32)}
-PARTS = {128: ((0, 64), (64, 96), (96, 128)), 80: ((0, 32), (32, 64), (64, 80)), 64: ((0, 32), (32, 64))}
+PARTS = {128: ((0, 32), (32, 64), (64, 96), (96, 128)), 80: ((0, 32), (32, 64), (64, 80)), 64: ((0, 32), (32, 64))}
+APARTS = PARTS
 ZEARLY = 0.0
 OPENING = {128: (32, 32, 32, 32), 64: (32, 32)}
 
@@ -33,52 +35,76 @@ for _n, _w, _t in (
         ("f", FW, "bfloat16"), ("nbw", NULL + 16, "int32"), ("pl", OWN + S, "bfloat16"), ("wti", 1, "int32"), ("wni", 27, "int32"), ("sdi", 49, "int32"),
         ("sdp", 56, "uint16"), ("sdf", 56, "float32"), ("sdw", 800, "float32"), ("sdx", 784, "float32"), ("wl", 30, "uint16"), ("rep", 50, "uint16"),
         ("wq", 432, "float32"), ("jf", 128, "float32"), ("jmf", 256, "float32"), ("jm1", 256, "float32"), ("j4", 128, "float32"), ("j7", 128, "float32"),
-        ("j16", 8, "float32"), ("ji", 64, "int32"), ("cols", 40, "float32"), ("idf", 128, "float32"), ("mask1", 144, "float32"), ("rep1", 10, "uint16"), ("idb", 128, "bfloat16"),
-        ("nid", 128, "bfloat16"), ("hug", 128, "bfloat16"), ("da4", 256, "float32"), ("far", 512, "float32"), ("nco", 8, "float32"), ("mask", 256, "float32"), ("rep8", 8, "uint16"), ("rep87", 16, "uint16"), ("gl", 2, "uint16"), ("blk", 128, "float32"),
-        ("wa", 16, "bfloat16"), ("wm", 16, "bfloat16"), ("wn", 8, "bfloat16"), ("wz", 144, "bfloat16"), ("wk", 128, "bfloat16"), ("ws", 128, "bfloat16"), ("mn", 128, "bfloat16"),
-        ("ww", 9 * 128, "bfloat16"), ("wwf", 8, "float32"),
-        ("cm8", 8, "bfloat16"), ("rsa", 128, "float32"), ("rs8", 128, "float32"), ("tril", 128, "bfloat16"), ("ones", 128, "bfloat16"),
-        ("mhalf", 256, "bfloat16"), ("ec", 128, "float32"), ("onf", 128, "float32"), ("b", 256, "bfloat16"), ("xx", 288, "float32"), ("dx", 256, "float32"),
-        ("x2", 256, "bfloat16"), ("dl", 32, "uint16"), ("fd", 256, "bfloat16"), ("uu", 256, "bfloat16"),
+        ("j16", 8, "float32"), ("ji", 64, "int32"), ("cols", 40, "float32"), ("idf", 128, "float32"), ("mask1", 80, "float32"), ("rep1", 10, "uint16"), ("idb", 128, "bfloat16"),
+        ("nco", 16, "float32"), ("mask", 256, "float32"), ("rep8", 8, "uint16"), ("rep87", 16, "uint16"), ("gl", 2, "uint16"), ("blk", 128, "float32"),
+        ("wa", 16, "bfloat16"), ("wm", 16, "bfloat16"), ("wn", 8, "bfloat16"), ("wz", 144, "bfloat16"), ("wk", 128, "bfloat16"), ("ws", 128, "bfloat16"), ("mn", 64, "bfloat16"), ("rb", 16, "bfloat16"),
+        ("wall", 256, "bfloat16"), ("wtri", 256, "bfloat16"), ("idw", 128, "bfloat16"), ("own", 8, "bfloat16"),
+        ("cm8", 16, "bfloat16"), ("rsa", 128, "float32"), ("rs8", 128, "float32"), ("tril", 128, "bfloat16"), ("ones", 128, "bfloat16"),
+        ("mhalf", 256, "bfloat16"), ("ec", 128, "float32"), ("onf", 128, "float32"), ("b", 256, "bfloat16"), ("cm2", 16, "float32"),
+        ("dl", 32, "uint16"), ("fd", 256, "bfloat16"), ("uu", 256, "bfloat16"),
         ("uv", 256, "float32"), ("val", 512, "bfloat16"), ("ramp", OWN + S, "float32"), ("da", 256, "float16"), ("ofl", 32, "uint16"), ("on", 128, "bfloat16"),
-        ("qs", 128, "float32"), ("mh", 256, "float16"), ("ek", 128, "float16"), ("rq", 64, "float32"), ("gg", 16 * BW, "bfloat16"), ("ld0", 7 * BW, "bfloat16"),
+        ("qs", 128, "float16"), ("mh", 256, "float16"), ("mi", 256, "float16"), ("idh", 256, "float16"), ("jh", 256, "float16"), ("ek", 128, "float16"), ("rq", 64, "float32"), ("gg", 16 * BW, "bfloat16"), ("ld0", 7 * BW, "bfloat16"),
         ("ld1", 7 * BW, "bfloat16"), ("ld2", 7 * BW, "bfloat16"), ("rki", 8, "uint16"), ("rkj", 8, "uint16"), ("qa", 128, "float32"), ("qc", 128, "float32")):
     SCRATCH[_n] = ("sbuf", [128, _w], _t)
 for _x in "AB":
     for _n, _w, _t in (("l", 8, "uint16"), ("off", 128, "uint16"), ("a", 2048, "bfloat16"), ("m", 2048, "bfloat16"), ("cp", 128, "float32"),
-                       ("nf", 128, "bfloat16"), ("gf", 128, "bfloat16"), ("tx", 128, "float32"), ("nx", 128, "bfloat16")):
+                       ("nf", 128, "bfloat16"), ("nx", 144, "bfloat16"), ("ny", 136, "bfloat16"), ("xx", 168, "float32"), ("tx", 64, "float32")):
         SCRATCH[_n + _x] = ("sbuf", [128, _w], _t)
     SCRATCH["t" + _x] = ("sbuf", [128, 8, 18], "float32")
-    SCRATCH["s" + _x] = ("psum", [128, 8, 16, 4], "float32")
-SCRATCH["e3"] = ("sbuf", [128, 16 * 256], "bfloat16")
+for _n in ("e3", "e4"):
+    SCRATCH[_n] = ("sbuf", [128, 16, 256], "bfloat16")
+for _n in ("tb0", "tb1", "tb2"):
+    SCRATCH[_n] = ("sbuf", [128, 16, 18], "float32")
+for _n in ("q1", "q2"):
+    SCRATCH[_n] = ("psum", [128, 16, 32], "float32")
 SCRATCH["wb"] = ("sbuf", [128, 128], "bfloat16")
-SCRATCH["mc"] = ("sbuf", [128, 384], "bfloat16")
-SCRATCH["mt"] = ("sbuf", [128, 16], "bfloat16")
-for _n in ("kA", "kB", "bpA", "bpB", "q1", "q2"):
+SCRATCH["mc"] = ("sbuf", [128, 8, 18, 3], "bfloat16")
+for _n in ("kA", "kB", "bpA", "bpB"):
     SCRATCH[_n] = ("psum", [128, 512], "float32")
+for _n in ("sA", "sB"):
+    SCRATCH[_n] = ("psum", [128, 9, 18, 3], "float32")
 PSUMS = [k for k in SCRATCH if SCRATCH[k][0] == "psum"]
 ALIAS = {}
 for _buf, _t, _names in (
-        ("tf", "float32", (("dT", 16), ("idm", 16), ("ce", 16), ("c112", 8), ("cm", 8), ("base", 32), ("base2", 32), ("wf", 32))),
+        ("tf", "float32", (("dT", 16), ("idm", 16), ("ce", 16), ("c112", 8), ("cm", 8), ("rr", 32), ("rs", 32), ("wf", 32))),
         ("ti", "int32", (("vi", 16), ("id0", 16), ("id1", 16), ("zi", 16), ("zm", 16), ("zq", 16), ("zh", 16), ("zg", 16), ("ebi", 16), ("ci", 8)))):
     _o = 0
     for _n, _w in _names:
         ALIAS[_n] = (_buf, _o, _w)
         _o += _w
     SCRATCH[_buf] = ("sbuf", [128, _o], _t)
-SEMAPHORES = ["sv", "ss", "sp", "sg", "go"] + ["d%d" % i for i in range(12)] + ["arr%d" % i for i in range(6)] + ["snd%d" % i for i in range(6)]
+SEMAPHORES = ["sv", "ss", "sp", "sg", "go"] + ["d%d" % i for i in range(12)] + ["arr%d" % i for i in range(9)] + ["snd%d" % i for i in range(9)]
 
 CYC, GATHER, SCATTER, PECYC, WAKE = 0.00083, 1.56, 3.8, 0.00042, 0.17
 TAIL, EARLY = 1.0, 1.5
-BV, MES = (True, False), (False, False)
+BV = ("", "")
+OFF2 = ("AB", "AB")
 ALL8, ALL16, HALVES = (0, 8), (0, 16), ((0, 8),)
 CLOSING = {128: (32, 32, 32, 16, 16), 80: (32, 32, 16)}
 SCOLS = (0, 0)
 PASSES = 1
 CPS = False
-ONV = {}
-NEAR = 2
-FILL = 0.12
+LATE = 99
+RAMP = {2: 5, 3: 9}
+ZPIN = (None, (4, 1.5))
+RULES = "bc"
+CK = (9, 9)
+ZAFTER = "bp"
+BEARLY = (1.0, 1.0)
+MHS = True
+FDE = 0.0
+LS = ("", "")
+GROUP = 1
+CALLS = (0, 4, 6)
+RVP = (True, True, False)
+NXP = (False, False)
+TENT = (True, False, True)
+GGV = ((1, 3, 5), (1, 3, 5), (1, 3, 5))
+ONV = ("A2A3A4", "A1A2A3B2B3B4")
+OFFS = ("", "")
+SHARED = {128: ((32, 32, 32, 16, 16), 4), 80: ((32, 32, 16), 2), 64: ((32, 16, 16), 2)}
+NEAR = 4
+FILL = 0.2
 
 
 def R(name, lo=None, hi=None, step=None, rows=128):
@@ -231,6 +257,7 @@ def rank_program(g, core, T, topo):
     ops = []
     hist = {}
     dman = [0]
+    chosen = [0]
     turn = []
 
     def ap(r):
@@ -240,7 +267,7 @@ def rank_program(g, core, T, topo):
             return T[name][(slice(p0, p1),) + r[5]]
         return T[name][p0:p1, lo:hi] if step is None else T[name][p0:p1, lo:hi:step]
 
-    def record(q, fn, reads, writes, occ, lat=WAKE, sem=None, inc=1, after=()):
+    def record(q, fn, reads, writes, occ, lat=WAKE, sem=None, inc=1, after=(), ind=0):
         me = len(ops)
         deps = {d: True for d in after}
         acc = [(r, False) for r in reads] + [(r, True) for r in writes]
@@ -261,7 +288,7 @@ def rank_program(g, core, T, topo):
             elif w and not bank and r[3] is None and r[4] == 128 and len(r) == 5:
                 lst = [x for x in lst if not (x[0] >= r[1] and x[1] <= r[2])]
             hist[name] = lst + [(r[1], r[2], w, q if sem is None else None, me, r[3], r[5:6])]
-        ops.append({"q": q, "fn": fn, "deps": deps, "occ": occ, "lat": lat, "sem": sem, "inc": inc, "early": 0.0, "lazy": False})
+        ops.append({"q": q, "fn": fn, "deps": deps, "occ": occ, "lat": lat, "sem": sem, "inc": inc, "early": 0.0, "lazy": False, "ind": ind})
         return me
 
     def emit_all():
@@ -317,16 +344,17 @@ def rank_program(g, core, T, topo):
     def ts(out, in0, s1, s2, o0, o1=None, ind=None):
         rd = [in0] + [x for x in (s1, s2, ind) if isinstance(x, tuple)]
         a = [ap(x) if isinstance(x, tuple) else x for x in (s1, s2)] + ([o0] if o1 is None else [o0, o1])
-        record("v", lambda: g.vector.tensor_scalar(ap(out), src(in0, ind), *a), rd, [out], vcost(out, [in0], ind))
+        record("v", lambda: g.vector.tensor_scalar(ap(out), src(in0, ind), *a), rd, [out], vcost(out, [in0], ind), ind=width(out) if ind else 0)
 
     def tt(out, in0, in1, op, ind=None):
         both = in0[0] not in PSUMS and in1[0] not in PSUMS
         record("v", lambda: g.vector.tensor_tensor(ap(out), src(in0, ind), ap(in1), op), [in0, in1] + ([ind] if ind else []), [out],
-               vcost(out, [("tf",)], ind, both))
+               vcost(out, [("tf",)], ind, both), ind=width(out) if ind else 0)
 
     def tc(out, in_, ind=None, oind=None):
         cost = 0.05 + width(in_) * SCATTER * CYC if oind else vcost(out, [in_], ind)
-        record("v", lambda: g.vector.tensor_copy(src(out, oind), src(in_, ind)), [in_] + [x for x in (ind, oind) if x], [out], cost)
+        record("v", lambda: g.vector.tensor_copy(src(out, oind), src(in_, ind)), [in_] + [x for x in (ind, oind) if x], [out], cost,
+               ind=width(out) if ind else 0)
 
     def scan(out, d0, d1, init, o0, o1):
         record("v", lambda: g.vector.tensor_tensor_scan(ap(out), ap(d0), ap(d1), init, o0, o1), [d0, d1], [out], vcost(out, [d0, d1], None))
@@ -338,6 +366,9 @@ def rank_program(g, core, T, topo):
         n = width(out)
         record("g", lambda: g.affine_select(ap(out), ap(in_), [[0, n]], GE, 0.0, 0, 0), [in_], [out], 0.17 + 2 * n * CYC)
 
+    def select(out, in_, pattern, op, other, base, cmul):
+        record("g", lambda: g.affine_select(ap(out), ap(in_), pattern, op, other, base, cmul), [in_], [out], 0.17 + 2 * width(out) * CYC)
+
     def ms(out, c):
         record("v", lambda: g.vector.memset(ap(out), c), [], [out], vcost(out, [], None))
 
@@ -345,11 +376,20 @@ def rank_program(g, core, T, topo):
         kw = {k: (ap(v) if isinstance(v, tuple) else v) for k, v in (("bias", bias), ("scale", scale)) if v is not None}
         rd = [in_] + [x for x in (ind, bias, scale) if isinstance(x, tuple)]
         cost = 0.065 + width(out) * GATHER * CYC if ind else 0.02 + max(64, width(out)) * CYC
-        record("s", lambda: g.scalar.activation(ap(out), src(in_, ind), func, **kw), rd, [out], cost + more)
+        record("s", lambda: g.scalar.activation(ap(out), src(in_, ind), func, **kw), rd, [out], cost + more, ind=width(out) if ind else 0)
 
     def mm(out, lhsT, rhs, start, stop):
         cost = max(min(64, width(lhsT)), width(rhs)) * (1 if narrow(lhsT) else 4) * PECYC
         record("p", lambda: g.tensor.matmul(ap(out), ap(lhsT), ap(rhs), start, stop), [lhsT, rhs], [out], cost)
+
+    def mms(calls):
+        if len(calls) > GROUP:
+            for k in range(0, len(calls), GROUP):
+                mms(calls[k:k + GROUP])
+            return
+        cost = sum(max(min(64, width(l)), width(r)) * (1 if narrow(l) else 4) * PECYC for _, l, r, _, _ in calls)
+        record("p", lambda: [g.tensor.matmul(ap(o), ap(l), ap(r), a, b) for o, l, r, a, b in calls][-1],
+               [x for c in calls for x in c[1:3]], [calls[0][0]], cost)
 
     def iota(out, pattern, base, cmul, flt=True):
         kw = {"allow_small_or_imprecise_dtypes": True} if flt else {}
@@ -370,8 +410,9 @@ def rank_program(g, core, T, topo):
     d2 = dma("y", T.f[:, OWN:OWN + hx], T.x0[:, 0:hx], [R("f", OWN, OWN + hx)], [], 3.0)
     last = {"y": d2, "s": d1}
     ops[d2]["deps"][d0] = False
-    for q, o, i, r, lat in (("s", T.wti[:], T.wt[:], R("wti"), 6.0), ("y", T.wni[:], T.wants[:], R("wni"), 6.0), ("y", T.pl[:, 0:M], T.pull[:], R("pl", 0, M), 6.5),
-                            ("s", T.nbw[:, hx:S], T.nb[:, hx:S], R("nbw", hx, S), 8.0), ("y", T.nbw[:, 0:hx], T.nb[:, 0:hx], R("nbw", 0, hx), 9.0)):
+    for q, o, i, r, lat in (("s", T.wti[:], T.wt[:], R("wti"), 6.0), ("y", T.wni[:], T.wants[:], R("wni"), 6.0),
+                            ("s", T.nbw[:, hx:S], T.nb[:, hx:S], R("nbw", hx, S), 8.0), ("y", T.nbw[:, 0:hx], T.nb[:, 0:hx], R("nbw", 0, hx), 9.0),
+                            ("y", T.pl[:, 0:M], T.pull[:], R("pl", 0, M), 9.5)):
         d = dma(q, o, i, [r], [], lat)
         ops[d]["deps"][last[q]] = False
         last[q] = d
@@ -383,25 +424,30 @@ def rank_program(g, core, T, topo):
     iota(R("ji"), [[1, 64]], 0, 0, False)
     iota(R("nbw", S, NULL + 1), [[1, NULL + 1 - S]], S, 0, False)
     iota(R("j7"), [[0, 16], [1, 8]], 0, 0)
-    iota(R("j16"), [[16, 8]], 0, 0)
     iota(R("c112"), [[G, 8]], 0, 0)
-    for lo in range(0, OWN + S, 256):
-        iota(R("ramp", lo, lo + 256), [[1, 256]], lo - OWN - 2048, 0)
-    ms(R("gg", 0, 7 * BW), 0.0)
+    ramp = []
+    for lo in range(0, S, 256):
+        iota(R("ramp", lo, lo + 256), [[1, 256]], lo - 2048, 0)
+        ramp.append(len(ops) - 1)
+
+    def fill(out, c):
+        act(out, R("jmf", 0, width(out), rows=out[4]), IDEN, scale=0.0, bias=c)
+
     for nm in ("id0", "id1", "vi"):
         ms(R(nm), 0)
     ms(R("dl"), 0)
-    for r in (R("txA"), R("txB"), R("bpA", 256, 384), R("val", WN, WN + 16), R("wz")):
-        ms(r, 0.0)
-    for c in range(1, 16):
-        ms(R("e3", 256 * c + (0 if c < 8 else 64 if c == 8 else 128), 256 * c + 16 * c), 0.0)
+    ms(R("bpA", 256, 384), 0.0)
+    for r in (R("xxA"), R("xxB"), R("nyA"), R("nyB"), R("txA"), R("txB"), R("val", 16 * 13, 16 * 14), R("wz"), R("gg", G + 1, 7 * BW, BW)):
+        fill(r, 0.0)
     ms(R("f", NULL, WIN), -1.0)
     ms(R("ones"), 1.0)
-    ms(R("mhalf"), -0.5)
+    fill(R("mhalf", rows=1), -0.5)
     ts(R("ci", 1, 2), R("ci", 0, 1), 15, None, AND)
     ts(R("ci", 2, 3), R("ci", 0, 1), 4, None, SHR)
     ts(R("ci", 3, 4), R("ci", 1, 2), 3, None, SHR)
-    for k, nm in enumerate(("p", "q", "g", "q8")):
+    ts(R("ci", 4, 5), R("ci", 0, 1), 15, 1, AND, SHR)
+    ts(R("ci", 5, 6), R("ci", 0, 1), 1, None, AND)
+    for k, nm in enumerate(("p", "q", "g", "q8", "q2", "q1")):
         tc(col(nm), R("ci", k, k + 1))
     for e in range(7):
         tc(R("sdp", 8 * e, 8 * e + 7), R("sdi", 7 * e, 7 * e + 7))
@@ -411,65 +457,69 @@ def rank_program(g, core, T, topo):
                       ("big", "rl", 2 * PEN), ("nbig", "rl", -2 * PEN)):
         ts(col(nm), col(of), float(c), None, MUL)
     for t in range(RO):
-        ts(col("vb%d" % t), col("r15"), float(T0 + t), col("mag"), MUL, ADD)
+        act(col("vb%d" % t), col("r15"), IDEN, scale=float(T0 + t), bias=col("mag"))
     ts(R("cm"), R("jf", 0, 8), col("g"), None, EQ)
     ts(R("idf"), R("jf"), col("p"), None, EQ)
     ts(R("blk"), R("j4"), col("g"), None, EQ)
     ts(R("mask"), R("jmf"), col("q"), None, EQ)
-    ts(R("rsa"), R("jmf", 0, 128), 0.0, None, GT)
-    ts(R("jm1"), R("jmf"), 1024.0, None, ADD)
+    act(R("rsa"), R("jmf", 0, 128), SIGN)
     tc(col("wt"), R("wti"))
     tt(col("wtl"), col("wt"), col("rl"), MUL)
     act(R("idb"), R("idf"), COPY)
-    act(R("hug"), R("idf"), COPY, scale=HUGE)
     act(R("wa", 0, 16, 2), R("cm"), COPY, scale=col("nbig"))
     act(R("wa", 1, 16, 2), R("cm"), COPY, scale=col("k17"))
     for k in (0, 1):
         act(R("wm", k, 16, 2), R("cm"), COPY, scale=col("big"))
     act(R("wb"), R("blk"), COPY, scale=col("nbig"))
-    ms(R("mc", rows=1), -PEN)
-    ts(R("mc", 2, 384, 3, rows=1), R("jmf", 0, 128, rows=1), -8192.0, -8192.0, MUL, ADD)
-    ms(R("mt", rows=3), 0.0)
+    ms(RN("mc", ALL8, (0, 18), (0, 3), rows=3), 0.0)
+    ms(RN("mc", ALL8, ALL16, (0, 2), rows=1), -PEN)
+    ms(RN("mc", ALL8, (16, 18), (0, 2), rows=1), PEN)
+    ts(RN("mc", ALL8, ALL16, 2, rows=1), R("jmf", 0, 128, rows=1), -8192.0, -8192.0, MUL, ADD)
     for k, c in enumerate((NULL % 4096, NULL - NULL % 4096, TOP)):
-        ms(R("mt", 1, 16, 2, rows=3 - k), float(c))
+        ms(RN("mc", ALL8, 17, 2, rows=3 - k), float(c))
     act(R("wn"), R("cm"), COPY, scale=col("full"))
     act(R("wk"), R("blk"), COPY, scale=col("k17"))
     act(R("ws"), R("blk"), COPY, scale=col("full"))
-    act(R("mn"), R("mask", 0, 128), IDEN, scale=PEN, bias=-PEN)
     act(R("wz", 15, 143, 16), R("cm"), COPY, scale=col("wtl"))
-    act(R("cm8"), R("cm"), COPY, scale=8192.0)
-    for k in range(1, 7):
-        hi = min(M * (k + 1), OWN + S)
-        act(R("pl", M * k, hi), R("pl", 0, hi - M * k), COPY)
-    ts(col("wq"), col("q"), -DECAY, 62.0, MUL, ADD)
-    ts(col("wp"), col("p"), -DECAY, 62.74, MUL, ADD)
-    act(R("wwf"), R("j16"), EXP, bias=col("wq"), scale=-DECAY, more=1.3)
-    act(col("thr"), col("wp"), EXP)
-    for c in range(8):
-        act(R("ww", 128 * c, 128 * c + 128), R("blk"), COPY, scale=R("wwf", c, c + 1))
-    act(R("ww", 1024, 1152), R("blk"), COPY, scale=HUGE)
-    ts(R("rs8"), R("j7"), 0.0, None, GT)
-    ts(R("ec"), R("j7"), -1.0, 7.0, MUL, ADD)
-    ts(R("onf"), R("j7"), 7.0, 50.0, EQ, MUL)
-    tt(R("ec"), R("ec"), R("onf"), ADD)
-    ts(R("onf"), R("jf"), col("p"), None, GT)
-    ts(R("qs"), R("idf"), 1024.0, None, MUL)
-    tt(R("tril"), R("onf"), R("qs"), ADD)
-    ts(R("ce"), R("jf", 0, 16), float(-G), float(6 * G), MUL, ADD)
-    ts(R("ce"), R("ce"), 0.0, None, MAX)
-    ts(col("g8"), col("g"), 8.0, None, MUL)
+    act(R("wall", 0, 128), R("blk"), COPY, scale=RIVAL)
+    select(R("onf"), R("wall", 0, 128), [[1, 128]], GT, 0.0, 0, -1)
+    select(R("wtri", 0, 128), R("onf"), [[1, 128]], NE, -RIVAL, 0, -1)
+    act(R("rs8"), R("j7"), SIGN)
+    act(R("ec"), R("j7"), IDEN, scale=-1.0, bias=7.0)
+    select(R("qc"), R("ones"), [[1, 128]], GT, 0.0, 0, -1)
+    select(R("tril"), R("qc"), [[1, 128]], NE, 1024.0, 0, -1)
+    fill(R("idh", 0, 128, rows=1), 1.0)
+    act(R("idh", 128, 256), R("idf"), COPY)
+    act(R("jh", rows=1), R("jmf", rows=1), IDEN, scale=-1.0, bias=-1024.0)
+    fill(col("half"), 0.5)
+    act(R("ce"), R("jf", 0, 16), RELU, scale=float(-G), bias=float(6 * G))
+    act(col("g8"), col("g"), COPY, scale=8.0)
     ts(R("gl", 0, 1), col("q"), 7.0, col("g8"), MIN, ADD)
-    ts(col("qb"), col("q"), float(WIN - 16 * 8192), None, ADD)
-    for nm in ("base", "base2"):
-        ts(R(nm), R("jf", 0, 32), 16.0, col("qb"), MUL, ADD)
-    ts(R("base", WN // 16, WN // 16 + 1), R("base2", WN // 16, WN // 16 + 1), float(16 * 8192), None, ADD)
+    act(col("qb"), col("q"), IDEN, bias=float(WIN))
+    act(R("rr"), R("jf", 0, 32), IDEN, scale=16.0, bias=col("qb"))
+
+    def aside(k, cuts):
+        act(RN("tb%d" % k, ALL16, (1, 17)), R("mask"), IDEN, scale=RIVAL / 2 - 2 ** 22, bias=float(2 ** 22))
+        if RVP[k]:
+            fill(RN("tb%d" % k, ALL16, 0), 0.0)
+            fill(RN("tb%d" % k, ALL16, 17), 0.0)
+        for h in (0, 1):
+            for j, at in zip((17, 0), LISTS[k > 0][h]):
+                if not RVP[k]:
+                    act(RN("tb%d" % k, cuts[h:h + 2], j), R("jf", at, at + cuts[h + 1] - cuts[h]), IDEN, scale=16.0, bias=col("qb"))
+
+    aside(0, (0, 4, 9))
     tc(R("rep"), R("ji", 0, 50))
-    tc(R("rep1", 0, 8), R("ji", 0, 8))
-    ts(R("rep1", 8, 9), col("q"), 7.0, None, MIN)
-    act(R("mask1", 0, 128), R("mask", 0, 128), COPY)
-    ms(R("mask1", 128, 144), 1.0)
+    ts(R("rep1", 0, 4), R("jf", 0, 4), 2.0, col("q8"), MUL, ADD)
+    ts(R("rep1", 4, 5), col("q"), 7.0, None, MIN)
+    ts(R("mask1", 0, 64), R("j7", 0, 64), col("q2"), None, EQ)
+    ms(R("mask1", 64, 80), 1.0)
+    for k in (0, 1):
+        ts(col("odd%d" % k), col("q1"), float(k), None, EQ)
+        ts(R("cm2", 8 * k, 8 * k + 8), R("cm"), col("odd%d" % k), None, MUL)
+    act(R("mn"), R("mask1", 0, 64), IDEN, scale=PEN, bias=-PEN)
+    act(R("cm8"), R("cm2"), COPY, scale=8192.0)
     ts(R("rep8"), R("jf", 0, 8), 2.0, col("q8"), MUL, ADD)
-    ts(R("rep87"), R("jf", 0, 16), 8.0, 7.0, MUL, ADD)
     tc(R("wl", 0, 9), R("wni", 0, 9))
     ms(R("wf"), 0.0)
     tc(R("wf", 0, 27), R("wni"))
@@ -478,6 +528,7 @@ def rank_program(g, core, T, topo):
     def later_tables():
         first, moved = len(ops), hist["ofl"][-1][4]
         for t in (1, 2):
+            aside(t, (0, 8, 16))
             tc(R("wl", 10 * t + 1, 10 * t + 10), R("wni", 9 * t, 9 * t + 9))
         for lo, hi in ((10, 18), (18, 27)):
             tt(R("wq", 16 * lo, 16 * hi), R("wf"), R("mask", 0, 16 * (hi - lo)), MUL, ind=R("rep", lo, hi))
@@ -492,12 +543,15 @@ def rank_program(g, core, T, topo):
             act(R("sdw", 1 + lo, 1 + hi), R("bpB", 0, hi - lo), COPY)
         for o in ops[first:]:
             o["lazy"] = True
-            if o["q"] == "v":
+            if o["q"] in "vs":
                 o["deps"].setdefault(moved, False)
 
     def calls_of(r):
         off = [e for e in range(1, N) if topo.chip(T.cores[(r + e) % N]) != topo.chip(T.cores[r])]
-        return [off[0:4], off[4:] + [e for e in range(1, N) if e not in off]]
+        near = [e for e in range(1, N) if e not in off]
+        here = topo.chip(T.cores[r])
+        off.sort(key=lambda e: (topo.mates(here, topo.chip(T.cores[(r + e) % N])), topo.same_plane(here, topo.chip(T.cores[(r + e) % N]))))
+        return [off[a:b] + (near if b == len(off) else []) for a, b in zip(CALLS, CALLS[1:])]
 
     def engines_of(r, es):
         me = T.cores[r]
@@ -511,7 +565,7 @@ def rank_program(g, core, T, topo):
             n = 1
             while n * 2 <= room:
                 n *= 2
-            out[x] = free[0:n]
+            out[x] = free[0:n] if x in away else free[0:2 * n:2]
             used = used + out[x]
         return out
 
@@ -519,20 +573,22 @@ def rank_program(g, core, T, topo):
         calls = calls_of(rank)
         for k, e in enumerate(sum(calls, [])):
             o, w, i = R("gg", (e - 1) * BW, (e - 1) * BW + G), R("f", OWN, OWN + S), R("sdp", 8 * (e - 1), 8 * e - 1)
-            if k % 2:
+            if k in GGV[t]:
                 tc(o, w, ind=i)
             else:
                 act(o, w, COPY, ind=i)
         sent = []
+        bw = G + 2 if t else G
         for k, es in enumerate(calls):
             eng = engines_of(rank, es)
             trs = []
             for e in es:
                 rid, pid, se = topo.addr(T.cores[(rank + e) % N])
                 there = calls_of(rank)
-                trs.append(RemoteDMATransfer(dst_ids=[DstId(rid=rid, pnc=pid)], dma_engine_mask=sum(1 << x for x in eng[e]), remote_sem=T.sem["arr%d" % (2 * t + k)],
-                                             srcs=[T.gg[:, (e - 1) * BW:e * BW]], dsts=[T["ld%d" % t][:, (7 - e) * BW:(8 - e) * BW]]))
-            sem = "snd%d" % (2 * t + k)
+                trs.append(RemoteDMATransfer(dst_ids=[DstId(rid=rid, pnc=pid)], dma_engine_mask=sum(1 << x for x in eng[e]), remote_sem=T.sem["arr%d" % (3 * t + k)],
+                                             srcs=[T.gg[:, (e - 1) * BW:(e - 1) * BW + bw]],
+                                             dsts=[T["ld%d" % t][:, (7 - e) * BW:(7 - e) * BW + bw] if t else T.f[:, S + (e - 1) * G:S + e * G]]))
+            sem = "snd%d" % (3 * t + k)
             sent.append(record("g", lambda trs=trs, sem=sem: g.remote_dma_fused(trs, local_sem=T.sem[sem]), [R("gg", (e - 1) * BW, e * BW) for e in es], [],
                                2.5 if t + k == 0 else 0.6, 4.0, sem, sum(len(x) for x in eng.values()), ()))
         for k in range(1, len(calls)):
@@ -540,8 +596,9 @@ def rank_program(g, core, T, topo):
         for k in range(len(calls)):
             es = [e for e in range(1, N) if e in calls_of((rank - e) % N)[k]]
             n = sum(len(engines_of((rank - e) % N, calls_of((rank - e) % N)[k])[e]) for e in es)
-            record("r", None, [], [R("ld%d" % t, (7 - e) * BW, (8 - e) * BW) for e in es], 0.0, 0.0, "arr%d" % (2 * t + k), n, [sent[k]])
-            for j, e in enumerate(es):
+            land = [R("ld%d" % t, (7 - e) * BW, (8 - e) * BW) if t else R("f", S + (e - 1) * G, S + e * G) for e in es]
+            record("r", None, [], land, 0.0, 0.0, "arr%d" % (3 * t + k), n, [sent[k]])
+            for j, e in enumerate(es if t else []):
                 o, i = R("f", OWN + S + (e - 1) * G, OWN + S + e * G), R("ld%d" % t, (7 - e) * BW, (7 - e) * BW + G)
                 if j % 2:
                     act(o, i, COPY)
@@ -552,7 +609,8 @@ def rank_program(g, core, T, topo):
         h = 0 if X == "A" else 1
         nc = (4, 5)[h] if t == 0 else 8
         c0 = 0 if h == 0 else (4 if t == 0 else 8)
-        return {"X": X, "h": h, "nl": 16 * nc, "nc": nc, "c0": c0, "l0": 16 * c0, "t": t, "own": t == 0 or h == 1, "opens": (t == 0) == (h == 0)}
+        s, d = LISTS[t > 0][h]
+        return {"X": X, "h": h, "s": s, "d": d, "nl": 16 * nc, "nc": nc, "c0": c0, "l0": 16 * c0, "t": t, "own": t == 0 or h == 1, "opens": (t == 0) == (h == 0)}
 
     def start(st):
         t, h, nl = st["t"], st["h"], st["nl"]
@@ -574,15 +632,19 @@ def rank_program(g, core, T, topo):
     def look(st, hop, ncs):
         X, h, nl, l0, nc = st["X"], st["h"], st["nl"], st["l0"], st["nc"]
         sq, hh = "s" + X, (8 * h, 8 * h + 8)
-        win, bb, me = R("f", 0, WIN), R("b", l0, l0 + nl), R("k" + X, 256, 272, 2, rows=nl)
+        gs = (h, 8 + h)
+        win, bb, me = R("f", 0, WIN), R("b", l0, l0 + nl), RN(sq, gs, 16, 2, rows=nl)
         ls = st["list"]
         named = hop < H or st["t"] < RO - 1
         wide = 18 if hop == 1 else 17
         first = len(ops)
-        for c0, c1 in (((0, 2), (2, nc)) if hop > 1 else ((0, nc),)):
-            tc(R("off" + X, 16 * c0, 16 * c1), R("nbw"), ind=R(ls[0], ls[1] + c0, ls[1] + c1))
+        for c0, c1 in (((0, 2), (2, nc)) if hop > 1 and X in OFF2[st["t"] > 0] else ((0, nc),)):
+            if c0 and X + str(hop) in OFFS[st["t"] > 0]:
+                act(R("off" + X, 16 * c0, 16 * c1), R("nbw"), COPY, ind=R(ls[0], ls[1] + c0, ls[1] + c1))
+            else:
+                tc(R("off" + X, 16 * c0, 16 * c1), R("nbw"), ind=R(ls[0], ls[1] + c0, ls[1] + c1))
             ops[-1]["early"] = TAIL
-        if st["own"] and hop == 1 or BV[st["t"] > 0]:
+        if st["own"] and hop == 1 or X + str(hop) in BV[st["t"] > 0]:
             ts(bb, R("f", OWN, OWN + S) if hop == 1 and st["own"] else win, col("mid"), None, ADD, ind=st["list"])
         else:
             act(bb, win, IDEN, bias=col("mid"), ind=st["list"])
@@ -591,35 +653,34 @@ def rank_program(g, core, T, topo):
             act(R("cp" + X, 0, nl), R("off" + X, 0, nl), COPY)
         elif named:
             gcopy(R("cp" + X, 0, nl), R("off" + X, 0, nl))
+            st["cp"] = len(ops) - 1
         if hop == 1:
             ts(R("nf" + X, 0, nl), bb, -MID - 0.5, None, GE)
         if hop == 1 and st["own"]:
             for o in ops[first:]:
                 o["early"], o["lazy"] = 0.0, True
-        for j in range(RR):
-            mm(R("bp" + X, j, RR * nl, RR), R("idb"), bb, True, True)
-        mm(RN(sq, ALL8, ALL16, (0, 3), rows=nl), R("ones", 0, nl, rows=1), R("mc", rows=1), True, False)
-        mm(RN(sq, ALL8, ALL16, 0, rows=nl), bb, R("wb"), False, False)
+        mms([(R("bp" + X, j, RR * nl, RR), R("idb"), bb, True, True) for j in range(RR)])
+        st["bp"] = len(ops) - 1
+        mm(RN(sq, gs, (0, wide), (0, 3), rows=nl), R("ones", 0, nl, rows=3), RN("mc", ALL8, (0, wide), (0, 3), rows=3), True, False)
+        mm(RN(sq, gs, ALL16, 0, rows=nl), bb, R("wb"), False, False)
         if hop == 1:
-            mm(R("k" + X, 256, 272, rows=nl), R("ones", 0, nl, rows=3), R("mt", rows=3), True, False)
             mm(me, st["diag"], R("cm"), False, False)
-            mm(R("k" + X, 257, 272, 2, rows=nl), R("nf" + X, 0, nl), R("wn"), False, False)
+            mm(RN(sq, gs, 17, 2, rows=nl), R("nf" + X, 0, nl), R("wn"), False, False)
         else:
-            mm(me, R("idf", 0, nl, rows=nl), R("xx", 144 * h + 128, 144 * h + 136, rows=nl), True, False)
-        mm(me, bb, R("wa", 1, 16, 2), False, True)
-        own = (RN("t" + X, ALL8, (16, 18), rows=nl), R("k" + X, 256, 272, rows=nl)) if hop == 1 else (RN("t" + X, ALL8, 16, rows=nl), me)
-        if MES[st["t"] > 0]:
-            act(own[0], own[1], COPY)
-        else:
-            tc(own[0], own[1])
+            mm(me, R("idf", 0, nl, rows=nl), R("xx" + X, 129, 145, 2, rows=nl), False, False)
+        mm(me, bb, R("wa", 1, 16, 2), False, False)
         if named:
-            mm(RN(sq, ALL8, ALL16, 2, rows=nl), R("cp" + X, 0, nl), R("idf"), False, False)
+            mm(RN(sq, gs, ALL16, 2, rows=nl), R("cp" + X, 0, nl), R("idf"), False, False)
         lo = 0
+        st["max"] = []
         opening = hop == 1 and st["opens"]
         closing = hop == H and not st["opens"]
-        for k, w in enumerate((OPENING if opening else CLOSING if closing else CHUNKS)[nl]):
+        chunks, onv = (OPENING if opening else CLOSING if closing else CHUNKS)[nl], None
+        if X + str(hop) in ONV[st["t"] > 0] and not opening:
+            chunks, onv = SHARED[nl]
+        for k, w in enumerate(chunks):
             hi = lo + w
-            if k == (0 if opening else ONV.get(nl)):
+            if k == (0 if opening else onv):
                 ts(R("a" + X, 16 * lo, 16 * hi), win, col("mid"), None, ADD, ind=R("off" + X, lo, hi))
             else:
                 act(R("a" + X, 16 * lo, 16 * hi), win, IDEN, bias=col("mid"), ind=R("off" + X, lo, hi))
@@ -628,104 +689,185 @@ def rank_program(g, core, T, topo):
                 turn.append(len(ops) - 1)
             for n in range(NC):
                 tt(R("m" + X, RR * (n * nl + lo), RR * (n * nl + hi)), R("a" + X, 16 * lo + n, 16 * hi, NC), R("bp" + X, RR * lo, RR * hi), MAX)
+                st["max"].append(len(ops) - 1)
+                if closing and k == CK[st["t"] > 0] and n == 0:
+                    ops[-1]["deps"].setdefault(chosen[0], False)
             lo = hi
+        sums = len(ops)
         for p0, p1 in PARTS[nl]:
-            for n in range(NV):
-                mm(RN(sq, ALL8, n, (1, 3), rows=(p0, p1)), R("a" + X, 16 * p0 + n, 16 * p1, 16), R("wa"), False, False)
+            for a0, a1 in APARTS[nl]:
+                if p0 < a1 <= p1:
+                    mms([(RN(sq, gs, n, (1, 3), rows=(a0, a1)), R("a" + X, 16 * a0 + n, 16 * a1, 16), R("wa"), False, False) for n in range(NV)])
             for n in range(NC):
-                for j in range(RR):
-                    mm(RN(sq, ALL8, n + NC * j, (0, 2), rows=(p0, p1)), R("m" + X, RR * (n * nl + p0) + j, RR * (n * nl + p1), RR), R("wm"), False,
-                       n == NC - 1 and j == RR - 1)
+                mms([(RN(sq, gs, n + NC * j, (0, 2), rows=(p0, p1)), R("m" + X, RR * (n * nl + p0) + j, RR * (n * nl + p1), RR), R("wm"), False,
+                      n == NC - 1 and j == RR - 1) for j in range(RR)])
         chain = len(ops)
+        st["sums"] = chain - 1 if st["opens"] else st["bp"]
         for g0, g1 in HALVES:
-            red(RN("t" + X, (g0, g1), ALL16, rows=nl), RN(sq, (g0, g1), ALL16, (0, 3), rows=nl), MIN)
+            red(RN("t" + X, (g0, g1), (0, wide), rows=nl), RN(sq, (g0 + h, g1 + h), (0, wide), (0, 3), rows=nl), MIN)
         red(R("vi", hh[0], hh[1], rows=nl), RN("t" + X, ALL8, (0, wide), rows=nl), MAX)
+        chosen[0] = len(ops) - 1
         if named:
             ts(R("id%d" % (hop % 2), hh[0], hh[1], rows=nl), R("vi", hh[0], hh[1], rows=nl), 8191, None, AND)
         if hop < H:
-            tt(R("xx", 144 * h, 144 * h + 144), R("id%d" % (hop % 2), hh[0], hh[1]), R("mask1"), MUL, ind=R("rep1", 0, 9))
-            mm(R("k" + X, 0, nc), R("xx", 144 * h, 144 * h + 128, rows=nl), R("cm", 0, nc, rows=nl), True, True)
-            at = ncs + ncs % 2 + st["c0"]
-            st["list"] = R("l" + X, 0, nc) if hop < H - 1 else R("dl", at, at + nc)
-            tc(st["list"], R("k" + X, 0, nc))
+            tt(R("xx" + X, 1, 161, 2), R("id%d" % (hop % 2), hh[0], hh[1]), R("mask1"), MUL, ind=R("rep1", 0, 5))
+            mms([(R("k" + X, 0, nc), R("xx" + X, 1 - k, 129 - k, rows=nl), R("cm2", 8 * k, 8 * k + nc, rows=nl), k == 0, k == 1) for k in (0, 1)])
+            st["list"] = R("l" + X, 0, nc) if hop < H - 1 else R("dl", st["s"], st["s"] + nc)
+            if X + str(hop) in LS[st["t"] > 0]:
+                act(st["list"], R("k" + X, 0, nc), COPY)
+            else:
+                tc(st["list"], R("k" + X, 0, nc))
         for o in ops[chain:]:
             o["early"] = TAIL
+        if hop == H and st["opens"]:
+            for o in ops[sums:]:
+                o["early"] = BEARLY[st["t"] > 0]
 
     def places(t, sts, F):
         nc = sum(st["nc"] for st in sts)
         L = 16 * nc
         first = len(ops)
-        for q in range(16):
-            mm(R("q1", 0, nc), R("wz", 15 - q, 143 - q), R("b", q, L, 16), q == 0, q == 15)
+        for q0 in range(0, 16, 4):
+            mms([(R("k" + F, 320, 320 + nc), R("wz", 15 - q, 143 - q), R("b", q, L, 16), q == 0, q == 15) for q in range(q0, q0 + 4)])
+        for st in sts:
+            ops[first]["deps"].setdefault(st[ZAFTER], False)
         zi, zm, zq, zh, zg = (R(x, 0, nc) for x in ("zi", "zm", "zq", "zh", "zg"))
-        tc(zi, R("q1", 0, nc))
+        d0 = sts[0]["d"]
+        dl = R("dl", d0, d0 + nc)
+        tc(zi, R("k" + F, 320, 320 + nc))
         ts(zm, zi, 4095, None, AND)
         tt(zq, zm, zm, MUL)
         if t:
             ts(zi, zq, float(97 * 32 * t), None, ADD)
         ts(zh, zi if t else zq, 5, 4095, SHR, AND)
         ts(zg, zh, float(S), float(-S), GE, MUL)
-        tt(R("dl", 0, nc), zh, zg, ADD)
-        for o in ops[first + 16:]:
+        tt(dl, zh, zg, ADD)
+        for o in ops[first:]:
             o["early"] = ZEARLY
-        gcopy(R("dT", 0, nc), R("dl", 0, nc))
-        act(R("fd", 0, L), R("f", 0, S), IDEN, bias=col("r15"), ind=R("dl", 0, nc))
-        act(R("uu", 0, L), R("pl"), COPY, ind=R("dl", 0, nc))
+        if ZPIN[t > 0]:
+            zs = [i for i in range(first, len(ops)) if ops[i]["q"] == "v"]
+            mx = [st["max"] for st in sts if st["X"] != F][0]
+            for k, i in enumerate(zs):
+                ops[mx[min(len(mx) - 1, ZPIN[t > 0][0] + int(k * ZPIN[t > 0][1]))]]["deps"].setdefault(i, False)
+        gcopy(R("dT", 0, nc), dl)
+        act(R("fd", 0, L), R("f", 0, S), IDEN, bias=col("r15"), ind=dl)
+        ops[-1]["early"] = FDE
+        act(R("uu", 0, L), R("pl"), COPY, ind=dl)
+        uu = len(ops) - 1
         for st in sts:
             X, nl, l0 = st["X"], st["nl"], st["l0"]
-            o = R("k" + X, 128, 256, rows=nl)
-            mm(o, R("b", l0, l0 + nl), R("wk"), True, False)
-            mm(o, R("idb", 0, nl, rows=nl), R("mn", rows=nl), False, False)
-            mm(o, R("fd", l0, l0 + nl), R("ws"), False, True)
-            act(R("tx" + X, rows=nl), o, IDEN, bias=float(S - 1))
-        act(R("da", 0, L), R("ramp"), COPY, ind=R("dl", 0, nc))
+            st["F"] = F
+            if NXP[X == F]:
+                o = R("bp" + X, 384, 392, rows=nl)
+                mm(o, R("b", l0, l0 + nl), R("wa", 1, 16, 2), True, False)
+                mm(o, R("ones", 0, nl, rows=1), R("own", rows=1), False, False)
+                mm(o, R("fd", l0, l0 + nl), R("wn"), False, True)
+            else:
+                o = R("bp" + X, 384, 448, rows=nl)
+                mm(o, R("b", l0, l0 + nl), R("wk", 0, 128, 2), True, False)
+                mm(o, R("idb", 0, nl, rows=nl), R("mn", rows=nl), False, False)
+                mm(o, R("fd", l0, l0 + nl), R("ws", 0, 128, 2), False, True)
+                act(R("tx" + X, rows=nl), o, IDEN, bias=float(S))
+                st["tx"] = len(ops) - 1
+        act(R("da", 0, L), R("ramp"), COPY, ind=dl)
+        da = len(ops) - 1
+        if "a" in RULES:
+            ops[da]["deps"].setdefault([st["tx"] for st in sts if st["X"] == F][0], False)
+        if "b" in RULES:
+            ops[uu]["deps"].setdefault(da, False)
         bp = "bp" + F
         mm(R(bp, 0, L), R("idb"), R("uu", 0, L), True, False)
         mm(R(bp, 0, L), R("idb"), R("b", 0, L), False, False)
         mm(R(bp, 0, L), R("ones", rows=1), R("mhalf", 0, L, rows=1), False, True)
         act(R("uv", 0, L), R(bp, 0, L), IDEN, bias=MAGIC, scale=0.5)
-        act(R("val", 0, L), R("uv", 0, L), IDEN, bias=col("vb%d" % t), scale=col("rl"))
-        at = L + 16 * (nc % 2)
-        act(R("val", at, at + L), R("b", 0, L), IDEN, bias=col("neg"), scale=col("rl"))
-
-    def rivals(st, sts, F):
-        X, h, nl, nc, c0 = st["X"], st["h"], st["nl"], st["nc"], st["c0"]
-        L = sum(x["nl"] for x in sts)
-        rows = max(x["nl"] for x in sts)
-        nx, off = R("nx" + X, rows=nl), float(2048 + 15 * 8192)
-        mm(R("k" + X, 0, nc), R("idf"), R("dT", c0, c0 + nc), True, False)
-        tt(R("nx" + X), R("vi", 8 * h, 8 * h + 8), R("tx" + X), GT, ind=R("rep", 0, 8))
-        mm(R("k" + X, 0, nc), nx, R("cm8", 0, nc, rows=nl), False, True)
-        mm(R("q2", 128 * h, 128 * h + 128, rows=rows), R("hug", 0, rows, rows=nl), nx, X == F, False)
-        scols = SCOLS[X != F]
-        if scols:
-            act(R("nco", 0, nc), R("k" + X, 0, nc), IDEN, bias=off, scale=-1.0)
-        for c in range(c0, c0 + nc):
-            same = R("e3", 256 * c + 16 * c, 256 * c + L)
-            if c >= c0 + nc - scols:
-                far = R("far", 256 * (c % 2) + 16 * c, 256 * (c % 2) + L)
-                act(far, R("da", 16 * c, L), ABS, bias=R("nco", c - c0, c - c0 + 1))
-                act(same, far, RELU, bias=1.0, scale=-1.0)
-            else:
-                ts(same, R("da", 16 * c, L), off, R("k" + X, c - c0, c - c0 + 1), ADD, EQ)
-            for o in sts[h:]:
-                w = R("ww", 128 * (c - c0), 128 * (c - c0) + 128) if o is st else R("ww", 1024, 1152)
-                mm(R("q2", 128 * o["h"], 128 * o["h"] + 128, rows=rows), R("e3", 256 * c + o["l0"], 256 * c + o["l0"] + rows), w,
-                   False, X != F and c == c0 + nc - 1 and o is sts[-1])
-
-    def moves(sts):
-        nc = sum(st["nc"] for st in sts)
-        rows = max(x["nl"] for x in sts)
-        w = 2 * nc + nc % 2
-        mm(R("q1", 64, 64 + w), R("idf"), R("base2" if nc % 2 == 0 else "base", 0, w), True, False)
-        ts(R("x2", rows=rows), R("q2", 0, 256, rows=rows), R("cols", COL["thr"], COL["thr"] + 1, rows=rows), None, GE)
+        act(R("val", 16 * d0, 16 * d0 + L), R("uv", 0, L), IDEN, bias=col("vb%d" % t), scale=col("rl"))
         for st in sts:
-            for k in (0, nc + nc % 2):
-                o = 64 + k + st["c0"]
-                mm(R("q1", o, o + st["nc"]), R("x2", 128 * st["h"], 128 * st["h"] + 128, rows=st["nl"]), R("cm8", 0, st["nc"], rows=st["nl"]), False,
-                   st["h"] == 1 and k > 0)
-        tt(R("ofl", 0, w), R("dl", 0, w), R("q1", 64, 64 + w), MAX)
-        tc(R("f"), R("val", 0, 16 * w), oind=R("ofl", 0, w))
+            act(R("val", 16 * st["s"], 16 * st["s"] + st["nl"]), R("b", st["l0"], st["l0"] + st["nl"]), IDEN, bias=col("neg"), scale=col("rl"))
+            if "c" in RULES:
+                ops[-1]["deps"].setdefault(uu, False)
+
+    def compare(st, L, scols):
+        X, h, nl, nc, c0 = st["X"], st["h"], st["nl"], st["nc"], st["c0"]
+        off = 2048.0
+        mm(R("k" + X, 0, nc), R("idf"), R("dT", c0, c0 + nc), True, False)
+        if NXP[X == st["F"]]:
+            tt(R("nx" + X, 15, 143, 16, rows=nl), R("vi", 8 * h, 8 * h + 8, rows=nl), R("bp" + X, 384, 392, rows=nl), GE)
+            for q in range(16):
+                mm(R("k" + X, 0, nc), R("nx" + X, 15 - q, 143 - q, rows=nl), R("idw", q, nl, 16, rows=nl), False, q == 15)
+        else:
+            off += 7 * 8192
+            tt(R("ny" + X, 1, 129, 2), R("vi", 8 * h, 8 * h + 8), R("tx" + X), GE, ind=R("rep8", 0, 4))
+            for k in (0, 1):
+                mm(R("k" + X, 0, nc), R("ny" + X, 1 - k, 129 - k, rows=nl), R("cm8", 8 * k, 8 * k + nc, rows=nl), False, k == 1)
+        st["cut"] = cut = c0 + nc - scols
+        if scols:
+            act(R("nco", 0, nc), R("k" + X, 0, nc), IDEN, bias=off + 0.5, scale=-1.0)
+            act(R("nco", 8, 8 + nc), R("k" + X, 0, nc), IDEN, bias=0.5 - off)
+        for c in range(c0, c0 + nc):
+            if c >= cut:
+                act(RN("e3", c, (0, L - 16 * c)), R("da", 16 * c, L), SIGN, bias=R("nco", c - c0, c - c0 + 1))
+                act(RN("e4", c, (0, L - 16 * c)), R("da", 16 * c, L), SIGN, bias=R("nco", 8 + c - c0, 9 + c - c0), scale=-1.0)
+            else:
+                ts(RN("e3", c, (0, L - 16 * c)), R("da", 16 * c, L), off, R("k" + X, c - c0, c - c0 + 1), ADD, EQ)
+
+    def rivals(bank, table, c0, c1, sts):
+        calls, late = [(RN(bank, (c0, c1), (0, 18)), R("idf"), RN(table, (c0, c1), (0, 18)))], []
+        for st in sts:
+            for a, b, half, es in ((st["c0"], st["cut"], 0, ("e3",)), (st["cut"], st["c0"] + st["nc"], 128, ("e3", "e4"))):
+                for e in es:
+                    to = late if half else calls
+                    for c in range(a, min(b, c1 - 1)):
+                        lo = max(c0, c + 1)
+                        to.append((RN(bank, (lo, c1), (1, 17)), R("wall", half, half + 128), RN(e, c, (16 * (lo - c), 16 * (c1 - c)))))
+                    if c0 <= a < b:
+                        to.append((RN(bank, (a, b), (1, 17)), R("wtri", half, half + 128), RN(e, (a, b), (0, 16))))
+        calls = calls[:LATE] + late + calls[LATE:] if late else calls
+        for k, (o, l, r) in enumerate(calls):
+            mm(o, l, r, k == 0, k == len(calls) - 1)
+            if k == 0:
+                ops[-1]["early"] = 20.0
+
+    def scatter(bank, parts, lo, hi):
+        if RVP[parts[0][0]["t"]]:
+            c0, c1 = min(st["c0"] for st, _ in parts), max(st["c0"] + st["nc"] for st, _ in parts)
+            at = "k" + parts[0][0]["X"]
+            mm(R(at, 448 + lo, 448 + hi), R("idf"), R("rr", lo, hi), True, False)
+            red(R("rb", c0, c1), RN(bank, (c0, c1), (0, 17)), MIN)
+            for k, (st, kind) in enumerate(parts):
+                mm(R(at, 448 + st[kind], 448 + st[kind] + st["nc"]), R("idb"), R("rb", st["c0"], st["c0"] + st["nc"]), False, k == len(parts) - 1)
+            tt(R("ofl", lo, hi), R("dl", lo, hi), R(at, 448 + lo, 448 + hi), MAX)
+            tc(R("f"), R("val", 16 * lo, 16 * hi), oind=R("ofl", lo, hi))
+            return
+        for st, kind in parts:
+            k = 0 if kind == "d" else 1
+            red(R("rs", st[kind], st[kind] + st["nc"]), RN(bank, (st["c0"], st["c0"] + st["nc"]), (k, 17 + k)), MIN)
+        tt(R("ofl", lo, hi), R("rs", lo, hi), R("dl", lo, hi), MAX)
+        tc(R("f"), R("val", 16 * lo, 16 * hi), oind=R("ofl", lo, hi))
+
+    def moves(t, sts):
+        A, B = sts
+        nc = A["nc"] + B["nc"]
+        if t == 0:
+            compare(A, 16 * nc, SCOLS[0])
+            rivals("q2", "tb0", 0, A["nc"], [A])
+            scatter("q2", [(A, "s"), (A, "d")], A["s"], B["d"])
+            compare(B, 16 * nc, 0)
+            rivals("q1", "tb0", B["c0"], nc, [A, B])
+            requests(sts, "A")
+            scatter("q1", [(B, "d"), (B, "s")], B["d"], B["s"] + B["nc"])
+        else:
+            compare(B, 16 * nc, SCOLS[1])
+            if TENT[t]:
+                rivals("q2", "tb%d" % t, B["c0"], nc, [B])
+                scatter("q2", [(B, "d")], B["d"], B["d"] + B["nc"])
+            compare(A, 16 * nc, 0)
+            rivals("q1", "tb%d" % t, 0, nc, [B, A])
+            if t + 1 < RO:
+                requests(sts, "B")
+            if TENT[t]:
+                scatter("q1", [(A, "d"), (A, "s"), (B, "s")], B["s"], B["d"])
+            else:
+                scatter("q1", [(dict(A, nc=nc), "d"), (A, "s"), (B, "s")], 0, 2 * nc)
 
     def requests(sts, F):
         ts(R("ebi"), R("id0"), 1.0 / G, 1.0 - (S + (G - 1) / 2) / G, MUL, ADD)
@@ -738,12 +880,21 @@ def rank_program(g, core, T, topo):
         mm(R(bp, 320, 384, rows=B["nl"]), R("ones", 0, B["nl"], rows=A["nl"]), R("on", 0, 64, rows=A["nl"]), False, True)
         scan(R("qs"), R("rs8"), R(bp, 256, 384), 0.0, MUL, MAX)
         tt(R("ek"), R("idm"), R("on"), MUL, ind=R("rep8"))
-        for k in (0, 1):
-            tt(R("mh", 128 * k, 128 * k + 128), R("qs"), R("jm1", 0, 128), EQ, ind=R("rep87", 8 * k, 8 * k + 8))
-        for st in sts:
-            nl, h = st["nl"], st["h"]
-            mm(RN("s" + F, 0, ALL16, (0, 4)), R("mh", 128 * h, 128 * h + 128, rows=nl), R("ek", 64 * h, 64 * h + 64, rows=nl), h == 0, h == 1)
-        act(R("rq"), RN("s" + F, 0, ALL16, (0, 4)), COPY)
+        if MHS:
+            bq = "bpB" if F == "A" else "bpA"
+            mm(R(bq, 0, 256), R("idh", 0, 128, rows=1), R("jh", rows=1), True, False)
+            mms([(R(bq, m, 256, 16), R("idh", 128, 256), R("qs", 7, 128, 8), False, m == 15) for m in range(16)])
+            act(R("mh"), R(bq, 0, 256), SIGN, bias=col("half"))
+            act(R("mi"), R(bq, 0, 256), SIGN, bias=col("half"), scale=-1.0)
+        else:
+            for k in (0, 1):
+                tt(R("mh", 128 * k, 128 * k + 128), R("qs"), R("jm1", 0, 128), EQ, ind=R("rep87", 8 * k, 8 * k + 8))
+        for nm in ("mh", "mi") if MHS else ("mh",):
+            for st in sts:
+                nl, h = st["nl"], st["h"]
+                mm(R("k" + F, 384, 448), R(nm, 128 * h, 128 * h + 128, rows=nl), R("ek", 64 * h, 64 * h + 64, rows=nl), h == 0 and nm == "mh",
+                   h == 1 and (nm == "mi" or not MHS))
+        act(R("rq"), R("k" + F, 384, 448), COPY, scale=0.5 if MHS else 1.0)
         tt(R("gg", G, 16 * BW, BW), R("rq"), R("ce"), SUB, ind=R("gl", 0, 1))
 
     for o in ops:
@@ -759,15 +910,20 @@ def rank_program(g, core, T, topo):
         for hop in range(1, H + 1):
             for st in order:
                 look(st, hop, ncs)
+            if t == 0 and hop in RAMP:
+                ops[ramp[RAMP[hop]]]["deps"][order[1]["cp"]] = False
+            if t == 0 and hop < H:
+                for k in range(2 * hop - 1, 2 * hop + 1):
+                    hi = min(M * (k + 1), S)
+                    act(R("pl", M * k, hi), R("pl", 0, hi - M * k), COPY)
+                    ops[-1]["lazy"] = True
+                    ops[-1]["deps"].setdefault(turn[0], False)
         places(t, sts, F)
-        for st in order:
-            rivals(st, sts, F)
-        if t + 1 < RO:
-            requests(sts, F)
-        moves(sts)
+        moves(t, sts)
         if t == 0:
             later_tables()
         if t + 1 < RO:
             exchange(t + 1)
-    dma("y", T.y[:], T.f[:, OWN:OWN + S], [], [R("f", OWN, OWN + S)], 5.0)
+    for q, lo in (("y", 0), ("s", hx)):
+        dma(q, T.y[:, lo:lo + hx], T.f[:, lo:lo + hx], [], [R("f", lo, lo + hx)], 4.0)
     emit_all()

from concourse.bass import DstId, RemoteDMATransfer
from concourse.mybir import dt, AluOpType, AxisListType, ActivationFunctionType

ADD, SUB, MUL, MAX, MIN = AluOpType.add, AluOpType.subtract, AluOpType.mult, AluOpType.max, AluOpType.min
GE, GT, LE, LT, EQ = AluOpType.is_ge, AluOpType.is_gt, AluOpType.is_le, AluOpType.is_lt, AluOpType.is_equal
NE = AluOpType.not_equal
SHR, AND = AluOpType.arith_shift_right, AluOpType.bitwise_and
SIGN = ActivationFunctionType.Sign
IDEN, COPY, RELU, EXP = ActivationFunctionType.Identity, ActivationFunctionType.Copy, ActivationFunctionType.Relu, ActivationFunctionType.Exp

N, S, G, CAP, WN, M, RO, H, T0 = 8, 3328, 112, 16, 144, 512, 3, 4, 192
OWN = 0
NULL = S + (N - 1) * G
WIN = NULL + 16
FW = WIN + 512
BW = 120
K17 = 17 * 8192
MID = 97
NV = 16
RR = 4
NC = NV // RR
MAGIC = 12582912.0
PEN = float(2 ** 26)
TOP = 14 * 2 ** 20
RIVAL = 32768.0
LISTS = (((0, 4), (14, 8)), ((8, 16), (0, 24)))
CHUNKS = {128: (32, 32, 32, 32), 80: (32, 32, 16), 64: (32, 32)}
PARTS = {128: ((0, 32), (32, 64), (64, 96), (96, 128)), 80: ((0, 32), (32, 64), (64, 80)), 64: ((0, 32), (32, 64))}
APARTS = PARTS
ZEARLY = 0.0
OPENING = {128: (32, 32, 32, 32), 64: (32, 32)}

SCRATCH = {}
for _n, _w, _t in (
        ("f", FW, "bfloat16"), ("nbw", NULL + 16, "int32"), ("pl", OWN + S, "bfloat16"), ("wti", 1, "int32"), ("wni", 27, "int32"), ("sdi", 49, "int32"),
        ("sdp", 56, "uint16"), ("sdf", 56, "float32"), ("sdw", 800, "float32"), ("sdx", 784, "float32"), ("wl", 30, "uint16"), ("rep", 50, "uint16"),
        ("wq", 432, "float32"), ("jf", 128, "float32"), ("jmf", 256, "float32"), ("jm1", 256, "float32"), ("j4", 128, "float32"), ("j7", 128, "float32"),
        ("j16", 8, "float32"), ("ji", 64, "int32"), ("cols", 40, "float32"), ("idf", 128, "float32"), ("mask1", 80, "float32"), ("rep1", 10, "uint16"), ("idb", 128, "bfloat16"),
        ("nco", 16, "float32"), ("mask", 256, "float32"), ("rep8", 8, "uint16"), ("rep87", 16, "uint16"), ("gl", 2, "uint16"), ("blk", 128, "float32"),
        ("wa", 16, "bfloat16"), ("wm", 16, "bfloat16"), ("wn", 8, "bfloat16"), ("wz", 144, "bfloat16"), ("wk", 128, "bfloat16"), ("ws", 128, "bfloat16"), ("mn", 64, "bfloat16"), ("rb", 16, "bfloat16"),
        ("wall", 256, "bfloat16"), ("wtri", 256, "bfloat16"), ("idw", 128, "bfloat16"), ("own", 8, "bfloat16"),
        ("cm8", 16, "bfloat16"), ("rsa", 128, "float32"), ("rs8", 128, "float32"), ("tril", 128, "bfloat16"), ("ones", 128, "bfloat16"),
        ("mhalf", 256, "bfloat16"), ("ec", 128, "float32"), ("onf", 128, "float32"), ("b", 256, "bfloat16"), ("cm2", 16, "float32"),
        ("dl", 32, "uint16"), ("fd", 256, "bfloat16"), ("uu", 256, "bfloat16"),
        ("uv", 256, "float32"), ("val", 512, "bfloat16"), ("ramp", OWN + S, "float32"), ("da", 256, "float16"), ("ofl", 32, "uint16"), ("on", 128, "bfloat16"),
        ("qs", 128, "float16"), ("mh", 256, "float16"), ("mi", 256, "float16"), ("idh", 256, "float16"), ("jh", 256, "float16"), ("ek", 128, "float16"), ("rq", 64, "float32"), ("gg", 16 * BW, "bfloat16"), ("ld0", 7 * BW, "bfloat16"),
        ("ld1", 7 * BW, "bfloat16"), ("ld2", 7 * BW, "bfloat16"), ("rki", 8, "uint16"), ("rkj", 8, "uint16"), ("qa", 128, "float32"), ("qc", 128, "float32")):
    SCRATCH[_n] = ("sbuf", [128, _w], _t)
for _x in "AB":
    for _n, _w, _t in (("l", 8, "uint16"), ("off", 128, "uint16"), ("a", 2048, "bfloat16"), ("m", 2048, "bfloat16"), ("cp", 128, "float32"),
                       ("nf", 128, "bfloat16"), ("nx", 144, "bfloat16"), ("ny", 136, "bfloat16"), ("xx", 168, "float32"), ("tx", 64, "float32")):
        SCRATCH[_n + _x] = ("sbuf", [128, _w], _t)
    SCRATCH["t" + _x] = ("sbuf", [128, 8, 18], "float32")
for _n in ("e3", "e4"):
    SCRATCH[_n] = ("sbuf", [128, 16, 256], "bfloat16")
for _n in ("tb0", "tb1", "tb2"):
    SCRATCH[_n] = ("sbuf", [128, 16, 18], "float32")
for _n in ("q1", "q2"):
    SCRATCH[_n] = ("psum", [128, 16, 32], "float32")
SCRATCH["wb"] = ("sbuf", [128, 128], "bfloat16")
SCRATCH["mc"] = ("sbuf", [128, 8, 18, 3], "bfloat16")
for _n in ("kA", "kB", "bpA", "bpB"):
    SCRATCH[_n] = ("psum", [128, 512], "float32")
for _n in ("sA", "sB"):
    SCRATCH[_n] = ("psum", [128, 9, 18, 3], "float32")
PSUMS = [k for k in SCRATCH if SCRATCH[k][0] == "psum"]
ALIAS = {}
for _buf, _t, _names in (
        ("tf", "float32", (("dT", 16), ("idm", 16), ("ce", 16), ("c112", 8), ("cm", 8), ("rr", 32), ("rs", 32), ("wf", 32))),
        ("ti", "int32", (("vi", 16), ("id0", 16), ("id1", 16), ("zi", 16), ("zm", 16), ("zq", 16), ("zh", 16), ("zg", 16), ("ebi", 16), ("ci", 8)))):
    _o = 0
    for _n, _w in _names:
        ALIAS[_n] = (_buf, _o, _w)
        _o += _w
    SCRATCH[_buf] = ("sbuf", [128, _o], _t)
SEMAPHORES = ["sv", "ss", "sp", "sg", "go"] + ["d%d" % i for i in range(12)] + ["arr%d" % i for i in range(9)] + ["snd%d" % i for i in range(9)]

CYC, GATHER, SCATTER, PECYC, WAKE = 0.00083, 1.56, 3.8, 0.00042, 0.17
TAIL, EARLY = 1.0, 1.5
BV = ("", "")
OFF2 = ("AB", "AB")
ALL8, ALL16, HALVES = (0, 8), (0, 16), ((0, 8),)
CLOSING = {128: (32, 32, 32, 16, 16), 80: (32, 32, 16)}
SCOLS = (0, 0)
PASSES = 1
CPS = False
LATE = 99
RAMP = {2: 5, 3: 9}
ZPIN = (None, (4, 1.5))
RULES = "bc"
CK = (9, 9)
ZAFTER = "bp"
BEARLY = (1.0, 1.0)
MHS = True
FDE = 0.0
LS = ("", "")
GROUP = 1
CALLS = (0, 4, 6)
RVP = (True, True, False)
NXP = (False, False)
TENT = (True, False, True)
GGV = ((1, 3, 5), (1, 3, 5), (1, 3, 5))
ONV = ("A2A3A4", "A1A2A3B2B3B4")
OFFS = ("", "")
SHARED = {128: ((32, 32, 32, 16, 16), 4), 80: ((32, 32, 16), 2), 64: ((32, 16, 16), 2)}
NEAR = 4
FILL = 0.2


def R(name, lo=None, hi=None, step=None, rows=128):
    if name in ALIAS:
        buf, o, w = ALIAS[name]
        return (buf, o + (0 if lo is None else lo), o + (w if hi is None else hi), step, rows)
    if lo is None:
        return (name, 0, SCRATCH[name][1][1], None, rows)
    return (name, lo, hi, step, rows)


def RN(name, *idx, rows=128):
    dims = SCRATCH[name][1][1:]
    n = total = 1
    for d, i in zip(dims, idx):
        n, total = n * (1 if isinstance(i, int) else i[1] - i[0]), total * d
    return (name, 0, total, None, rows, tuple(i if isinstance(i, int) else slice(i[0], i[1]) for i in idx), n)


def width(r):
    return r[6] if len(r) > 5 else len(range(r[1], r[2], r[3] or 1))


def narrow(*rs):
    return all(SCRATCH[r[0]][2] in ("bfloat16", "float16", "uint16") for r in rs)


def meet(r, lo, hi, step):
    if r[2] <= lo or hi <= r[1]:
        return False
    if (r[3] is None) == (step is None):
        return True
    (a, b, s), (c, d) = ((lo, hi, step), r[1:3]) if step else (r[1:4], (lo, hi))
    return a + max(0, -((a - c) // s)) * s < min(b, d)


def boxes_meet(a, b):
    if not a or not b:
        return True
    ends = [[(i, i + 1) if isinstance(i, int) else (i.start, i.stop) for i in x[0]] for x in (a, b)]
    return all(p[0] < q[1] and q[0] < p[1] for p, q in zip(*ends))


def topological(ops, users):
    left = [len(o["deps"]) for o in ops]
    out = [i for i, x in enumerate(left) if not x]
    for i in out:
        for u in users[i]:
            left[u] -= 1
            if not left[u]:
                out.append(u)
    return out


def in_order(ops):
    n = len(ops)
    users = [[] for _ in range(n)]
    for i, o in enumerate(ops):
        for d in o["deps"]:
            users[d].append(i)
    prio = [0.0] * n
    for i in topological(ops, users)[::-1]:
        o = ops[i]
        prio[i] = o["occ"] + max([o["lat"]] + [prio[u] + (o["lat"] if ops[u]["deps"][i] else 0.0) for u in users[i]])
    prio = [p + o["early"] for p, o in zip(prio, ops)]
    left = [len(o["deps"]) for o in ops]
    ready_at = [0.0] * n
    cand = {}
    for i, o in enumerate(ops):
        cand.setdefault(o["q"], [])
        if not left[i]:
            cand[o["q"]].append(i)
    free = {q: 0.0 for q in cand}
    out = []
    while len(out) < n:
        q = min((x for x in cand if cand[x]), key=lambda x: max(free[x], min(ready_at[i] for i in cand[x])))
        now = max(free[q], min(ready_at[i] for i in cand[q]))
        here = sorted((i for i in cand[q] if ready_at[i] <= now), key=lambda i: (-prio[i], i))
        top = max(cand[q], key=lambda i: (prio[i], -i))
        pick = None
        for i in here:
            go = max(now + prio[i], max(now + ops[i]["occ"], ready_at[top]) + prio[top])
            hold = max(ready_at[top] + prio[top], ready_at[top] + ops[top]["occ"] + prio[i])
            if i == top or go <= hold + (0.0 if ops[i]["lazy"] else FILL):
                pick = i
                break
        if pick is None:
            free[q] = min(ready_at[top], now + 0.03)
            continue
        cand[q].remove(pick)
        out.append((now, len(out), pick))
        free[q] = now + ops[pick]["occ"]
        for u in users[pick]:
            ready_at[u] = max(ready_at[u], free[q] + (ops[pick]["lat"] if ops[u]["deps"][pick] else 0.0))
            left[u] -= 1
            if not left[u]:
                cand[ops[u]["q"]].append(u)
    start = [0.0] * n
    for now, _, i in out:
        start[i] = now
    back = [{u: ops[u]["deps"][i] for u in users[i]} for i in range(n)]
    for _ in range(PASSES):
        late = justify(ops, back, [-(start[i] + ops[i]["occ"]) for i in range(n)], True)
        start = justify(ops, [o["deps"] for o in ops], [-(late[i] + ops[i]["occ"]) for i in range(n)], False)
    rank = {i: k for k, i in enumerate(topological(ops, users))}
    return sorted(range(n), key=lambda i: (start[i], rank[i]))


def justify(ops, before, key, backward):
    n = len(ops)
    after = [[] for _ in range(n)]
    for i in range(n):
        for d in before[i]:
            after[d].append(i)
    left = [len(before[i]) for i in range(n)]
    pool = sorted(((key[i], i) for i in range(n) if not left[i]), reverse=True)
    busy = {}
    start = [0.0] * n
    while pool:
        i = pool.pop()[1]
        o = ops[i]
        t = o["lat"] if backward and not before[i] else 0.0
        for d, wait in before[i].items():
            t = max(t, start[d] + ops[d]["occ"] + ((o if backward else ops[d])["lat"] if wait else 1e-6))
        line = busy.setdefault(o["q"], [])
        k = len(line)
        while k and line[k - 1][1] > t:
            k -= 1
        while k < len(line) and line[k][0] < t + o["occ"]:
            t = max(t, line[k][1])
            k += 1
        line.insert(k, (t, t + o["occ"]))
        start[i] = t
        for u in after[i]:
            left[u] -= 1
            if not left[u]:
                j = len(pool)
                while j and pool[j - 1] < (key[u], u):
                    j -= 1
                pool.insert(j, (key[u], u))
    return start


def rank_program(g, core, T, topo):
    rank = T.rank_of(core)
    if rank is None:
        return
    qs = {"v": g.vector, "s": g.scalar, "p": g.tensor, "g": g, "y": g.sync}
    semof = {"v": "sv", "s": "ss", "p": "sp", "g": "sg"}
    ops = []
    hist = {}
    dman = [0]
    chosen = [0]
    turn = []

    def ap(r):
        name, lo, hi, step, rows = r[0:5]
        p0, p1 = rows if isinstance(rows, tuple) else (0, rows)
        if len(r) > 5:
            return T[name][(slice(p0, p1),) + r[5]]
        return T[name][p0:p1, lo:hi] if step is None else T[name][p0:p1, lo:hi:step]

    def record(q, fn, reads, writes, occ, lat=WAKE, sem=None, inc=1, after=(), ind=0):
        me = len(ops)
        deps = {d: True for d in after}
        acc = [(r, False) for r in reads] + [(r, True) for r in writes]
        for r, w in acc:
            name, bank = r[0], r[0] in PSUMS
            for lo, hi, ow, oq, o, st, box in hist.get(name, ()):
                if bank and oq == q == "p":
                    deps.setdefault(o, False)
                elif (bank and oq != q) or ((w or ow) and meet(r, lo, hi, st) and boxes_meet(r[5:6], box)):
                    deps[o] = True
        for r, w in acc:
            name, bank = r[0], r[0] in PSUMS
            lst = hist.get(name, [])
            if bank and q == "p":
                lst = []
            elif bank and lst and lst[-1][3] != q:
                lst = [x for x in lst if x[3] == lst[-1][3]]
            elif w and not bank and r[3] is None and r[4] == 128 and len(r) == 5:
                lst = [x for x in lst if not (x[0] >= r[1] and x[1] <= r[2])]
            hist[name] = lst + [(r[1], r[2], w, q if sem is None else None, me, r[3], r[5:6])]
        ops.append({"q": q, "fn": fn, "deps": deps, "occ": occ, "lat": lat, "sem": sem, "inc": inc, "early": 0.0, "lazy": False, "ind": ind})
        return me

    def emit_all():
        cnt = {q: 0 for q in semof}
        known = {q: {} for q in qs}
        done = {}
        for i in in_order(ops):
            o = ops[i]
            q = o["q"]
            if o["fn"] is None:
                done[i] = (o["sem"], o["inc"], {})
                continue
            need = {}
            for d, wait in o["deps"].items():
                if wait and done[d][1] > need.get(done[d][0], (0,))[0]:
                    need[done[d][0]] = (done[d][1], done[d][2])
            kn = known[q]
            for sem in sorted(need, key=lambda s: -len(need[s][1])):
                val, snap = need[sem]
                if kn.get(sem, 0) >= val:
                    continue
                qs[q].wait_ge(T.sem[sem], val)
                kn[sem] = val
                for k, v in snap.items():
                    if kn.get(k, 0) < v:
                        kn[k] = v
            ins = o["fn"]()
            if o["sem"] is None:
                cnt[q] += 1
                ins.then_inc(T.sem[semof[q]], 1)
                done[i] = (semof[q], cnt[q], dict(kn))
            else:
                done[i] = (o["sem"], o["inc"], dict(kn))
        for q in semof:
            g.wait_ge(T.sem[semof[q]], cnt[q])
        for o in ops:
            if o["sem"] is not None and known["g"].get(o["sem"], 0) < o["inc"]:
                g.wait_ge(T.sem[o["sem"]], o["inc"])

    def dma(q, out, in_, outr, inr, lat, after=()):
        sem = "d%d" % dman[0]
        dman[0] += 1
        return record(q, lambda: qs[q].dma_start(out, in_).then_inc(T.sem[sem], 16), inr, outr, 0.05, lat, sem, 16, after)

    def vcost(out, ins, ind, both=False):
        if ind:
            return 0.05 + width(out) * GATHER * CYC
        return max(64, width(out) * (2 if both else 0.5 if narrow(out, *ins) else 1)) * CYC

    def src(r, ind):
        return ap(r).indirect(ap(ind)) if ind else ap(r)

    def ts(out, in0, s1, s2, o0, o1=None, ind=None):
        rd = [in0] + [x for x in (s1, s2, ind) if isinstance(x, tuple)]
        a = [ap(x) if isinstance(x, tuple) else x for x in (s1, s2)] + ([o0] if o1 is None else [o0, o1])
        record("v", lambda: g.vector.tensor_scalar(ap(out), src(in0, ind), *a), rd, [out], vcost(out, [in0], ind), ind=width(out) if ind else 0)

    def tt(out, in0, in1, op, ind=None):
        both = in0[0] not in PSUMS and in1[0] not in PSUMS
        record("v", lambda: g.vector.tensor_tensor(ap(out), src(in0, ind), ap(in1), op), [in0, in1] + ([ind] if ind else []), [out],
               vcost(out, [("tf",)], ind, both), ind=width(out) if ind else 0)

    def tc(out, in_, ind=None, oind=None):
        cost = 0.05 + width(in_) * SCATTER * CYC if oind else vcost(out, [in_], ind)
        record("v", lambda: g.vector.tensor_copy(src(out, oind), src(in_, ind)), [in_] + [x for x in (ind, oind) if x], [out], cost,
               ind=width(out) if ind else 0)

    def scan(out, d0, d1, init, o0, o1):
        record("v", lambda: g.vector.tensor_tensor_scan(ap(out), ap(d0), ap(d1), init, o0, o1), [d0, d1], [out], vcost(out, [d0, d1], None))

    def red(out, in_, op):
        record("v", lambda: g.vector.tensor_reduce(ap(out), ap(in_), AxisListType.X, op), [in_], [out], max(64, width(in_)) * CYC)

    def gcopy(out, in_):
        n = width(out)
        record("g", lambda: g.affine_select(ap(out), ap(in_), [[0, n]], GE, 0.0, 0, 0), [in_], [out], 0.17 + 2 * n * CYC)

    def select(out, in_, pattern, op, other, base, cmul):
        record("g", lambda: g.affine_select(ap(out), ap(in_), pattern, op, other, base, cmul), [in_], [out], 0.17 + 2 * width(out) * CYC)

    def ms(out, c):
        record("v", lambda: g.vector.memset(ap(out), c), [], [out], vcost(out, [], None))

    def act(out, in_, func, bias=None, scale=None, ind=None, more=0.0):
        kw = {k: (ap(v) if isinstance(v, tuple) else v) for k, v in (("bias", bias), ("scale", scale)) if v is not None}
        rd = [in_] + [x for x in (ind, bias, scale) if isinstance(x, tuple)]
        cost = 0.065 + width(out) * GATHER * CYC if ind else 0.02 + max(64, width(out)) * CYC
        record("s", lambda: g.scalar.activation(ap(out), src(in_, ind), func, **kw), rd, [out], cost + more, ind=width(out) if ind else 0)

    def mm(out, lhsT, rhs, start, stop):
        cost = max(min(64, width(lhsT)), width(rhs)) * (1 if narrow(lhsT) else 4) * PECYC
        record("p", lambda: g.tensor.matmul(ap(out), ap(lhsT), ap(rhs), start, stop), [lhsT, rhs], [out], cost)

    def mms(calls):
        if len(calls) > GROUP:
            for k in range(0, len(calls), GROUP):
                mms(calls[k:k + GROUP])
            return
        cost = sum(max(min(64, width(l)), width(r)) * (1 if narrow(l) else 4) * PECYC for _, l, r, _, _ in calls)
        record("p", lambda: [g.tensor.matmul(ap(o), ap(l), ap(r), a, b) for o, l, r, a, b in calls][-1],
               [x for c in calls for x in c[1:3]], [calls[0][0]], cost)

    def iota(out, pattern, base, cmul, flt=True):
        kw = {"allow_small_or_imprecise_dtypes": True} if flt else {}
        i = record("g", lambda: g.iota(ap(out), pattern, base, cmul, **kw), [], [out], 0.13 + 2 * width(out) * CYC)
        if ops[i - 1]["q"] == "g":
            ops[i]["deps"][i - 1] = False

    COL = {}

    def col(name):
        if name not in COL:
            COL[name] = len(COL)
        return R("cols", COL[name], COL[name] + 1)

    hx = S // 2
    d0 = dma("y", T.sdi[:], T.snd[:], [R("sdi")], [], 2.0)
    d1 = dma("s", T.f[:, OWN + hx:OWN + S], T.x0[:, hx:S], [R("f", OWN + hx, OWN + S)], [], 3.0)
    d2 = dma("y", T.f[:, OWN:OWN + hx], T.x0[:, 0:hx], [R("f", OWN, OWN + hx)], [], 3.0)
    last = {"y": d2, "s": d1}
    ops[d2]["deps"][d0] = False
    for q, o, i, r, lat in (("s", T.wti[:], T.wt[:], R("wti"), 6.0), ("y", T.wni[:], T.wants[:], R("wni"), 6.0),
                            ("s", T.nbw[:, hx:S], T.nb[:, hx:S], R("nbw", hx, S), 8.0), ("y", T.nbw[:, 0:hx], T.nb[:, 0:hx], R("nbw", 0, hx), 9.0),
                            ("y", T.pl[:, 0:M], T.pull[:], R("pl", 0, M), 9.5)):
        d = dma(q, o, i, [r], [], lat)
        ops[d]["deps"][last[q]] = False
        last[q] = d

    iota(R("ci", 0, 1), [[0, 1]], 0, 1, False)
    iota(R("jf"), [[1, 128]], 0, 0)
    iota(R("jmf"), [[0, 16], [1, 16]], 0, 0)
    iota(R("j4"), [[1, 8], [0, 16]], 0, 0)
    iota(R("ji"), [[1, 64]], 0, 0, False)
    iota(R("nbw", S, NULL + 1), [[1, NULL + 1 - S]], S, 0, False)
    iota(R("j7"), [[0, 16], [1, 8]], 0, 0)
    iota(R("c112"), [[G, 8]], 0, 0)
    ramp = []
    for lo in range(0, S, 256):
        iota(R("ramp", lo, lo + 256), [[1, 256]], lo - 2048, 0)
        ramp.append(len(ops) - 1)

    def fill(out, c):
        act(out, R("jmf", 0, width(out), rows=out[4]), IDEN, scale=0.0, bias=c)

    for nm in ("id0", "id1", "vi"):
        ms(R(nm), 0)
    ms(R("dl"), 0)
    ms(R("bpA", 256, 384), 0.0)
    for r in (R("xxA"), R("xxB"), R("nyA"), R("nyB"), R("txA"), R("txB"), R("val", 16 * 13, 16 * 14), R("wz"), R("gg", G + 1, 7 * BW, BW)):
        fill(r, 0.0)
    ms(R("f", NULL, WIN), -1.0)
    ms(R("ones"), 1.0)
    fill(R("mhalf", rows=1), -0.5)
    ts(R("ci", 1, 2), R("ci", 0, 1), 15, None, AND)
    ts(R("ci", 2, 3), R("ci", 0, 1), 4, None, SHR)
    ts(R("ci", 3, 4), R("ci", 1, 2), 3, None, SHR)
    ts(R("ci", 4, 5), R("ci", 0, 1), 15, 1, AND, SHR)
    ts(R("ci", 5, 6), R("ci", 0, 1), 1, None, AND)
    for k, nm in enumerate(("p", "q", "g", "q8", "q2", "q1")):
        tc(col(nm), R("ci", k, k + 1))
    for e in range(7):
        tc(R("sdp", 8 * e, 8 * e + 7), R("sdi", 7 * e, 7 * e + 7))
    ts(col("r15"), col("q"), 15.0, None, EQ)
    ts(col("rl"), col("q"), 15.0, None, LT)
    for nm, of, c in (("mid", "r15", -MID), ("k17", "r15", K17), ("neg", "r15", -1), ("full", "r15", -PEN), ("mag", "rl", -MAGIC),
                      ("big", "rl", 2 * PEN), ("nbig", "rl", -2 * PEN)):
        ts(col(nm), col(of), float(c), None, MUL)
    for t in range(RO):
        act(col("vb%d" % t), col("r15"), IDEN, scale=float(T0 + t), bias=col("mag"))
    ts(R("cm"), R("jf", 0, 8), col("g"), None, EQ)
    ts(R("idf"), R("jf"), col("p"), None, EQ)
    ts(R("blk"), R("j4"), col("g"), None, EQ)
    ts(R("mask"), R("jmf"), col("q"), None, EQ)
    act(R("rsa"), R("jmf", 0, 128), SIGN)
    tc(col("wt"), R("wti"))
    tt(col("wtl"), col("wt"), col("rl"), MUL)
    act(R("idb"), R("idf"), COPY)
    act(R("wa", 0, 16, 2), R("cm"), COPY, scale=col("nbig"))
    act(R("wa", 1, 16, 2), R("cm"), COPY, scale=col("k17"))
    for k in (0, 1):
        act(R("wm", k, 16, 2), R("cm"), COPY, scale=col("big"))
    act(R("wb"), R("blk"), COPY, scale=col("nbig"))
    ms(RN("mc", ALL8, (0, 18), (0, 3), rows=3), 0.0)
    ms(RN("mc", ALL8, ALL16, (0, 2), rows=1), -PEN)
    ms(RN("mc", ALL8, (16, 18), (0, 2), rows=1), PEN)
    ts(RN("mc", ALL8, ALL16, 2, rows=1), R("jmf", 0, 128, rows=1), -8192.0, -8192.0, MUL, ADD)
    for k, c in enumerate((NULL % 4096, NULL - NULL % 4096, TOP)):
        ms(RN("mc", ALL8, 17, 2, rows=3 - k), float(c))
    act(R("wn"), R("cm"), COPY, scale=col("full"))
    act(R("wk"), R("blk"), COPY, scale=col("k17"))
    act(R("ws"), R("blk"), COPY, scale=col("full"))
    act(R("wz", 15, 143, 16), R("cm"), COPY, scale=col("wtl"))
    act(R("wall", 0, 128), R("blk"), COPY, scale=RIVAL)
    select(R("onf"), R("wall", 0, 128), [[1, 128]], GT, 0.0, 0, -1)
    select(R("wtri", 0, 128), R("onf"), [[1, 128]], NE, -RIVAL, 0, -1)
    act(R("rs8"), R("j7"), SIGN)
    act(R("ec"), R("j7"), IDEN, scale=-1.0, bias=7.0)
    select(R("qc"), R("ones"), [[1, 128]], GT, 0.0, 0, -1)
    select(R("tril"), R("qc"), [[1, 128]], NE, 1024.0, 0, -1)
    fill(R("idh", 0, 128, rows=1), 1.0)
    act(R("idh", 128, 256), R("idf"), COPY)
    act(R("jh", rows=1), R("jmf", rows=1), IDEN, scale=-1.0, bias=-1024.0)
    fill(col("half"), 0.5)
    act(R("ce"), R("jf", 0, 16), RELU, scale=float(-G), bias=float(6 * G))
    act(col("g8"), col("g"), COPY, scale=8.0)
    ts(R("gl", 0, 1), col("q"), 7.0, col("g8"), MIN, ADD)
    act(col("qb"), col("q"), IDEN, bias=float(WIN))
    act(R("rr"), R("jf", 0, 32), IDEN, scale=16.0, bias=col("qb"))

    def aside(k, cuts):
        act(RN("tb%d" % k, ALL16, (1, 17)), R("mask"), IDEN, scale=RIVAL / 2 - 2 ** 22, bias=float(2 ** 22))
        if RVP[k]:
            fill(RN("tb%d" % k, ALL16, 0), 0.0)
            fill(RN("tb%d" % k, ALL16, 17), 0.0)
        for h in (0, 1):
            for j, at in zip((17, 0), LISTS[k > 0][h]):
                if not RVP[k]:
                    act(RN("tb%d" % k, cuts[h:h + 2], j), R("jf", at, at + cuts[h + 1] - cuts[h]), IDEN, scale=16.0, bias=col("qb"))

    aside(0, (0, 4, 9))
    tc(R("rep"), R("ji", 0, 50))
    ts(R("rep1", 0, 4), R("jf", 0, 4), 2.0, col("q8"), MUL, ADD)
    ts(R("rep1", 4, 5), col("q"), 7.0, None, MIN)
    ts(R("mask1", 0, 64), R("j7", 0, 64), col("q2"), None, EQ)
    ms(R("mask1", 64, 80), 1.0)
    for k in (0, 1):
        ts(col("odd%d" % k), col("q1"), float(k), None, EQ)
        ts(R("cm2", 8 * k, 8 * k + 8), R("cm"), col("odd%d" % k), None, MUL)
    act(R("mn"), R("mask1", 0, 64), IDEN, scale=PEN, bias=-PEN)
    act(R("cm8"), R("cm2"), COPY, scale=8192.0)
    ts(R("rep8"), R("jf", 0, 8), 2.0, col("q8"), MUL, ADD)
    tc(R("wl", 0, 9), R("wni", 0, 9))
    ms(R("wf"), 0.0)
    tc(R("wf", 0, 27), R("wni"))
    tt(R("wq", 0, 160), R("wf"), R("mask", 0, 160), MUL, ind=R("rep", 0, 10))

    def later_tables():
        first, moved = len(ops), hist["ofl"][-1][4]
        for t in (1, 2):
            aside(t, (0, 8, 16))
            tc(R("wl", 10 * t + 1, 10 * t + 10), R("wni", 9 * t, 9 * t + 9))
        for lo, hi in ((10, 18), (18, 27)):
            tt(R("wq", 16 * lo, 16 * hi), R("wf"), R("mask", 0, 16 * (hi - lo)), MUL, ind=R("rep", lo, hi))
        tc(R("sdf", 0, 49), R("sdi"))
        ms(R("sdf", 49, 56), 0.0)
        for lo in range(0, 49, 8):
            hi = min(49, lo + 8)
            tt(R("sdx", 16 * lo, 16 * hi), R("sdf"), R("mask", 0, 16 * (hi - lo)), MUL, ind=R("rep", lo, hi))
        ms(R("sdw", 0, 1), float(NULL))
        for lo, hi in ((0, 4 * G), (4 * G, 7 * G)):
            mm(R("bpB", 0, hi - lo), R("blk"), R("sdx", lo, hi), True, True)
            act(R("sdw", 1 + lo, 1 + hi), R("bpB", 0, hi - lo), COPY)
        for o in ops[first:]:
            o["lazy"] = True
            if o["q"] in "vs":
                o["deps"].setdefault(moved, False)

    def calls_of(r):
        off = [e for e in range(1, N) if topo.chip(T.cores[(r + e) % N]) != topo.chip(T.cores[r])]
        near = [e for e in range(1, N) if e not in off]
        here = topo.chip(T.cores[r])
        off.sort(key=lambda e: (topo.mates(here, topo.chip(T.cores[(r + e) % N])), topo.same_plane(here, topo.chip(T.cores[(r + e) % N]))))
        return [off[a:b] + (near if b == len(off) else []) for a, b in zip(CALLS, CALLS[1:])]

    def engines_of(r, es):
        me = T.cores[r]
        away = [x for x in es if topo.chip(T.cores[(r + x) % N]) != topo.chip(me)]
        out = {}
        used = []
        for x in away + [y for y in es if y not in away]:
            eng = topo.engines(me, T.cores[(r + x) % N])
            free = [y for y in eng if y not in used]
            room = len(eng) // len(away) if x in away else NEAR
            n = 1
            while n * 2 <= room:
                n *= 2
            out[x] = free[0:n] if x in away else free[0:2 * n:2]
            used = used + out[x]
        return out

    def exchange(t):
        calls = calls_of(rank)
        for k, e in enumerate(sum(calls, [])):
            o, w, i = R("gg", (e - 1) * BW, (e - 1) * BW + G), R("f", OWN, OWN + S), R("sdp", 8 * (e - 1), 8 * e - 1)
            if k in GGV[t]:
                tc(o, w, ind=i)
            else:
                act(o, w, COPY, ind=i)
        sent = []
        bw = G + 2 if t else G
        for k, es in enumerate(calls):
            eng = engines_of(rank, es)
            trs = []
            for e in es:
                rid, pid, se = topo.addr(T.cores[(rank + e) % N])
                there = calls_of(rank)
                trs.append(RemoteDMATransfer(dst_ids=[DstId(rid=rid, pnc=pid)], dma_engine_mask=sum(1 << x for x in eng[e]), remote_sem=T.sem["arr%d" % (3 * t + k)],
                                             srcs=[T.gg[:, (e - 1) * BW:(e - 1) * BW + bw]],
                                             dsts=[T["ld%d" % t][:, (7 - e) * BW:(7 - e) * BW + bw] if t else T.f[:, S + (e - 1) * G:S + e * G]]))
            sem = "snd%d" % (3 * t + k)
            sent.append(record("g", lambda trs=trs, sem=sem: g.remote_dma_fused(trs, local_sem=T.sem[sem]), [R("gg", (e - 1) * BW, e * BW) for e in es], [],
                               2.5 if t + k == 0 else 0.6, 4.0, sem, sum(len(x) for x in eng.values()), ()))
        for k in range(1, len(calls)):
            ops[sent[k]]["deps"].setdefault(sent[k - 1], False)
        for k in range(len(calls)):
            es = [e for e in range(1, N) if e in calls_of((rank - e) % N)[k]]
            n = sum(len(engines_of((rank - e) % N, calls_of((rank - e) % N)[k])[e]) for e in es)
            land = [R("ld%d" % t, (7 - e) * BW, (8 - e) * BW) if t else R("f", S + (e - 1) * G, S + e * G) for e in es]
            record("r", None, [], land, 0.0, 0.0, "arr%d" % (3 * t + k), n, [sent[k]])
            for j, e in enumerate(es if t else []):
                o, i = R("f", OWN + S + (e - 1) * G, OWN + S + e * G), R("ld%d" % t, (7 - e) * BW, (7 - e) * BW + G)
                if j % 2:
                    act(o, i, COPY)
                else:
                    tc(o, i)

    def stream(X, t):
        h = 0 if X == "A" else 1
        nc = (4, 5)[h] if t == 0 else 8
        c0 = 0 if h == 0 else (4 if t == 0 else 8)
        s, d = LISTS[t > 0][h]
        return {"X": X, "h": h, "s": s, "d": d, "nl": 16 * nc, "nc": nc, "c0": c0, "l0": 16 * c0, "t": t, "own": t == 0 or h == 1, "opens": (t == 0) == (h == 0)}

    def start(st):
        t, h, nl = st["t"], st["h"], st["nl"]
        if t == 0:
            st["list"] = R("wl", st["c0"], st["c0"] + st["nc"])
            st["diag"] = R("wq", st["l0"], st["l0"] + nl)
        elif h == 1:
            st["list"] = R("wl", 10 * t + 2, 10 * t + 10)
            st["diag"] = R("wq", 144 * t + 16, 144 * t + 144)
        else:
            act(R("qa", 112, 128), R("wq", 144 * t, 144 * t + 16), COPY)
            tt(R("rki", 0, 7), R("ld%d" % t, G, 7 * BW, BW), R("c112", 0, 7), ADD)
            tt(R("qa", 0, 112), R("sdw", 0, 785), R("mask", 0, 112), MUL, ind=R("rki", 0, 7))
            scan(R("qc"), R("rsa"), R("qa"), 0.0, MUL, ADD)
            tc(R("lA"), R("qc", 15, 128, 16))
            st["list"] = R("lA")
            st["diag"] = R("qa")

    def look(st, hop, ncs):
        X, h, nl, l0, nc = st["X"], st["h"], st["nl"], st["l0"], st["nc"]
        sq, hh = "s" + X, (8 * h, 8 * h + 8)
        gs = (h, 8 + h)
        win, bb, me = R("f", 0, WIN), R("b", l0, l0 + nl), RN(sq, gs, 16, 2, rows=nl)
        ls = st["list"]
        named = hop < H or st["t"] < RO - 1
        wide = 18 if hop == 1 else 17
        first = len(ops)
        for c0, c1 in (((0, 2), (2, nc)) if hop > 1 and X in OFF2[st["t"] > 0] else ((0, nc),)):
            if c0 and X + str(hop) in OFFS[st["t"] > 0]:
                act(R("off" + X, 16 * c0, 16 * c1), R("nbw"), COPY, ind=R(ls[0], ls[1] + c0, ls[1] + c1))
            else:
                tc(R("off" + X, 16 * c0, 16 * c1), R("nbw"), ind=R(ls[0], ls[1] + c0, ls[1] + c1))
            ops[-1]["early"] = TAIL
        if st["own"] and hop == 1 or X + str(hop) in BV[st["t"] > 0]:
            ts(bb, R("f", OWN, OWN + S) if hop == 1 and st["own"] else win, col("mid"), None, ADD, ind=st["list"])
        else:
            act(bb, win, IDEN, bias=col("mid"), ind=st["list"])
        ops[-1]["early"] = EARLY
        if named and st["t"] == 0 and (hop == 1 or CPS):
            act(R("cp" + X, 0, nl), R("off" + X, 0, nl), COPY)
        elif named:
            gcopy(R("cp" + X, 0, nl), R("off" + X, 0, nl))
            st["cp"] = len(ops) - 1
        if hop == 1:
            ts(R("nf" + X, 0, nl), bb, -MID - 0.5, None, GE)
        if hop == 1 and st["own"]:
            for o in ops[first:]:
                o["early"], o["lazy"] = 0.0, True
        mms([(R("bp" + X, j, RR * nl, RR), R("idb"), bb, True, True) for j in range(RR)])
        st["bp"] = len(ops) - 1
        mm(RN(sq, gs, (0, wide), (0, 3), rows=nl), R("ones", 0, nl, rows=3), RN("mc", ALL8, (0, wide), (0, 3), rows=3), True, False)
        mm(RN(sq, gs, ALL16, 0, rows=nl), bb, R("wb"), False, False)
        if hop == 1:
            mm(me, st["diag"], R("cm"), False, False)
            mm(RN(sq, gs, 17, 2, rows=nl), R("nf" + X, 0, nl), R("wn"), False, False)
        else:
            mm(me, R("idf", 0, nl, rows=nl), R("xx" + X, 129, 145, 2, rows=nl), False, False)
        mm(me, bb, R("wa", 1, 16, 2), False, False)
        if named:
            mm(RN(sq, gs, ALL16, 2, rows=nl), R("cp" + X, 0, nl), R("idf"), False, False)
        lo = 0
        st["max"] = []
        opening = hop == 1 and st["opens"]
        closing = hop == H and not st["opens"]
        chunks, onv = (OPENING if opening else CLOSING if closing else CHUNKS)[nl], None
        if X + str(hop) in ONV[st["t"] > 0] and not opening:
            chunks, onv = SHARED[nl]
        for k, w in enumerate(chunks):
            hi = lo + w
            if k == (0 if opening else onv):
                ts(R("a" + X, 16 * lo, 16 * hi), win, col("mid"), None, ADD, ind=R("off" + X, lo, hi))
            else:
                act(R("a" + X, 16 * lo, 16 * hi), win, IDEN, bias=col("mid"), ind=R("off" + X, lo, hi))
                if turn:
                    ops[-1]["deps"].setdefault(turn.pop(), False)
                turn.append(len(ops) - 1)
            for n in range(NC):
                tt(R("m" + X, RR * (n * nl + lo), RR * (n * nl + hi)), R("a" + X, 16 * lo + n, 16 * hi, NC), R("bp" + X, RR * lo, RR * hi), MAX)
                st["max"].append(len(ops) - 1)
                if closing and k == CK[st["t"] > 0] and n == 0:
                    ops[-1]["deps"].setdefault(chosen[0], False)
            lo = hi
        sums = len(ops)
        for p0, p1 in PARTS[nl]:
            for a0, a1 in APARTS[nl]:
                if p0 < a1 <= p1:
                    mms([(RN(sq, gs, n, (1, 3), rows=(a0, a1)), R("a" + X, 16 * a0 + n, 16 * a1, 16), R("wa"), False, False) for n in range(NV)])
            for n in range(NC):
                mms([(RN(sq, gs, n + NC * j, (0, 2), rows=(p0, p1)), R("m" + X, RR * (n * nl + p0) + j, RR * (n * nl + p1), RR), R("wm"), False,
                      n == NC - 1 and j == RR - 1) for j in range(RR)])
        chain = len(ops)
        st["sums"] = chain - 1 if st["opens"] else st["bp"]
        for g0, g1 in HALVES:
            red(RN("t" + X, (g0, g1), (0, wide), rows=nl), RN(sq, (g0 + h, g1 + h), (0, wide), (0, 3), rows=nl), MIN)
        red(R("vi", hh[0], hh[1], rows=nl), RN("t" + X, ALL8, (0, wide), rows=nl), MAX)
        chosen[0] = len(ops) - 1
        if named:
            ts(R("id%d" % (hop % 2), hh[0], hh[1], rows=nl), R("vi", hh[0], hh[1], rows=nl), 8191, None, AND)
        if hop < H:
            tt(R("xx" + X, 1, 161, 2), R("id%d" % (hop % 2), hh[0], hh[1]), R("mask1"), MUL, ind=R("rep1", 0, 5))
            mms([(R("k" + X, 0, nc), R("xx" + X, 1 - k, 129 - k, rows=nl), R("cm2", 8 * k, 8 * k + nc, rows=nl), k == 0, k == 1) for k in (0, 1)])
            st["list"] = R("l" + X, 0, nc) if hop < H - 1 else R("dl", st["s"], st["s"] + nc)
            if X + str(hop) in LS[st["t"] > 0]:
                act(st["list"], R("k" + X, 0, nc), COPY)
            else:
                tc(st["list"], R("k" + X, 0, nc))
        for o in ops[chain:]:
            o["early"] = TAIL
        if hop == H and st["opens"]:
            for o in ops[sums:]:
                o["early"] = BEARLY[st["t"] > 0]

    def places(t, sts, F):
        nc = sum(st["nc"] for st in sts)
        L = 16 * nc
        first = len(ops)
        for q0 in range(0, 16, 4):
            mms([(R("k" + F, 320, 320 + nc), R("wz", 15 - q, 143 - q), R("b", q, L, 16), q == 0, q == 15) for q in range(q0, q0 + 4)])
        for st in sts:
            ops[first]["deps"].setdefault(st[ZAFTER], False)
        zi, zm, zq, zh, zg = (R(x, 0, nc) for x in ("zi", "zm", "zq", "zh", "zg"))
        d0 = sts[0]["d"]
        dl = R("dl", d0, d0 + nc)
        tc(zi, R("k" + F, 320, 320 + nc))
        ts(zm, zi, 4095, None, AND)
        tt(zq, zm, zm, MUL)
        if t:
            ts(zi, zq, float(97 * 32 * t), None, ADD)
        ts(zh, zi if t else zq, 5, 4095, SHR, AND)
        ts(zg, zh, float(S), float(-S), GE, MUL)
        tt(dl, zh, zg, ADD)
        for o in ops[first:]:
            o["early"] = ZEARLY
        if ZPIN[t > 0]:
            zs = [i for i in range(first, len(ops)) if ops[i]["q"] == "v"]
            mx = [st["max"] for st in sts if st["X"] != F][0]
            for k, i in enumerate(zs):
                ops[mx[min(len(mx) - 1, ZPIN[t > 0][0] + int(k * ZPIN[t > 0][1]))]]["deps"].setdefault(i, False)
        gcopy(R("dT", 0, nc), dl)
        act(R("fd", 0, L), R("f", 0, S), IDEN, bias=col("r15"), ind=dl)
        ops[-1]["early"] = FDE
        act(R("uu", 0, L), R("pl"), COPY, ind=dl)
        uu = len(ops) - 1
        for st in sts:
            X, nl, l0 = st["X"], st["nl"], st["l0"]
            st["F"] = F
            if NXP[X == F]:
                o = R("bp" + X, 384, 392, rows=nl)
                mm(o, R("b", l0, l0 + nl), R("wa", 1, 16, 2), True, False)
                mm(o, R("ones", 0, nl, rows=1), R("own", rows=1), False, False)
                mm(o, R("fd", l0, l0 + nl), R("wn"), False, True)
            else:
                o = R("bp" + X, 384, 448, rows=nl)
                mm(o, R("b", l0, l0 + nl), R("wk", 0, 128, 2), True, False)
                mm(o, R("idb", 0, nl, rows=nl), R("mn", rows=nl), False, False)
                mm(o, R("fd", l0, l0 + nl), R("ws", 0, 128, 2), False, True)
                act(R("tx" + X, rows=nl), o, IDEN, bias=float(S))
                st["tx"] = len(ops) - 1
        act(R("da", 0, L), R("ramp"), COPY, ind=dl)
        da = len(ops) - 1
        if "a" in RULES:
            ops[da]["deps"].setdefault([st["tx"] for st in sts if st["X"] == F][0], False)
        if "b" in RULES:
            ops[uu]["deps"].setdefault(da, False)
        bp = "bp" + F
        mm(R(bp, 0, L), R("idb"), R("uu", 0, L), True, False)
        mm(R(bp, 0, L), R("idb"), R("b", 0, L), False, False)
        mm(R(bp, 0, L), R("ones", rows=1), R("mhalf", 0, L, rows=1), False, True)
        act(R("uv", 0, L), R(bp, 0, L), IDEN, bias=MAGIC, scale=0.5)
        act(R("val", 16 * d0, 16 * d0 + L), R("uv", 0, L), IDEN, bias=col("vb%d" % t), scale=col("rl"))
        for st in sts:
            act(R("val", 16 * st["s"], 16 * st["s"] + st["nl"]), R("b", st["l0"], st["l0"] + st["nl"]), IDEN, bias=col("neg"), scale=col("rl"))
            if "c" in RULES:
                ops[-1]["deps"].setdefault(uu, False)

    def compare(st, L, scols):
        X, h, nl, nc, c0 = st["X"], st["h"], st["nl"], st["nc"], st["c0"]
        off = 2048.0
        mm(R("k" + X, 0, nc), R("idf"), R("dT", c0, c0 + nc), True, False)
        if NXP[X == st["F"]]:
            tt(R("nx" + X, 15, 143, 16, rows=nl), R("vi", 8 * h, 8 * h + 8, rows=nl), R("bp" + X, 384, 392, rows=nl), GE)
            for q in range(16):
                mm(R("k" + X, 0, nc), R("nx" + X, 15 - q, 143 - q, rows=nl), R("idw", q, nl, 16, rows=nl), False, q == 15)
        else:
            off += 7 * 8192
            tt(R("ny" + X, 1, 129, 2), R("vi", 8 * h, 8 * h + 8), R("tx" + X), GE, ind=R("rep8", 0, 4))
            for k in (0, 1):
                mm(R("k" + X, 0, nc), R("ny" + X, 1 - k, 129 - k, rows=nl), R("cm8", 8 * k, 8 * k + nc, rows=nl), False, k == 1)
        st["cut"] = cut = c0 + nc - scols
        if scols:
            act(R("nco", 0, nc), R("k" + X, 0, nc), IDEN, bias=off + 0.5, scale=-1.0)
            act(R("nco", 8, 8 + nc), R("k" + X, 0, nc), IDEN, bias=0.5 - off)
        for c in range(c0, c0 + nc):
            if c >= cut:
                act(RN("e3", c, (0, L - 16 * c)), R("da", 16 * c, L), SIGN, bias=R("nco", c - c0, c - c0 + 1))
                act(RN("e4", c, (0, L - 16 * c)), R("da", 16 * c, L), SIGN, bias=R("nco", 8 + c - c0, 9 + c - c0), scale=-1.0)
            else:
                ts(RN("e3", c, (0, L - 16 * c)), R("da", 16 * c, L), off, R("k" + X, c - c0, c - c0 + 1), ADD, EQ)

    def rivals(bank, table, c0, c1, sts):
        calls, late = [(RN(bank, (c0, c1), (0, 18)), R("idf"), RN(table, (c0, c1), (0, 18)))], []
        for st in sts:
            for a, b, half, es in ((st["c0"], st["cut"], 0, ("e3",)), (st["cut"], st["c0"] + st["nc"], 128, ("e3", "e4"))):
                for e in es:
                    to = late if half else calls
                    for c in range(a, min(b, c1 - 1)):
                        lo = max(c0, c + 1)
                        to.append((RN(bank, (lo, c1), (1, 17)), R("wall", half, half + 128), RN(e, c, (16 * (lo - c), 16 * (c1 - c)))))
                    if c0 <= a < b:
                        to.append((RN(bank, (a, b), (1, 17)), R("wtri", half, half + 128), RN(e, (a, b), (0, 16))))
        calls = calls[:LATE] + late + calls[LATE:] if late else calls
        for k, (o, l, r) in enumerate(calls):
            mm(o, l, r, k == 0, k == len(calls) - 1)
            if k == 0:
                ops[-1]["early"] = 20.0

    def scatter(bank, parts, lo, hi):
        if RVP[parts[0][0]["t"]]:
            c0, c1 = min(st["c0"] for st, _ in parts), max(st["c0"] + st["nc"] for st, _ in parts)
            at = "k" + parts[0][0]["X"]
            mm(R(at, 448 + lo, 448 + hi), R("idf"), R("rr", lo, hi), True, False)
            red(R("rb", c0, c1), RN(bank, (c0, c1), (0, 17)), MIN)
            for k, (st, kind) in enumerate(parts):
                mm(R(at, 448 + st[kind], 448 + st[kind] + st["nc"]), R("idb"), R("rb", st["c0"], st["c0"] + st["nc"]), False, k == len(parts) - 1)
            tt(R("ofl", lo, hi), R("dl", lo, hi), R(at, 448 + lo, 448 + hi), MAX)
            tc(R("f"), R("val", 16 * lo, 16 * hi), oind=R("ofl", lo, hi))
            return
        for st, kind in parts:
            k = 0 if kind == "d" else 1
            red(R("rs", st[kind], st[kind] + st["nc"]), RN(bank, (st["c0"], st["c0"] + st["nc"]), (k, 17 + k)), MIN)
        tt(R("ofl", lo, hi), R("rs", lo, hi), R("dl", lo, hi), MAX)
        tc(R("f"), R("val", 16 * lo, 16 * hi), oind=R("ofl", lo, hi))

    def moves(t, sts):
        A, B = sts
        nc = A["nc"] + B["nc"]
        if t == 0:
            compare(A, 16 * nc, SCOLS[0])
            rivals("q2", "tb0", 0, A["nc"], [A])
            scatter("q2", [(A, "s"), (A, "d")], A["s"], B["d"])
            compare(B, 16 * nc, 0)
            rivals("q1", "tb0", B["c0"], nc, [A, B])
            requests(sts, "A")
            scatter("q1", [(B, "d"), (B, "s")], B["d"], B["s"] + B["nc"])
        else:
            compare(B, 16 * nc, SCOLS[1])
            if TENT[t]:
                rivals("q2", "tb%d" % t, B["c0"], nc, [B])
                scatter("q2", [(B, "d")], B["d"], B["d"] + B["nc"])
            compare(A, 16 * nc, 0)
            rivals("q1", "tb%d" % t, 0, nc, [B, A])
            if t + 1 < RO:
                requests(sts, "B")
            if TENT[t]:
                scatter("q1", [(A, "d"), (A, "s"), (B, "s")], B["s"], B["d"])
            else:
                scatter("q1", [(dict(A, nc=nc), "d"), (A, "s"), (B, "s")], 0, 2 * nc)

    def requests(sts, F):
        ts(R("ebi"), R("id0"), 1.0 / G, 1.0 - (S + (G - 1) / 2) / G, MUL, ADD)
        ts(R("idm"), R("id0"), float(1 - S), None, ADD)
        tt(R("on"), R("ebi"), R("ec"), EQ, ind=R("rep8"))
        A, B = sts
        bp = "bp" + F
        mm(R(bp, 256, 320, rows=A["nl"]), R("tril", 0, A["nl"], rows=A["nl"]), R("on", 0, 64, rows=A["nl"]), True, True)
        mm(R(bp, 320, 384, rows=B["nl"]), R("tril", 0, B["nl"], rows=B["nl"]), R("on", 64, 128, rows=B["nl"]), True, False)
        mm(R(bp, 320, 384, rows=B["nl"]), R("ones", 0, B["nl"], rows=A["nl"]), R("on", 0, 64, rows=A["nl"]), False, True)
        scan(R("qs"), R("rs8"), R(bp, 256, 384), 0.0, MUL, MAX)
        tt(R("ek"), R("idm"), R("on"), MUL, ind=R("rep8"))
        if MHS:
            bq = "bpB" if F == "A" else "bpA"
            mm(R(bq, 0, 256), R("idh", 0, 128, rows=1), R("jh", rows=1), True, False)
            mms([(R(bq, m, 256, 16), R("idh", 128, 256), R("qs", 7, 128, 8), False, m == 15) for m in range(16)])
            act(R("mh"), R(bq, 0, 256), SIGN, bias=col("half"))
            act(R("mi"), R(bq, 0, 256), SIGN, bias=col("half"), scale=-1.0)
        else:
            for k in (0, 1):
                tt(R("mh", 128 * k, 128 * k + 128), R("qs"), R("jm1", 0, 128), EQ, ind=R("rep87", 8 * k, 8 * k + 8))
        for nm in ("mh", "mi") if MHS else ("mh",):
            for st in sts:
                nl, h = st["nl"], st["h"]
                mm(R("k" + F, 384, 448), R(nm, 128 * h, 128 * h + 128, rows=nl), R("ek", 64 * h, 64 * h + 64, rows=nl), h == 0 and nm == "mh",
                   h == 1 and (nm == "mi" or not MHS))
        act(R("rq"), R("k" + F, 384, 448), COPY, scale=0.5 if MHS else 1.0)
        tt(R("gg", G, 16 * BW, BW), R("rq"), R("ce"), SUB, ind=R("gl", 0, 1))

    for o in ops:
        o["lazy"] = True
    exchange(0)
    for t in range(RO):
        sts = (stream("A", t), stream("B", t))
        order = sts if t == 0 else sts[::-1]
        F = order[0]["X"]
        ncs = sum(st["nc"] for st in sts)
        for st in order:
            start(st)
        for hop in range(1, H + 1):
            for st in order:
                look(st, hop, ncs)
            if t == 0 and hop in RAMP:
                ops[ramp[RAMP[hop]]]["deps"][order[1]["cp"]] = False
            if t == 0 and hop < H:
                for k in range(2 * hop - 1, 2 * hop + 1):
                    hi = min(M * (k + 1), S)
                    act(R("pl", M * k, hi), R("pl", 0, hi - M * k), COPY)
                    ops[-1]["lazy"] = True
                    ops[-1]["deps"].setdefault(turn[0], False)
        places(t, sts, F)
        moves(t, sts)
        if t == 0:
            later_tables()
        if t + 1 < RO:
            exchange(t + 1)
    for q, lo in (("y", 0), ("s", hx)):
        dma(q, T.y[:, lo:lo + hx], T.f[:, lo:lo + hx], [], [R("f", lo, lo + hx)], 4.0)
    emit_all()
